import numpy as np
import ml_dtypes


def mxq(x, axis, fmt="e4m3"):
    dtype, down = {"e4m3": (ml_dtypes.float8_e4m3fn, 7), "e5m2": (ml_dtypes.float8_e5m2, 14)}[fmt]
    v = np.moveaxis(np.asarray(x, np.float32).astype(ml_dtypes.bfloat16).astype(np.float64), axis, -1)
    blocks = v.reshape(v.shape[:-1] + (-1, 32))
    amax = np.abs(blocks).max(-1, keepdims=True)
    byte = np.maximum(np.where(amax > 0, np.frexp(amax)[1] - 1 + 127, 0) - down, 1)
    scale = np.exp2(byte - 127.0)
    codes = (blocks / scale).astype(np.float32).astype(dtype).astype(np.float64)
    return np.moveaxis((codes * scale).reshape(v.shape), -1, axis)


WIDE = False


def mx_kscale(k):
    if not WIDE:
        return np.ones(k)
    levels = np.array([10, -10, 5, -5, 0])
    if k % 512:
        return np.exp2(np.random.permutation(np.resize(levels, k // 32))).repeat(32)
    a = np.empty((k // 512, 16))
    for p in range(k // 512):
        a[p, :8] = np.random.permutation(np.resize(levels, 8))
        for g in range(8):
            far = levels[np.abs(levels - a[p, g]) >= 10]
            a[p, g + 8] = far[np.random.randint(len(far))]
    return np.exp2(a.ravel()).repeat(32)


def f64(x):
    return np.asarray(x).astype(np.float64)


def striped(idx):
    return np.tile(idx.reshape(-1, 16).T, (8, 1)).astype(np.uint16)


def unstriped(offs):
    return offs[:16].T.reshape(-1).astype(np.int64)


E2M1 = np.array([0.0, 0.5, 1.0, 1.5, 2.0, 3.0, 4.0, 6.0, -0.0, -0.5, -1.0, -1.5, -2.0, -3.0, -4.0, -6.0])


def pack_weight(w, fmt):
    k, n = w.shape
    w = f64(np.asarray(w, np.float32).astype(ml_dtypes.bfloat16)).reshape(k // 32, 32, n)
    amax = np.abs(w).max(1)
    if fmt == "e4m3":
        byte = np.frexp(amax)[1] - 1 + 127 - 7
    else:
        mant, ex = np.frexp(amax / 6.0)
        byte = np.where(mant > 0.5, ex, ex - 1) + 127
    byte = np.clip(np.where(amax > 0, byte, 1), 1, 254)
    scaled = (w * np.exp2(127.0 - byte)[:, None, :]).reshape(k, n).astype(np.float32)
    by_word = np.ascontiguousarray(scaled.reshape(k // 512, 128, 4, n).transpose(0, 1, 3, 2))
    if fmt == "e4m3":
        words = by_word.astype(ml_dtypes.float8_e4m3fn).view(np.uint8)
    else:
        c = by_word.astype(ml_dtypes.float4_e2m1fn).view(np.uint8) & 0xF
        words = (c[..., 0::2] | (c[..., 1::2] << 4)).reshape(k // 512, 128, 2 * n)
    return np.ascontiguousarray(words), np.ascontiguousarray(byte.astype(np.uint8).reshape(k // 512, 16, n))


def unpack_weight(words, scales, fmt):
    g, _, n = scales.shape
    words = np.ascontiguousarray(words).reshape(g, 128, n, -1)
    if fmt == "e4m3":
        vals = words.view(ml_dtypes.float8_e4m3fn).astype(np.float64)
    else:
        nib = np.empty((g, 128, n, 4), np.uint8)
        nib[..., 0::2] = words & 0xF
        nib[..., 1::2] = words >> 4
        vals = E2M1[nib]
    vals = vals * np.repeat(np.exp2(scales.astype(np.float64) - 127.0), 8, axis=1)[..., None]
    return vals.transpose(0, 1, 3, 2).reshape(g * 512, n)


def gelu(v):
    return 0.5 * v * (1.0 + np.tanh(np.sqrt(2.0 / np.pi) * (v + 0.044715 * v**3)))


def bf(x):
    return np.asarray(x, np.float32).astype(ml_dtypes.bfloat16)

def planes(Y):
    n, m = Y.shape
    b = f64(bf(Y)).reshape(n // 32, 32, m)
    amax = np.abs(b).max(1)
    byte = np.clip(np.where(amax > 0, np.frexp(amax)[1] - 1 + 127 - 7, 1), 1, 254)
    codes = (b * np.exp2(127.0 - byte)[:, None, :]).reshape(n, m).astype(np.float32).astype(ml_dtypes.float8_e4m3fn).view(np.uint8)
    words = codes.reshape(n // 512, 128, 4, m).transpose(0, 1, 3, 2)
    return np.ascontiguousarray(words), np.ascontiguousarray(byte.astype(np.uint8).reshape(n // 512, 16, m))


K, T, S, P, H, N = 1024, 4096, 1024, 512, 1536, 1024


def setup_inputs():
    n = np.random.standard_normal
    s = mx_kscale(K)[:, None]
    u = mx_kscale(H)[:, None]
    tab_words, tab_scales = pack_weight(n((K, T)) * s, "e4m3")
    w1 = n((K, H)) * 1.5 / np.sqrt(K) / s
    vmax = np.exp(0.3 * n(H)) * u[:, 0]
    pool = np.exp(0.8 * n(N))[None, :]
    w2_words, w2_scales = pack_weight(n((H, N)) * 3.0 / np.sqrt(H) * pool / u, "e2m1")
    return {
        "tab_words": tab_words, "tab_scales": tab_scales,
        "offs": striped(np.random.permutation(T)[:S]),
        "pos1": striped(np.random.permutation(S)[:P]),
        "pos2": striped(np.random.permutation(S)[:P]),
        "w1": w1.astype(np.float32),
        "vmax": vmax.astype(np.float32),
        "w2_words": w2_words, "w2_scales": w2_scales,
    }


def reference(tab_words, tab_scales, offs, pos1, pos2, w1, vmax, w2_words, w2_scales):
    v = unpack_weight(tab_words, tab_scales, "e4m3")[:, unstriped(offs)]
    w2 = unpack_weight(w2_words, w2_scales, "e2m1")
    h = np.maximum(mxq(f64(w1), 0, "e4m3").T @ v, 0.0)
    a = h[:, unstriped(pos1)]
    b = h[:, unstriped(pos2)]
    z = a / (1.0 + a + b) * f64(vmax)[:, None]
    y = w2.T @ mxq(z, 0, "e4m3")
    words, scales = planes(y)
    return y, words, scales

@@ -1,0 +1,292 @@
+from contextlib import ExitStack
+
+import concourse.mybir as mybir
+
+K, T, S, PAIRS, H, N = 1024, 4096, 1024, 512, 1536, 1024
+FLOPS = 2 * K * H * S + 2 * H * N * PAIRS
+
+F32 = mybir.dt.float32
+BF16 = mybir.dt.bfloat16
+I32 = mybir.dt.int32
+U32 = mybir.dt.uint32
+U16 = mybir.dt.uint16
+U8 = mybir.dt.uint8
+FP8X4 = mybir.dt.float8_e4m3fn_x4
+FP4X4 = mybir.dt.float4_e2m1fn_x4
+ACT = mybir.ActivationFunctionType
+ALU = mybir.AluOpType
+
+P = 128
+KA = K // 512
+HB = H // 512
+NG = N // 512
+CHUNK = 128
+NC = PAIRS // CHUNK
+M_VECTOR = 88
+
+
+def tile_list_inhibited_enzyme_flux_kernel(
+    tc, tab_words, tab_scales, offs, pos1, pos2, w1, vmax, w2_words, w2_scales, out_0, out_1, out_2
+):
+    nc = tc.nc
+    with ExitStack() as ctx:
+        keep = ctx.enter_context(tc.tile_pool(name="keep", bufs=1))
+        ring = ctx.enter_context(tc.tile_pool(name="ring", bufs=2))
+        psum = ctx.enter_context(tc.psum_pool(name="psum", bufs=1))
+
+        offs_t = keep.tile([P, S // 16], U16, name="offs_t")
+        pos1_t = keep.tile([P, PAIRS // 16], U16, name="pos1_t")
+        pos2_t = keep.tile([P, PAIRS // 16], U16, name="pos2_t")
+        tabw = [keep.tile([P, T], U32, name=f"tabw{a}", align_bytes=64) for a in range(KA)]
+        tabs = keep.tile([P, T], U8, name="tabs", align_bytes=64)
+        w2raw = keep.tile([P, HB * 2 * N], U8, name="w2raw", align_bytes=64)
+        w2sraw = keep.tile([P, N], U8, name="w2sraw", align_bytes=64)
+        w2w = keep.tile([P, HB * 2 * N], U8, name="w2w", align_bytes=64)
+        w2s = [keep.tile([P, N], U8, name=f"w2s{b}", align_bytes=64) for b in range(HB)]
+        vm = keep.tile([P, HB, 4], F32, name="vm")
+        w1c = [[keep.tile([P, 512], U32, name=f"w1c{b}{a}", align_bytes=64) for a in range(KA)] for b in range(HB)]
+        w1s = [[keep.tile([P, 512], U8, name=f"w1s{b}{a}", align_bytes=64) for a in range(KA)] for b in range(HB)]
+        gw = [[keep.tile([P, 512], U32, name=f"gw{a}{f}", align_bytes=64) for f in range(2)] for a in range(KA)]
+        gs = [keep.tile([P, 512], U8, name=f"gs{f}", align_bytes=64) for f in range(2)]
+        den = [keep.tile([P, 512], F32, name=f"den{i}") for i in range(2)]
+        banks = [psum.tile([P, 512], F32, name=f"bank{i}") for i in range(8)]
+        yscales = keep.tile([P, NG * PAIRS], U8, name="yscales", align_bytes=64)
+        warm = keep.tile([P, 2], F32, name="warm")
+
+        nc.vector.memset(tabs[:].bitcast(I32), 0)
+        nc.vector.memset(w2sraw[:].bitcast(I32), 0)
+        for b in range(1, HB):
+            nc.vector.memset(w2s[b][:].bitcast(I32), 0)
+        nc.vector.memset(warm[:, 0:1], 1.0)
+        nc.scalar.activation(out=warm[:, 1:2], in_=warm[:, 0:1], func=ACT.Abs_reciprocal_sqrt)
+
+        w1raw = {}
+
+        def load_w1(b, a):
+            w1raw[b, a] = ring.tile([P, 4, 512], F32, name="w1raw", bufs=4, align_bytes=64)
+            rows = w1[512 * a : 512 * (a + 1), 512 * b : 512 * (b + 1)]
+            nc.sync.dma_start(out=w1raw[b, a][:], in_=rows.rearrange("(p j) c -> p j c", j=4))
+
+        def load_tab(a):
+            nc.sync.dma_start(out=tabw[a][:].bitcast(I32), in_=tab_words[a].rearrange("p t i -> p (t i)").bitcast(I32))
+
+        nc.sync.dma_start(offs_t[:], offs)
+        load_tab(0)
+        for q in range(4):
+            nc.sync.dma_start(out=tabs[32 * q : 32 * q + 4 * KA, :].bitcast(I32), in_=tab_scales[:, 4 * q : 4 * q + 4, :].bitcast(I32))
+        load_w1(0, 0)
+        load_tab(1)
+        load_w1(0, 1)
+        nc.sync.dma_start(pos1_t[:], pos1)
+        nc.sync.dma_start(pos2_t[:], pos2)
+        nc.sync.dma_start(out=vm[:], in_=vmax.rearrange("(b p t) -> p b t", p=P, t=4))
+        nc.sync.dma_start(
+            out=w2raw[:].bitcast(I32).rearrange("p (a c) -> p a c", a=HB), in_=w2_words.bitcast(I32).rearrange("a p c -> p a c")
+        )
+        load_w1(1, 0)
+        load_w1(1, 1)
+        for q in range(4):
+            nc.sync.dma_start(out=w2sraw[32 * q : 32 * q + 4 * HB, :].bitcast(I32), in_=w2_scales[:, 4 * q : 4 * q + 4, :].bitcast(I32))
+
+        def gather_words(a, f):
+            nc.vector.tensor_copy(gw[a][f][:], tabw[a][:].indirect(offs_t[:, 32 * f : 32 * (f + 1)]))
+
+        def gather_scales(f):
+            nc.vector.tensor_copy(gs[f][:], tabs[:].indirect(offs_t[:, 32 * f : 32 * (f + 1)]))
+
+        grouped = {}
+
+        def round_w1(b, a, m_vector=0):
+            g = ring.tile([P, 2048], BF16, name="w1g", align_bytes=64)
+            grouped[b, a] = g
+            dst = g[:].rearrange("p (t m j) -> p m j t", t=4, j=4)
+            src = w1raw[b, a][:].rearrange("p j (m t) -> p m j t", t=4)
+            if m_vector:
+                nc.vector.tensor_copy(out=dst[:, :m_vector], in_=src[:, :m_vector])
+            nc.scalar.copy(out=dst[:, m_vector:], in_=src[:, m_vector:])
+
+        def quant_w1(b, a):
+            nc.vector.quantize_mx(out=w1c[b][a][:].bitcast(FP8X4), scales=w1s[b][a][:], in_=grouped[b, a][:])
+
+        gather_words(0, 0)
+        gather_words(0, 1)
+        gather_scales(0)
+        gather_scales(1)
+        round_w1(0, 0)
+        quant_w1(0, 0)
+        gather_words(1, 0)
+        gather_words(1, 1)
+        round_w1(0, 1, M_VECTOR)
+        quant_w1(0, 1)
+        load_w1(2, 0)
+        load_w1(2, 1)
+
+        nc.vector.tensor_copy(
+            out=w2w[:].bitcast(U16).rearrange("p (x t m) -> p x t m", t=4, m=P),
+            in_=w2raw[:].bitcast(U16).rearrange("p (x m t) -> p x t m", t=4, m=P),
+        )
+        nc.vector.tensor_copy(
+            out=w2s[0][:].rearrange("p (g t m) -> p g t m", t=4, m=P),
+            in_=w2sraw[:].rearrange("p (g m t) -> p g t m", t=4, m=P),
+        )
+        for b in range(1, HB):
+            nc.sync.dma_start(out=w2s[b][0 : P - 4 * b, :].bitcast(I32), in_=w2s[0][4 * b : P, :].bitcast(I32))
+
+        h, sub, zt, zc, zs = {}, {}, {}, {}, {}
+
+        def make_h(r):
+            b, t = divmod(r, 4)
+            h[r] = ring.tile([P, S], F32, name="h", bufs=6)
+            cols = slice(P * t, P * (t + 1))
+            for f in range(2):
+                acc = banks[(2 * r + f) % 8]
+                for a in range(KA):
+                    nc.tensor.matmul_mx(
+                        out=acc[:],
+                        lhsT=w1c[b][a][:, cols].bitcast(FP8X4),
+                        lhsT_scale=w1s[b][a][:, cols],
+                        rhs=gw[a][f][:].bitcast(FP8X4),
+                        rhs_scale=gs[f][4 * a : P, :],
+                        start=(a == 0),
+                        stop=(a == KA - 1),
+                    )
+                nc.scalar.activation(out=h[r][:, 512 * f : 512 * (f + 1)], in_=acc[:], func=ACT.Relu)
+
+        units = [(b, 0, PAIRS, [t]) for b in range(HB - 1) for t in range(4)]
+        units += [(HB - 1, CHUNK * c, CHUNK, [0, 1, 2, 3]) for c in range(NC - 1)]
+        units += [(HB - 1, CHUNK * (NC - 1), CHUNK, ts) for ts in ([0, 1], [2, 3])]
+
+        def pick_substrate(u):
+            b, i0, w, ts = units[u]
+            sub[u] = ring.tile([P, 512], F32, name="sub", bufs=3)
+            for x, t in enumerate(ts):
+                nc.vector.tensor_copy(sub[u][:, w * x : w * (x + 1)], h[4 * b + t][:].indirect(pos1_t[:, i0 // 16 : (i0 + w) // 16]))
+
+        def pick_inhibitor(u):
+            b, i0, w, ts = units[u]
+            for x, t in enumerate(ts):
+                cols = slice(w * x, w * (x + 1))
+                nc.vector.tensor_tensor(
+                    den[u % 2][:, cols], h[4 * b + t][:].indirect(pos2_t[:, i0 // 16 : (i0 + w) // 16]), sub[u][:, cols], ALU.add
+                )
+
+        def invert(u):
+            b, i0, w, ts = units[u]
+            cols = slice(0, w * len(ts))
+            root = ring.tile([P, 512], F32, name="root")
+            nc.scalar.activation(out=root[:, cols], in_=den[u % 2][:, cols], func=ACT.Abs_reciprocal_sqrt, bias=1.0)
+            nc.scalar.activation(out=den[u % 2][:, cols], in_=root[:, cols], func=ACT.Square)
+
+        def rate(u):
+            b, i0, w, ts = units[u]
+            if ts[0] == 0:
+                zt[b, i0] = ring.tile([P, 4 * w], BF16, name="zt", align_bytes=64)
+            for x, t in enumerate(ts):
+                cols = slice(w * x, w * (x + 1))
+                nc.vector.scalar_tensor_tensor(
+                    out=zt[b, i0][:, w * t : w * (t + 1)],
+                    in0=sub[u][:, cols],
+                    scalar=vm[:, b, t : t + 1],
+                    in1=den[u % 2][:, cols],
+                    op0=ALU.mult,
+                    op1=ALU.mult,
+                )
+
+        def quant_z(b, i0, w):
+            z4 = ring.tile([P, 4 * w], BF16, name="z4", align_bytes=64)
+            zc[b, i0] = keep.tile([P, w], U32, name=f"zc{b}_{i0}", align_bytes=64)
+            zs[b, i0] = keep.tile([P, w], U8, name=f"zs{b}_{i0}", align_bytes=64)
+            nc.vector.tensor_copy(
+                out=z4[:].rearrange("p (c i t) -> p c t i", i=4, t=4),
+                in_=zt[b, i0][:].rearrange("p (t c i) -> p c t i", i=4, t=4),
+            )
+            nc.vector.quantize_mx(out=zc[b, i0][:].bitcast(FP8X4), scales=zs[b, i0][:], in_=z4[:])
+
+        def flux_pass(b, c):
+            if b < HB - 1:
+                codes, scales = zc[b, 0][:, CHUNK * c : CHUNK * (c + 1)], zs[b, 0][:, CHUNK * c : CHUNK * (c + 1)]
+            else:
+                codes, scales = zc[b, CHUNK * c][:], zs[b, CHUNK * c][:]
+            for g in range(NG):
+                for t in range(4):
+                    c0 = 512 * g + P * t
+                    nc.tensor.matmul_mx(
+                        out=banks[NG * c + g][:, CHUNK * t : CHUNK * (t + 1)],
+                        lhsT=w2w[:, 2 * (N * b + c0) : 2 * (N * b + c0 + P)].bitcast(FP4X4),
+                        lhsT_scale=w2s[b][:, c0 : c0 + P],
+                        rhs=codes.bitcast(FP8X4),
+                        rhs_scale=scales,
+                        start=(b == 0 and t == 0),
+                        stop=(b == HB - 1 and t == 3),
+                    )
+
+        out_rows = out_0.rearrange("(g p t) i -> g p t i", p=P, t=4)
+        out_words = out_1.rearrange("g p m t -> p g (m t)").bitcast(I32)
+
+        def hand_out(c):
+            last = c == NC - 1
+            pairs = slice(CHUNK * c, CHUNK * (c + 1))
+            ycodes = ring.tile([P, NG * CHUNK], U32, name="ycodes", align_bytes=64)
+            y, y4 = {}, {}
+            for g in range(NG):
+                y[g] = ring.tile([P, 4 * CHUNK], F32, name="y", bufs=4, align_bytes=64)
+                if last and g == 1:
+                    nc.vector.tensor_copy(out=y[g][:], in_=banks[NG * c + g][:])
+                else:
+                    nc.scalar.copy(out=y[g][:], in_=banks[NG * c + g][:])
+                nc.sync.dma_start(out=out_rows[g, :, :, pairs], in_=y[g][:].rearrange("p (t i) -> p t i", t=4))
+            for g in range(NG):
+                y4[g] = ring.tile([P, 4 * CHUNK], BF16, name="y4", bufs=4, align_bytes=64)
+                if last and g == 1:
+                    nc.vector.tensor_copy(
+                        out=y4[g][:].rearrange("p (c i t) -> p c t i", i=4, t=4),
+                        in_=y[g][:].rearrange("p (t c i) -> p c t i", i=4, t=4),
+                    )
+                else:
+                    nc.scalar.copy(
+                        out=y4[g][:].rearrange("p (i t) -> p i t", t=4), in_=banks[NG * c + g][:].rearrange("p (t i) -> p i t", t=4)
+                    )
+            for g in reversed(range(NG)) if last else range(NG):
+                nc.vector.quantize_mx(
+                    out=ycodes[:, CHUNK * g : CHUNK * (g + 1)].bitcast(FP8X4),
+                    scales=yscales[:, PAIRS * g + CHUNK * c : PAIRS * g + CHUNK * (c + 1)],
+                    in_=y4[g][:],
+                )
+            nc.sync.dma_start(out=out_words[:, :, pairs], in_=ycodes[:].bitcast(I32).rearrange("p (g m) -> p g m", g=NG))
+
+        made = 3
+        for r in range(made):
+            make_h(r)
+        for u in range(len(units) + 2):
+            if u < len(units):
+                pick_substrate(u)
+            if u >= 2:
+                rate(u - 2)
+            if u < len(units):
+                pick_inhibitor(u)
+            if u in (0, 1, 3, 4):
+                round_w1(1 + u // 3, u % 3)
+                quant_w1(1 + u // 3, u % 3)
+            if u < len(units):
+                invert(u)
+            if u >= 2 and units[u - 2][3][-1] == 3:
+                b, i0, w, ts = units[u - 2]
+                quant_z(b, i0, w)
+                if b == 1:
+                    for c in range(NC):
+                        flux_pass(1, c)
+                if b == HB - 1:
+                    flux_pass(b, i0 // CHUNK)
+                    hand_out(i0 // CHUNK)
+            for r in range(made, min(4 * HB, made + (1 if u < 5 else 2))):
+                make_h(r)
+                made = r + 1
+                if r >= 8:
+                    flux_pass(0, r - 8)
+
+        queues = [nc.sync, nc.scalar, nc.sync, nc.scalar]
+        for q in range(4):
+            queues[q].dma_start(
+                out=out_2[:, 4 * q : 4 * q + 4, :].bitcast(I32).rearrange("g r m -> r g m"),
+                in_=yscales[32 * q : 32 * q + 4, :].bitcast(I32).rearrange("p (g m) -> p g m", g=NG),
+            )

@@ -48,7 +48,7 @@ def tile_list_inhibited_enzyme_flux_kernel(
         w1s = [[keep.tile([P, 512], U8, name=f"w1s{b}{a}", align_bytes=64) for a in range(KA)] for b in range(HB)]
         gw = [[keep.tile([P, 512], U32, name=f"gw{a}{f}", align_bytes=64) for f in range(2)] for a in range(KA)]
         gs = [keep.tile([P, 512], U8, name=f"gs{f}", align_bytes=64) for f in range(2)]
-        den = [keep.tile([P, 512], F32, name=f"den{i}") for i in range(2)]
+        picks = [keep.tile([P, 512], F32, name=f"picks{i}") for i in range(4)]
         banks = [psum.tile([P, 512], F32, name=f"bank{i}") for i in range(8)]
         yscales = keep.tile([P, NG * PAIRS], U8, name="yscales", align_bytes=64)
         warm = keep.tile([P, 2], F32, name="warm")
@@ -99,8 +99,8 @@ def tile_list_inhibited_enzyme_flux_kernel(
         def round_w1(b, a, m_vector=0):
             g = ring.tile([P, 2048], BF16, name="w1g", align_bytes=64)
             grouped[b, a] = g
-            dst = g[:].rearrange("p (t m j) -> p m j t", t=4, j=4)
-            src = w1raw[b, a][:].rearrange("p j (m t) -> p m j t", t=4)
+            dst = g[:].rearrange("p (t m j) -> p m t j", t=4, j=4)
+            src = w1raw[b, a][:].rearrange("p j (m t) -> p m t j", t=4)
             if m_vector:
                 nc.vector.tensor_copy(out=dst[:, :m_vector], in_=src[:, :m_vector])
             nc.scalar.copy(out=dst[:, m_vector:], in_=src[:, m_vector:])
@@ -132,7 +132,7 @@ def tile_list_inhibited_enzyme_flux_kernel(
         for b in range(1, HB):
             nc.sync.dma_start(out=w2s[b][0 : P - 4 * b, :].bitcast(I32), in_=w2s[0][4 * b : P, :].bitcast(I32))
 
-        h, sub, zt, zc, zs = {}, {}, {}, {}, {}
+        h, root, half, zc, zs = {}, {}, {}, {}, {}
 
         def make_h(r):
             b, t = divmod(r, 4)
@@ -158,36 +158,41 @@ def tile_list_inhibited_enzyme_flux_kernel(
 
         def pick_substrate(u):
             b, i0, w, ts = units[u]
-            sub[u] = ring.tile([P, 512], F32, name="sub", bufs=3)
             for x, t in enumerate(ts):
-                nc.vector.tensor_copy(sub[u][:, w * x : w * (x + 1)], h[4 * b + t][:].indirect(pos1_t[:, i0 // 16 : (i0 + w) // 16]))
+                nc.vector.tensor_copy(picks[u % 4][:, w * x : w * (x + 1)], h[4 * b + t][:].indirect(pos1_t[:, i0 // 16 : (i0 + w) // 16]))
 
         def pick_inhibitor(u):
             b, i0, w, ts = units[u]
             for x, t in enumerate(ts):
                 cols = slice(w * x, w * (x + 1))
                 nc.vector.tensor_tensor(
-                    den[u % 2][:, cols], h[4 * b + t][:].indirect(pos2_t[:, i0 // 16 : (i0 + w) // 16]), sub[u][:, cols], ALU.add
+                    picks[(u + 2) % 4][:, cols],
+                    h[4 * b + t][:].indirect(pos2_t[:, i0 // 16 : (i0 + w) // 16]),
+                    picks[u % 4][:, cols],
+                    ALU.add,
                 )
 
         def invert(u):
             b, i0, w, ts = units[u]
-            cols = slice(0, w * len(ts))
-            root = ring.tile([P, 512], F32, name="root")
-            nc.scalar.activation(out=root[:, cols], in_=den[u % 2][:, cols], func=ACT.Abs_reciprocal_sqrt, bias=1.0)
-            nc.scalar.activation(out=den[u % 2][:, cols], in_=root[:, cols], func=ACT.Square)
+            if ts[0] == 0:
+                root[b, i0] = ring.tile([P, 4 * w], F32, name="root")
+            nc.scalar.activation(
+                out=root[b, i0][:, w * ts[0] : w * (ts[-1] + 1)],
+                in_=picks[(u + 2) % 4][:, : w * len(ts)],
+                func=ACT.Abs_reciprocal_sqrt,
+                bias=1.0,
+            )
 
         def rate(u):
             b, i0, w, ts = units[u]
             if ts[0] == 0:
-                zt[b, i0] = ring.tile([P, 4 * w], BF16, name="zt", align_bytes=64)
+                half[b, i0] = ring.tile([P, 4 * w], F32, name="half")
             for x, t in enumerate(ts):
-                cols = slice(w * x, w * (x + 1))
                 nc.vector.scalar_tensor_tensor(
-                    out=zt[b, i0][:, w * t : w * (t + 1)],
-                    in0=sub[u][:, cols],
+                    out=half[b, i0][:, w * t : w * (t + 1)],
+                    in0=picks[u % 4][:, w * x : w * (x + 1)],
                     scalar=vm[:, b, t : t + 1],
-                    in1=den[u % 2][:, cols],
+                    in1=root[b, i0][:, w * t : w * (t + 1)],
                     op0=ALU.mult,
                     op1=ALU.mult,
                 )
@@ -196,9 +201,11 @@ def tile_list_inhibited_enzyme_flux_kernel(
             z4 = ring.tile([P, 4 * w], BF16, name="z4", align_bytes=64)
             zc[b, i0] = keep.tile([P, w], U32, name=f"zc{b}_{i0}", align_bytes=64)
             zs[b, i0] = keep.tile([P, w], U8, name=f"zs{b}_{i0}", align_bytes=64)
-            nc.vector.tensor_copy(
-                out=z4[:].rearrange("p (c i t) -> p c t i", i=4, t=4),
-                in_=zt[b, i0][:].rearrange("p (t c i) -> p c t i", i=4, t=4),
+            nc.vector.tensor_tensor(
+                out=z4[:].rearrange("p (c i t) -> p c t i", i=2, t=4),
+                in0=half[b, i0][:].rearrange("p (t c i) -> p c t i", i=2, t=4),
+                in1=root[b, i0][:].rearrange("p (t c i) -> p c t i", i=2, t=4),
+                op=ALU.mult,
             )
             nc.vector.quantize_mx(out=zc[b, i0][:].bitcast(FP8X4), scales=zs[b, i0][:], in_=z4[:])
 

@@ -48,7 +48,7 @@ def tile_list_inhibited_enzyme_flux_kernel(
         w1s = [[keep.tile([P, 512], U8, name=f"w1s{b}{a}", align_bytes=64) for a in range(KA)] for b in range(HB)]
         gw = [[keep.tile([P, 512], U32, name=f"gw{a}{f}", align_bytes=64) for f in range(2)] for a in range(KA)]
         gs = [keep.tile([P, 512], U8, name=f"gs{f}", align_bytes=64) for f in range(2)]
-        picks = [keep.tile([P, 512], F32, name=f"picks{i}") for i in range(4)]
+        picks = [keep.tile([P, 512], F32, name=f"picks{i}") for i in range(5)]
         banks = [psum.tile([P, 512], F32, name=f"bank{i}") for i in range(8)]
         yscales = keep.tile([P, NG * PAIRS], U8, name="yscales", align_bytes=64)
         warm = keep.tile([P, 2], F32, name="warm")
@@ -103,7 +103,10 @@ def tile_list_inhibited_enzyme_flux_kernel(
             src = w1raw[b, a][:].rearrange("p j (m t) -> p m t j", t=4)
             if m_vector:
                 nc.vector.tensor_copy(out=dst[:, :m_vector], in_=src[:, :m_vector])
-            nc.scalar.copy(out=dst[:, m_vector:], in_=src[:, m_vector:])
+                nc.scalar.copy(out=dst[:, m_vector:], in_=src[:, m_vector:])
+            else:
+                for m in range(0, P, P // 4):
+                    nc.scalar.copy(out=dst[:, m : m + P // 4], in_=src[:, m : m + P // 4])
 
         def quant_w1(b, a):
             nc.vector.quantize_mx(out=w1c[b][a][:].bitcast(FP8X4), scales=w1s[b][a][:], in_=grouped[b, a][:])
@@ -156,19 +159,45 @@ def tile_list_inhibited_enzyme_flux_kernel(
         units += [(HB - 1, CHUNK * c, CHUNK, [0, 1, 2, 3]) for c in range(NC - 1)]
         units += [(HB - 1, CHUNK * (NC - 1), CHUNK, ts) for ts in ([0, 1], [2, 3])]
 
-        def pick_substrate(u):
+        lag = [2 if u < 8 else 1 for u in range(len(units))]
+        sub_t, den_t = {}, {}
+        for u in range(len(units)):
+            sub_t[u] = picks[u % 3]
+            den_t[u] = picks[3 + u % 2]
+
+        late = keep.tile([P, NG * 512], F32, name="late", align_bytes=64)
+        last_unit = len(units) - 1
+
+        def den_piece(u, x):
+            w = units[u][2]
+            return late[:, 512 * x : 512 * x + w] if u == last_unit else den_t[u][:, w * x : w * (x + 1)]
+
+        def den_all(u):
+            w, n = units[u][2], len(units[u][3])
+            if u == last_unit:
+                return late[:].rearrange("p (x c) -> p x c", x=n)[:, :, :w]
+            return den_t[u][:, : w * n].rearrange("p (x c) -> p x c", x=n)
+
+        def squared_on_scalar(b, i0):
+            return b == 1 or (b == 2 and i0 < 256)
+
+        def pieces(u):
             b, i0, w, ts = units[u]
-            for x, t in enumerate(ts):
-                nc.vector.tensor_copy(picks[u % 4][:, w * x : w * (x + 1)], h[4 * b + t][:].indirect(pos1_t[:, i0 // 16 : (i0 + w) // 16]))
+            step = min(w, 256)
+            return [(4 * b + t, x, i0, o, step) for x, t in enumerate(ts) for o in range(0, w, step)]
+
+        def pick_substrate(u):
+            w = units[u][2]
+            for r, x, i0, o, n in pieces(u):
+                nc.vector.tensor_copy(sub_t[u][:, w * x + o : w * x + o + n], h[r][:].indirect(pos1_t[:, (i0 + o) // 16 : (i0 + o + n) // 16]))
 
         def pick_inhibitor(u):
-            b, i0, w, ts = units[u]
-            for x, t in enumerate(ts):
-                cols = slice(w * x, w * (x + 1))
+            w = units[u][2]
+            for r, x, i0, o, n in pieces(u):
                 nc.vector.tensor_tensor(
-                    picks[(u + 2) % 4][:, cols],
-                    h[4 * b + t][:].indirect(pos2_t[:, i0 // 16 : (i0 + w) // 16]),
-                    picks[u % 4][:, cols],
+                    den_piece(u, x)[:, o : o + n],
+                    h[r][:].indirect(pos2_t[:, (i0 + o) // 16 : (i0 + o + n) // 16]),
+                    sub_t[u][:, w * x + o : w * x + o + n],
                     ALU.add,
                 )
 
@@ -176,26 +205,40 @@ def tile_list_inhibited_enzyme_flux_kernel(
             b, i0, w, ts = units[u]
             if ts[0] == 0:
                 root[b, i0] = ring.tile([P, 4 * w], F32, name="root")
-            nc.scalar.activation(
-                out=root[b, i0][:, w * ts[0] : w * (ts[-1] + 1)],
-                in_=picks[(u + 2) % 4][:, : w * len(ts)],
-                func=ACT.Abs_reciprocal_sqrt,
-                bias=1.0,
-            )
+            cols = slice(w * ts[0], w * (ts[-1] + 1))
+            den = den_all(u)
+            if squared_on_scalar(b, i0):
+                first = ring.tile([P, 512], F32, name="first")
+                nc.scalar.activation(out=first[:, : w * len(ts)].rearrange("p (x c) -> p x c", c=w), in_=den, func=ACT.Abs_reciprocal_sqrt, bias=1.0)
+                nc.scalar.activation(out=root[b, i0][:, cols], in_=first[:, : w * len(ts)], func=ACT.Square)
+            else:
+                nc.scalar.activation(out=root[b, i0][:, cols].rearrange("p (x c) -> p x c", c=w), in_=den, func=ACT.Abs_reciprocal_sqrt, bias=1.0)
+
+        def scale(u):
+            b, i0, w, ts = units[u]
+            if ts[0] == 0:
+                half[b, i0] = ring.tile([P, 4 * w], F32, name="half", align_bytes=64)
+            if squared_on_scalar(b, i0):
+                for x, t in enumerate(ts):
+                    nc.scalar.activation(
+                        out=half[b, i0][:, w * t : w * (t + 1)],
+                        in_=sub_t[u][:, w * x : w * (x + 1)],
+                        func=ACT.Copy,
+                        scale=vm[:, b, t : t + 1],
+                    )
 
         def rate(u):
             b, i0, w, ts = units[u]
-            if ts[0] == 0:
-                half[b, i0] = ring.tile([P, 4 * w], F32, name="half")
-            for x, t in enumerate(ts):
-                nc.vector.scalar_tensor_tensor(
-                    out=half[b, i0][:, w * t : w * (t + 1)],
-                    in0=picks[u % 4][:, w * x : w * (x + 1)],
-                    scalar=vm[:, b, t : t + 1],
-                    in1=root[b, i0][:, w * t : w * (t + 1)],
-                    op0=ALU.mult,
-                    op1=ALU.mult,
-                )
+            if not squared_on_scalar(b, i0):
+                for x, t in enumerate(ts):
+                    nc.vector.scalar_tensor_tensor(
+                        out=half[b, i0][:, w * t : w * (t + 1)],
+                        in0=sub_t[u][:, w * x : w * (x + 1)],
+                        scalar=vm[:, b, t : t + 1],
+                        in1=root[b, i0][:, w * t : w * (t + 1)],
+                        op0=ALU.mult,
+                        op1=ALU.mult,
+                    )
 
         def quant_z(b, i0, w):
             z4 = ring.tile([P, 4 * w], BF16, name="z4", align_bytes=64)
@@ -230,61 +273,91 @@ def tile_list_inhibited_enzyme_flux_kernel(
         out_rows = out_0.rearrange("(g p t) i -> g p t i", p=P, t=4)
         out_words = out_1.rearrange("g p m t -> p g (m t)").bitcast(I32)
 
-        def hand_out(c):
-            last = c == NC - 1
-            pairs = slice(CHUNK * c, CHUNK * (c + 1))
-            ycodes = ring.tile([P, NG * CHUNK], U32, name="ycodes", align_bytes=64)
-            y, y4 = {}, {}
-            for g in range(NG):
-                y[g] = ring.tile([P, 4 * CHUNK], F32, name="y", bufs=4, align_bytes=64)
-                if last and g == 1:
-                    nc.vector.tensor_copy(out=y[g][:], in_=banks[NG * c + g][:])
-                else:
-                    nc.scalar.copy(out=y[g][:], in_=banks[NG * c + g][:])
-                nc.sync.dma_start(out=out_rows[g, :, :, pairs], in_=y[g][:].rearrange("p (t i) -> p t i", t=4))
-            for g in range(NG):
-                y4[g] = ring.tile([P, 4 * CHUNK], BF16, name="y4", bufs=4, align_bytes=64)
-                if last and g == 1:
-                    nc.vector.tensor_copy(
-                        out=y4[g][:].rearrange("p (c i t) -> p c t i", i=4, t=4),
-                        in_=y[g][:].rearrange("p (t c i) -> p c t i", i=4, t=4),
-                    )
-                else:
-                    nc.scalar.copy(
-                        out=y4[g][:].rearrange("p (i t) -> p i t", t=4), in_=banks[NG * c + g][:].rearrange("p (t i) -> p i t", t=4)
-                    )
-            for g in reversed(range(NG)) if last else range(NG):
-                nc.vector.quantize_mx(
-                    out=ycodes[:, CHUNK * g : CHUNK * (g + 1)].bitcast(FP8X4),
-                    scales=yscales[:, PAIRS * g + CHUNK * c : PAIRS * g + CHUNK * (c + 1)],
-                    in_=y4[g][:],
-                )
-            nc.sync.dma_start(out=out_words[:, :, pairs], in_=ycodes[:].bitcast(I32).rearrange("p (g m) -> p g m", g=NG))
+        y4 = [keep.tile([P, 4 * PAIRS], BF16, name=f"y4{g}", align_bytes=64) for g in range(NG)]
+        ycodes = keep.tile([P, NG * PAIRS], U32, name="ycodes", align_bytes=64)
 
+        def store_rows(c, g):
+            if c == NC - 2:
+                y = late[:, 512 * g : 512 * (g + 1)]
+            else:
+                y = ring.tile([P, 4 * CHUNK], F32, name="y", bufs=4, align_bytes=64)[:]
+            nc.scalar.copy(out=y, in_=banks[NG * c + g][:])
+            nc.sync.dma_start(out=out_rows[g, :, :, CHUNK * c : CHUNK * (c + 1)], in_=y.rearrange("p (t i) -> p t i", t=4))
+            return y
+
+        def round_bank(c, g):
+            nc.scalar.copy(
+                out=y4[g][:, 4 * CHUNK * c : 4 * CHUNK * (c + 1)].rearrange("p (i t) -> p i t", t=4),
+                in_=banks[NG * c + g][:].rearrange("p (t i) -> p i t", t=4),
+            )
+
+        def round_rows(c, g, y):
+            nc.vector.tensor_copy(
+                out=y4[g][:, 4 * CHUNK * c : 4 * CHUNK * (c + 1)].rearrange("p (c i t) -> p c t i", i=4, t=4),
+                in_=y.rearrange("p (t c i) -> p c t i", i=4, t=4),
+            )
+
+        def quant_rows(c0, c1, g):
+            lo, hi = CHUNK * c0, CHUNK * c1
+            nc.vector.quantize_mx(
+                out=ycodes[:, PAIRS * g + lo : PAIRS * g + hi].bitcast(FP8X4),
+                scales=yscales[:, PAIRS * g + lo : PAIRS * g + hi],
+                in_=y4[g][:, 4 * lo : 4 * hi],
+            )
+            if g == NG - 1:
+                nc.sync.dma_start(out=out_words[:, :, lo:hi], in_=ycodes[:].bitcast(I32).rearrange("p (g m) -> p g m", g=NG)[:, :, lo:hi])
+
+        def hand_out(c):
+            if c < NC - 2:
+                for g in range(NG):
+                    store_rows(c, g)
+                    round_bank(c, g)
+                if c == 0:
+                    for g in range(NG):
+                        quant_rows(0, 1, g)
+            elif c == NC - 1:
+                for g in range(NG):
+                    round_rows(c - 1, g, held[g])
+                for g in range(NG):
+                    quant_rows(1, c, g)
+                y = store_rows(c, 0)
+                round_bank(c, 1)
+                round_rows(c, 0, y)
+                quant_rows(c, NC, 0)
+                quant_rows(c, NC, 1)
+                store_rows(c, 1)
+
+        held = []
         made = 3
         for r in range(made):
             make_h(r)
-        for u in range(len(units) + 2):
-            if u < len(units):
+        rated = 0
+        for u in range(len(units) + 1):
+            live = u < len(units)
+            if live:
                 pick_substrate(u)
-            if u >= 2:
-                rate(u - 2)
-            if u < len(units):
+            else:
+                held.extend(store_rows(NC - 2, g) for g in range(NG))
+            finished = list(range(rated, u - lag[u] + 1 if live else u))
+            rated += len(finished)
+            for x in finished:
+                rate(x)
+            if live:
                 pick_inhibitor(u)
+                scale(u)
             if u in (0, 1, 3, 4):
                 round_w1(1 + u // 3, u % 3)
                 quant_w1(1 + u // 3, u % 3)
-            if u < len(units):
+            if live:
                 invert(u)
-            if u >= 2 and units[u - 2][3][-1] == 3:
-                b, i0, w, ts = units[u - 2]
-                quant_z(b, i0, w)
-                if b == 1:
-                    for c in range(NC):
-                        flux_pass(1, c)
-                if b == HB - 1:
-                    flux_pass(b, i0 // CHUNK)
-                    hand_out(i0 // CHUNK)
+            for x in finished:
+                b, i0, w, ts = units[x]
+                if ts[-1] == 3:
+                    quant_z(b, i0, w)
+                    if b == HB - 1:
+                        flux_pass(1, i0 // CHUNK)
+                        flux_pass(b, i0 // CHUNK)
+                        hand_out(i0 // CHUNK)
             for r in range(made, min(4 * HB, made + (1 if u < 5 else 2))):
                 make_h(r)
                 made = r + 1

@@ -70,20 +70,20 @@ def tile_list_inhibited_enzyme_flux_kernel(
         def load_tab(a):
             nc.sync.dma_start(out=tabw[a][:].bitcast(I32), in_=tab_words[a].rearrange("p t i -> p (t i)").bitcast(I32))
 
+        for q in range(4):
+            nc.gpsimd.dma_start(out=tabs[32 * q : 32 * q + 4 * KA, :].bitcast(I32), in_=tab_scales[:, 4 * q : 4 * q + 4, :].bitcast(I32))
         nc.sync.dma_start(offs_t[:], offs)
         load_tab(0)
-        for q in range(4):
-            nc.sync.dma_start(out=tabs[32 * q : 32 * q + 4 * KA, :].bitcast(I32), in_=tab_scales[:, 4 * q : 4 * q + 4, :].bitcast(I32))
         load_w1(0, 0)
         load_tab(1)
         load_w1(0, 1)
-        nc.sync.dma_start(pos1_t[:], pos1)
-        nc.sync.dma_start(pos2_t[:], pos2)
-        nc.sync.dma_start(out=vm[:], in_=vmax.rearrange("(b p t) -> p b t", p=P, t=4))
         nc.sync.dma_start(
             out=w2raw[:].bitcast(I32).rearrange("p (a c) -> p a c", a=HB), in_=w2_words.bitcast(I32).rearrange("a p c -> p a c")
         )
+        nc.sync.dma_start(pos1_t[:], pos1)
+        nc.sync.dma_start(pos2_t[:], pos2)
         load_w1(1, 0)
+        nc.sync.dma_start(out=vm[:], in_=vmax.rearrange("(b p t) -> p b t", p=P, t=4))
         load_w1(1, 1)
         for q in range(4):
             nc.sync.dma_start(out=w2sraw[32 * q : 32 * q + 4 * HB, :].bitcast(I32), in_=w2_scales[:, 4 * q : 4 * q + 4, :].bitcast(I32))
@@ -111,10 +111,10 @@ def tile_list_inhibited_enzyme_flux_kernel(
         def quant_w1(b, a):
             nc.vector.quantize_mx(out=w1c[b][a][:].bitcast(FP8X4), scales=w1s[b][a][:], in_=grouped[b, a][:])
 
-        gather_words(0, 0)
-        gather_words(0, 1)
         gather_scales(0)
         gather_scales(1)
+        gather_words(0, 0)
+        gather_words(0, 1)
         round_w1(0, 0)
         quant_w1(0, 0)
         gather_words(1, 0)

@@ -22,7 +22,18 @@ HB = H // 512
 NG = N // 512
 CHUNK = 128
 NC = PAIRS // CHUNK
-M_VECTOR = 88
+SQ0, SQ1 = 4, 11
+NSUB, NDEN, NFIRST, NH, NG1 = 3, 2, 2, 4, 2
+LAG_A, LAG_B = 1, 2
+MADE, TWO_FROM = 2, 3
+R0, R1, R2, R3 = 0, 0, 3, 2
+SPLIT1 = 1
+NSUB2, NDEN2, OS, OD, NZ, NY, NRC, SKIPA, SKIPB, RELUV = 3, 2, 0, 0, 2, 3, 2, -1, -1, 0
+GA, GB, H1, H2, NRAW, W2AT, SQLATE = 2, 3, -1, 7, 1, 3, 0
+STEP_TO = 8
+ROUND_FIRST = 0
+VM_LATE = 0
+STEP, WIDE, JOINT, STEPW, YS = 256, 0, 0, 256, 0
 
 
 def tile_list_inhibited_enzyme_flux_kernel(
@@ -37,18 +48,17 @@ def tile_list_inhibited_enzyme_flux_kernel(
         offs_t = keep.tile([P, S // 16], U16, name="offs_t")
         pos1_t = keep.tile([P, PAIRS // 16], U16, name="pos1_t")
         pos2_t = keep.tile([P, PAIRS // 16], U16, name="pos2_t")
-        tabw = [keep.tile([P, T], U32, name=f"tabw{a}", align_bytes=64) for a in range(KA)]
-        tabs = keep.tile([P, T], U8, name="tabs", align_bytes=64)
+        tabw = [keep.tile([P, T], U32, name=f"tabw{a}", tag=f"tabw{a}", align_bytes=64) for a in range(KA)]
+        tabs = keep.tile([P, T], U8, name="tabs", tag="tabs", align_bytes=64)
         w2raw = keep.tile([P, HB * 2 * N], U8, name="w2raw", align_bytes=64)
         w2sraw = keep.tile([P, N], U8, name="w2sraw", align_bytes=64)
-        w2w = keep.tile([P, HB * 2 * N], U8, name="w2w", align_bytes=64)
         w2s = [keep.tile([P, N], U8, name=f"w2s{b}", align_bytes=64) for b in range(HB)]
         vm = keep.tile([P, HB, 4], F32, name="vm")
-        w1c = [[keep.tile([P, 512], U32, name=f"w1c{b}{a}", align_bytes=64) for a in range(KA)] for b in range(HB)]
+        w1c = {(b, a): keep.tile([P, 512], U32, name=f"w1c{b}{a}", align_bytes=64) for a in range(KA) for b in range(HB) if (b, a) != (0, 0)}
         w1s = [[keep.tile([P, 512], U8, name=f"w1s{b}{a}", align_bytes=64) for a in range(KA)] for b in range(HB)]
         gw = [[keep.tile([P, 512], U32, name=f"gw{a}{f}", align_bytes=64) for f in range(2)] for a in range(KA)]
         gs = [keep.tile([P, 512], U8, name=f"gs{f}", align_bytes=64) for f in range(2)]
-        picks = [keep.tile([P, 512], F32, name=f"picks{i}") for i in range(5)]
+        picks = [keep.tile([P, 512], F32, name=f"picks{i}") for i in range(NSUB + NDEN)]
         banks = [psum.tile([P, 512], F32, name=f"bank{i}") for i in range(8)]
         yscales = keep.tile([P, NG * PAIRS], U8, name="yscales", align_bytes=64)
         warm = keep.tile([P, 2], F32, name="warm")
@@ -63,28 +73,41 @@ def tile_list_inhibited_enzyme_flux_kernel(
         w1raw = {}
 
         def load_w1(b, a):
-            w1raw[b, a] = ring.tile([P, 4, 512], F32, name="w1raw", bufs=4, align_bytes=64)
+            if a == 1:
+                w1raw[b, a] = keep.tile([P, 4, 512], F32, name=f"w1raw{b}", tag=f"raw{b}", align_bytes=64)
+            else:
+                w1raw[b, a] = ring.tile([P, 4, 512], F32, name="w1raw", bufs=NRAW, align_bytes=64)
             rows = w1[512 * a : 512 * (a + 1), 512 * b : 512 * (b + 1)]
             nc.sync.dma_start(out=w1raw[b, a][:], in_=rows.rearrange("(p j) c -> p j c", j=4))
+
+        def load_w1_half(b, a, x):
+            w1raw[b, a, x] = keep.tile([P, 4, 256], F32, name=f"w1half{x}", align_bytes=64)
+            rows = w1[512 * a : 512 * (a + 1), 512 * b + 256 * x : 512 * b + 256 * (x + 1)]
+            nc.sync.dma_start(out=w1raw[b, a, x][:], in_=rows.rearrange("(p j) c -> p j c", j=4))
 
         def load_tab(a):
             nc.sync.dma_start(out=tabw[a][:].bitcast(I32), in_=tab_words[a].rearrange("p t i -> p (t i)").bitcast(I32))
 
         for q in range(4):
             nc.gpsimd.dma_start(out=tabs[32 * q : 32 * q + 4 * KA, :].bitcast(I32), in_=tab_scales[:, 4 * q : 4 * q + 4, :].bitcast(I32))
-        nc.sync.dma_start(offs_t[:], offs)
         load_tab(0)
+        nc.sync.dma_start(offs_t[:], offs)
         load_w1(0, 0)
         load_tab(1)
-        load_w1(0, 1)
-        nc.sync.dma_start(
-            out=w2raw[:].bitcast(I32).rearrange("p (a c) -> p a c", a=HB), in_=w2_words.bitcast(I32).rearrange("a p c -> p a c")
-        )
+        load_w1_half(0, 1, 0)
+        load_w1_half(0, 1, 1)
         nc.sync.dma_start(pos1_t[:], pos1)
         nc.sync.dma_start(pos2_t[:], pos2)
+        def load_w2(b):
+            nc.sync.dma_start(out=w2raw[:, 2 * N * b : 2 * N * (b + 1)].bitcast(I32), in_=w2_words[b].bitcast(I32))
+
+        for b in range(W2AT):
+            load_w2(b)
         load_w1(1, 0)
         nc.sync.dma_start(out=vm[:], in_=vmax.rearrange("(b p t) -> p b t", p=P, t=4))
         load_w1(1, 1)
+        for b in range(W2AT, HB):
+            load_w2(b)
         for q in range(4):
             nc.sync.dma_start(out=w2sraw[32 * q : 32 * q + 4 * HB, :].bitcast(I32), in_=w2_scales[:, 4 * q : 4 * q + 4, :].bitcast(I32))
 
@@ -96,38 +119,55 @@ def tile_list_inhibited_enzyme_flux_kernel(
 
         grouped = {}
 
-        def round_w1(b, a, m_vector=0):
-            g = ring.tile([P, 2048], BF16, name="w1g", align_bytes=64)
-            grouped[b, a] = g
-            dst = g[:].rearrange("p (t m j) -> p m t j", t=4, j=4)
-            src = w1raw[b, a][:].rearrange("p j (m t) -> p m t j", t=4)
-            if m_vector:
-                nc.vector.tensor_copy(out=dst[:, :m_vector], in_=src[:, :m_vector])
-                nc.scalar.copy(out=dst[:, m_vector:], in_=src[:, m_vector:])
+        def round_piece(copy, g, raw, u, m0, m1, src_m0):
+            dst = g.rearrange("p (t m j) -> p m j t", t=2, j=4)
+            src = raw[:].rearrange("p j (m u t) -> p u m j t", u=2, t=2)
+            copy(out=dst[:, m0:m1], in_=src[:, u, m0 - src_m0 : m1 - src_m0])
+
+        def round_w1(b, a):
+            if b == 2 and (GA, GB)[a] >= 0:
+                grouped[b, a] = keep.tile([P, 2048], BF16, name=f"w1late{a}", tag=f"gate{a}", align_bytes=64)
             else:
-                for m in range(0, P, P // 4):
-                    nc.scalar.copy(out=dst[:, m : m + P // 4], in_=src[:, m : m + P // 4])
+                grouped[b, a] = ring.tile([P, 2048], BF16, name="w1g", bufs=NG1, align_bytes=64)
+            dst = grouped[b, a][:].rearrange("p (t m j) -> p m j t", t=4, j=4)
+            src = w1raw[b, a][:].rearrange("p j (m t) -> p m j t", t=4)
+            for m in range(0, P, P // 4):
+                nc.scalar.copy(out=dst[:, m : m + P // 4], in_=src[:, m : m + P // 4])
+
+        def quant_half(b, a, u):
+            cols = slice(256 * u, 256 * (u + 1))
+            nc.vector.quantize_mx(out=w1c[b, a][:, cols].bitcast(FP8X4), scales=w1s[b][a][:, cols], in_=grouped[b, a, u][:])
 
         def quant_w1(b, a):
-            nc.vector.quantize_mx(out=w1c[b][a][:].bitcast(FP8X4), scales=w1s[b][a][:], in_=grouped[b, a][:])
+            nc.vector.quantize_mx(out=w1c[b, a][:].bitcast(FP8X4), scales=w1s[b][a][:], in_=grouped[b, a][:])
 
-        gather_scales(0)
-        gather_scales(1)
         gather_words(0, 0)
         gather_words(0, 1)
+        gather_scales(0)
+        gather_scales(1)
+        w1c[0, 0] = keep.tile([P, 512], U32, name="w1c00", tag="tabs", align_bytes=64)
         round_w1(0, 0)
         quant_w1(0, 0)
         gather_words(1, 0)
         gather_words(1, 1)
-        round_w1(0, 1, M_VECTOR)
-        quant_w1(0, 1)
+        for u in range(2):
+            grouped[0, 1, u] = keep.tile([P, 1024], BF16, name=f"w1pair{u}", tag=f"w1pair{u}", align_bytes=64)
+            round_piece(nc.scalar.copy, grouped[0, 1, u][:], w1raw[0, 1, 0], u, 0, P // 2, 0)
+        round_piece(nc.vector.tensor_copy, grouped[0, 1, 0][:], w1raw[0, 1, 1], 0, P // 2, P, P // 2)
+        round_piece(nc.scalar.copy, grouped[0, 1, 1][:], w1raw[0, 1, 1], 1, P // 2, P, P // 2)
+        quant_half(0, 1, 0)
+        quant_half(0, 1, 1)
         load_w1(2, 0)
         load_w1(2, 1)
 
-        nc.vector.tensor_copy(
-            out=w2w[:].bitcast(U16).rearrange("p (x t m) -> p x t m", t=4, m=P),
-            in_=w2raw[:].bitcast(U16).rearrange("p (x m t) -> p x t m", t=4, m=P),
-        )
+        w2w = {}
+        for b in range(HB):
+            cols = slice(2 * N * b, 2 * N * (b + 1))
+            w2w[b] = keep.tile([P, 2 * N], U8, name=f"w2w{b}", tag=f"w1pair{b}", align_bytes=64)
+            nc.vector.tensor_copy(
+                out=w2w[b][:].bitcast(U16).rearrange("p (x t m) -> p x t m", t=4, m=P),
+                in_=w2raw[:, cols].bitcast(U16).rearrange("p (x m t) -> p x t m", t=4, m=P),
+            )
         nc.vector.tensor_copy(
             out=w2s[0][:].rearrange("p (g t m) -> p g t m", t=4, m=P),
             in_=w2sraw[:].rearrange("p (g m t) -> p g t m", t=4, m=P),
@@ -139,14 +179,19 @@ def tile_list_inhibited_enzyme_flux_kernel(
 
         def make_h(r):
             b, t = divmod(r, 4)
-            h[r] = ring.tile([P, S], F32, name="h", bufs=6)
+            if r in (GA, GB):
+                h[r] = keep.tile([P, S], F32, name=f"hgate{r}", tag=f"gate{(GA, GB).index(r)}", align_bytes=64)
+            elif r in (H1, H2):
+                h[r] = keep.tile([P, S], F32, name=f"hgate{r}", tag=f"raw{1 + r // 4}", align_bytes=64)
+            else:
+                h[r] = ring.tile([P, S], F32, name="h", bufs=NH)
             cols = slice(P * t, P * (t + 1))
             for f in range(2):
                 acc = banks[(2 * r + f) % 8]
                 for a in range(KA):
                     nc.tensor.matmul_mx(
                         out=acc[:],
-                        lhsT=w1c[b][a][:, cols].bitcast(FP8X4),
+                        lhsT=w1c[b, a][:, cols].bitcast(FP8X4),
                         lhsT_scale=w1s[b][a][:, cols],
                         rhs=gw[a][f][:].bitcast(FP8X4),
                         rhs_scale=gs[f][4 * a : P, :],
@@ -156,14 +201,18 @@ def tile_list_inhibited_enzyme_flux_kernel(
                 nc.scalar.activation(out=h[r][:, 512 * f : 512 * (f + 1)], in_=acc[:], func=ACT.Relu)
 
         units = [(b, 0, PAIRS, [t]) for b in range(HB - 1) for t in range(4)]
-        units += [(HB - 1, CHUNK * c, CHUNK, [0, 1, 2, 3]) for c in range(NC - 1)]
+        if WIDE:
+            units += [(HB - 1, 0, 2 * CHUNK, [0, 1]), (HB - 1, 0, 2 * CHUNK, [2, 3]), (HB - 1, 2 * CHUNK, CHUNK, [0, 1, 2, 3])]
+        else:
+            units += [(HB - 1, CHUNK * c, CHUNK, [0, 1, 2, 3]) for c in range(NC - 1)]
         units += [(HB - 1, CHUNK * (NC - 1), CHUNK, ts) for ts in ([0, 1], [2, 3])]
 
-        lag = [2 if u < 8 else 1 for u in range(len(units))]
+        lag = [LAG_A if u < 8 else LAG_B for u in range(len(units))]
         sub_t, den_t = {}, {}
+        work = [keep.tile([P, T], F32, name=f"work{a}", tag=f"tabw{a}", align_bytes=64) for a in range(KA)]
         for u in range(len(units)):
-            sub_t[u] = picks[u % 3]
-            den_t[u] = picks[3 + u % 2]
+            sub_t[u] = picks[u % NSUB] if u < 8 else picks[(8 + OS + (u - 8) % NSUB2) % NSUB]
+            den_t[u] = picks[NSUB + u % NDEN] if u < 8 else picks[NSUB + (8 + OD + (u - 8) % NDEN2) % NDEN]
 
         late = keep.tile([P, NG * 512], F32, name="late", align_bytes=64)
         last_unit = len(units) - 1
@@ -178,12 +227,12 @@ def tile_list_inhibited_enzyme_flux_kernel(
                 return late[:].rearrange("p (x c) -> p x c", x=n)[:, :, :w]
             return den_t[u][:, : w * n].rearrange("p (x c) -> p x c", x=n)
 
-        def squared_on_scalar(b, i0):
-            return b == 1 or (b == 2 and i0 < 256)
+        def squared_on_scalar(u):
+            return SQ0 <= u < SQ1 and u not in (SKIPA, SKIPB)
 
         def pieces(u):
             b, i0, w, ts = units[u]
-            step = min(w, 256)
+            step = min(w, STEP if u < STEP_TO else 256)
             return [(4 * b + t, x, i0, o, step) for x, t in enumerate(ts) for o in range(0, w, step)]
 
         def pick_substrate(u):
@@ -204,11 +253,11 @@ def tile_list_inhibited_enzyme_flux_kernel(
         def invert(u):
             b, i0, w, ts = units[u]
             if ts[0] == 0:
-                root[b, i0] = ring.tile([P, 4 * w], F32, name="root")
+                root[b, i0] = work[b][:, 2048:] if b < 2 else ring.tile([P, 4 * w], F32, name="rootc", bufs=NRC)
             cols = slice(w * ts[0], w * (ts[-1] + 1))
             den = den_all(u)
-            if squared_on_scalar(b, i0):
-                first = ring.tile([P, 512], F32, name="first")
+            if squared_on_scalar(u):
+                first = ring.tile([P, 512], F32, name="first", bufs=NFIRST)
                 nc.scalar.activation(out=first[:, : w * len(ts)].rearrange("p (x c) -> p x c", c=w), in_=den, func=ACT.Abs_reciprocal_sqrt, bias=1.0)
                 nc.scalar.activation(out=root[b, i0][:, cols], in_=first[:, : w * len(ts)], func=ACT.Square)
             else:
@@ -217,8 +266,8 @@ def tile_list_inhibited_enzyme_flux_kernel(
         def scale(u):
             b, i0, w, ts = units[u]
             if ts[0] == 0:
-                half[b, i0] = ring.tile([P, 4 * w], F32, name="half", align_bytes=64)
-            if squared_on_scalar(b, i0):
+                half[b, i0] = work[b][:, :2048] if b < 2 else ring.tile([P, 4 * w], F32, name="halfc", bufs=NRC, align_bytes=64)
+            if squared_on_scalar(u):
                 for x, t in enumerate(ts):
                     nc.scalar.activation(
                         out=half[b, i0][:, w * t : w * (t + 1)],
@@ -229,7 +278,7 @@ def tile_list_inhibited_enzyme_flux_kernel(
 
         def rate(u):
             b, i0, w, ts = units[u]
-            if not squared_on_scalar(b, i0):
+            if not squared_on_scalar(u):
                 for x, t in enumerate(ts):
                     nc.vector.scalar_tensor_tensor(
                         out=half[b, i0][:, w * t : w * (t + 1)],
@@ -240,29 +289,35 @@ def tile_list_inhibited_enzyme_flux_kernel(
                         op1=ALU.mult,
                     )
 
-        def quant_z(b, i0, w):
-            z4 = ring.tile([P, 4 * w], BF16, name="z4", align_bytes=64)
-            zc[b, i0] = keep.tile([P, w], U32, name=f"zc{b}_{i0}", align_bytes=64)
-            zs[b, i0] = keep.tile([P, w], U8, name=f"zs{b}_{i0}", align_bytes=64)
-            nc.vector.tensor_tensor(
-                out=z4[:].rearrange("p (c i t) -> p c t i", i=2, t=4),
-                in0=half[b, i0][:].rearrange("p (t c i) -> p c t i", i=2, t=4),
-                in1=root[b, i0][:].rearrange("p (t c i) -> p c t i", i=2, t=4),
-                op=ALU.mult,
-            )
-            nc.vector.quantize_mx(out=zc[b, i0][:].bitcast(FP8X4), scales=zs[b, i0][:], in_=z4[:])
+        def weave(out, b, src0, i0, w):
+            hv, rv = [
+                x[b, src0][:].rearrange("p (t c i) -> p c t i", i=2, t=4)[:, (i0 - src0) // 2 : (i0 - src0 + w) // 2] for x in (half, root)
+            ]
+            nc.vector.tensor_tensor(out=out.rearrange("p (c i t) -> p c t i", i=2, t=4), in0=hv, in1=rv, op=ALU.mult)
+
+        def quant_z(parts):
+            width = sum(w for b, src0, i0, w in parts)
+            z4 = ring.tile([P, 4 * width], BF16, name="z4", bufs=NZ, align_bytes=64)
+            name = f"{parts[0][0]}_{parts[0][2]}"
+            codes = keep.tile([P, width], U32, name=f"zc{name}", align_bytes=64)
+            scales = keep.tile([P, width], U8, name=f"zs{name}", align_bytes=64)
+            o = 0
+            for b, src0, i0, w in parts:
+                weave(z4[:, 4 * o : 4 * (o + w)], b, src0, i0, w)
+                for j in range(0, w, CHUNK):
+                    zc[b, (i0 + j) // CHUNK] = codes[:, o + j : o + j + CHUNK]
+                    zs[b, (i0 + j) // CHUNK] = scales[:, o + j : o + j + CHUNK]
+                o += w
+            nc.vector.quantize_mx(out=codes[:].bitcast(FP8X4), scales=scales[:], in_=z4[:])
 
         def flux_pass(b, c):
-            if b < HB - 1:
-                codes, scales = zc[b, 0][:, CHUNK * c : CHUNK * (c + 1)], zs[b, 0][:, CHUNK * c : CHUNK * (c + 1)]
-            else:
-                codes, scales = zc[b, CHUNK * c][:], zs[b, CHUNK * c][:]
+            codes, scales = zc[b, c], zs[b, c]
             for g in range(NG):
                 for t in range(4):
                     c0 = 512 * g + P * t
                     nc.tensor.matmul_mx(
                         out=banks[NG * c + g][:, CHUNK * t : CHUNK * (t + 1)],
-                        lhsT=w2w[:, 2 * (N * b + c0) : 2 * (N * b + c0 + P)].bitcast(FP4X4),
+                        lhsT=w2w[b][:, 2 * c0 : 2 * (c0 + P)].bitcast(FP4X4),
                         lhsT_scale=w2s[b][:, c0 : c0 + P],
                         rhs=codes.bitcast(FP8X4),
                         rhs_scale=scales,
@@ -280,7 +335,7 @@ def tile_list_inhibited_enzyme_flux_kernel(
             if c == NC - 2:
                 y = late[:, 512 * g : 512 * (g + 1)]
             else:
-                y = ring.tile([P, 4 * CHUNK], F32, name="y", bufs=4, align_bytes=64)[:]
+                y = ring.tile([P, 4 * CHUNK], F32, name="y", bufs=NY, align_bytes=64)[:]
             nc.scalar.copy(out=y, in_=banks[NG * c + g][:])
             nc.sync.dma_start(out=out_rows[g, :, :, CHUNK * c : CHUNK * (c + 1)], in_=y.rearrange("p (t i) -> p t i", t=4))
             return y
@@ -317,7 +372,10 @@ def tile_list_inhibited_enzyme_flux_kernel(
                         quant_rows(0, 1, g)
             elif c == NC - 1:
                 for g in range(NG):
-                    round_rows(c - 1, g, held[g])
+                    if g < YS:
+                        round_bank(c - 1, g)
+                    else:
+                        round_rows(c - 1, g, held[g])
                 for g in range(NG):
                     quant_rows(1, c, g)
                 y = store_rows(c, 0)
@@ -328,7 +386,7 @@ def tile_list_inhibited_enzyme_flux_kernel(
                 store_rows(c, 1)
 
         held = []
-        made = 3
+        made = MADE
         for r in range(made):
             make_h(r)
         rated = 0
@@ -344,21 +402,39 @@ def tile_list_inhibited_enzyme_flux_kernel(
                 rate(x)
             if live:
                 pick_inhibitor(u)
-                scale(u)
-            if u in (0, 1, 3, 4):
-                round_w1(1 + u // 3, u % 3)
-                quant_w1(1 + u // 3, u % 3)
-            if live:
+                if not VM_LATE:
+                    scale(u)
+            if live and not ROUND_FIRST:
                 invert(u)
+            for k, at in enumerate((R0, R1, R2, R3)):
+                if u == at:
+                    round_w1(1 + k // 2, k % 2)
+                    quant_w1(1 + k // 2, k % 2)
+            if live and ROUND_FIRST:
+                invert(u)
+            if live and VM_LATE:
+                scale(u)
             for x in finished:
                 b, i0, w, ts = units[x]
                 if ts[-1] == 3:
-                    quant_z(b, i0, w)
+                    if b == 0 or (b == 1 and SPLIT1 == 0):
+                        quant_z([(b, 0, 0, w)])
+                    if b == 1 and SPLIT1 == 2:
+                        quant_z([(b, 0, 0, w // 2)])
                     if b == HB - 1:
-                        flux_pass(1, i0 // CHUNK)
-                        flux_pass(b, i0 // CHUNK)
-                        hand_out(i0 // CHUNK)
-            for r in range(made, min(4 * HB, made + (1 if u < 5 else 2))):
+                        for j0 in range(i0, i0 + w, CHUNK):
+                            if SPLIT1 == 2 and j0 == CHUNK:
+                                quant_z([(1, 0, 2 * CHUNK, 2 * CHUNK)])
+                            if SPLIT1 == 1 and JOINT and j0 < 3 * CHUNK:
+                                quant_z([(1, 0, j0, CHUNK), (b, i0, j0, CHUNK)])
+                            else:
+                                if SPLIT1 == 1:
+                                    quant_z([(1, 0, j0, CHUNK)])
+                                quant_z([(b, i0, j0, CHUNK)])
+                            flux_pass(1, j0 // CHUNK)
+                            flux_pass(b, j0 // CHUNK)
+                            hand_out(j0 // CHUNK)
+            for r in range(made, min(4 * HB, made + (1 if u < TWO_FROM else 2))):
                 make_h(r)
                 made = r + 1
                 if r >= 8:

@@ -21,19 +21,18 @@ KA = K // 512
 HB = H // 512
 NG = N // 512
 CHUNK = 128
+HALF = PAIRS // 2
 NC = PAIRS // CHUNK
-SQ0, SQ1 = 4, 11
-NSUB, NDEN, NFIRST, NH, NG1 = 3, 2, 2, 4, 2
-LAG_A, LAG_B = 1, 2
-MADE, TWO_FROM = 2, 3
-R0, R1, R2, R3 = 0, 0, 3, 2
-SPLIT1 = 1
-NSUB2, NDEN2, OS, OD, NZ, NY, NRC, SKIPA, SKIPB, RELUV = 3, 2, 0, 0, 2, 3, 2, -1, -1, 0
-GA, GB, H1, H2, NRAW, W2AT, SQLATE = 2, 3, -1, 7, 1, 3, 0
-STEP_TO = 8
-ROUND_FIRST = 0
-VM_LATE = 0
-STEP, WIDE, JOINT, STEPW, YS = 256, 0, 0, 256, 0
+ON_VECTOR = ()
+M_VECTOR = {(1, 0): 0, (1, 1): 0, (2, 0): 64, (2, 1): 64}
+CHUNKS_ON_VECTOR = ()
+W2_FIRST = 3
+MV = 128
+YTAG = None
+NH = 12
+H_TAG = {8: "h0", 9: "h1", 11: "h4"}
+PLACED = {"raw10": 12, "h2": 12, "w1g11": 16, "raw11": 0, "h3": 0, "root0": 4, "w1g2": 16}
+SCALEQ = "gpsimd"
 
 
 def tile_list_inhibited_enzyme_flux_kernel(
@@ -42,72 +41,77 @@ def tile_list_inhibited_enzyme_flux_kernel(
     nc = tc.nc
     with ExitStack() as ctx:
         keep = ctx.enter_context(tc.tile_pool(name="keep", bufs=1))
-        ring = ctx.enter_context(tc.tile_pool(name="ring", bufs=2))
+        lay = ctx.enter_context(tc.tile_pool(name="lay", bufs=1))
         psum = ctx.enter_context(tc.psum_pool(name="psum", bufs=1))
+
+        def sb(shape, dtype, name, tag=None):
+            if name in PLACED:
+                return lay.tile(shape, dtype, name=name, offset=1024 * PLACED[name], align_bytes=64)
+            return keep.tile(shape, dtype, name=name, tag=tag or name, align_bytes=64)
 
         offs_t = keep.tile([P, S // 16], U16, name="offs_t")
         pos1_t = keep.tile([P, PAIRS // 16], U16, name="pos1_t")
         pos2_t = keep.tile([P, PAIRS // 16], U16, name="pos2_t")
-        tabw = [keep.tile([P, T], U32, name=f"tabw{a}", tag=f"tabw{a}", align_bytes=64) for a in range(KA)]
-        tabs = keep.tile([P, T], U8, name="tabs", tag="tabs", align_bytes=64)
-        w2raw = keep.tile([P, HB * 2 * N], U8, name="w2raw", align_bytes=64)
-        w2sraw = keep.tile([P, N], U8, name="w2sraw", align_bytes=64)
-        w2s = [keep.tile([P, N], U8, name=f"w2s{b}", align_bytes=64) for b in range(HB)]
-        vm = keep.tile([P, HB, 4], F32, name="vm")
-        w1c = {(b, a): keep.tile([P, 512], U32, name=f"w1c{b}{a}", align_bytes=64) for a in range(KA) for b in range(HB) if (b, a) != (0, 0)}
-        w1s = [[keep.tile([P, 512], U8, name=f"w1s{b}{a}", align_bytes=64) for a in range(KA)] for b in range(HB)]
-        gw = [[keep.tile([P, 512], U32, name=f"gw{a}{f}", align_bytes=64) for f in range(2)] for a in range(KA)]
-        gs = [keep.tile([P, 512], U8, name=f"gs{f}", align_bytes=64) for f in range(2)]
-        picks = [keep.tile([P, 512], F32, name=f"picks{i}") for i in range(NSUB + NDEN)]
+        tabw = [sb([P, T], U32, f"tabw{a}") for a in range(KA)]
+        tabs = sb([P, T], U8, "tabs")
+        w2raw = [sb([P, 2 * N], U8, f"w2raw{b}") for b in range(HB)]
+        w2sraw = sb([P, N], U8, "w2sraw")
+        w2s = {b: sb([P, N], U8, f"w2s{b}") for b in range(1, HB)}
+        vm = sb([P, HB, 4], F32, "vm")
+        w1c = {(b, a): sb([P, 512], U32, f"w1c{b}{a}") for a in range(KA) for b in range(HB - 1) if (b, a) != (0, 0)}
+        w1s = [[sb([P, 512], U8, f"w1s{b}{a}") for a in range(KA)] for b in range(HB - 1)]
+        last_c = sb([P, 1024], U32, "w1c2")
+        last_s = sb([P, 1024], U8, "w1s2")
+        w1s.append([last_s[:, 512 * a : 512 * (a + 1)] for a in range(KA)])
+        for a in range(KA):
+            w1c[2, a] = last_c[:, 512 * a : 512 * (a + 1)]
+        gw = [[sb([P, 512], U32, f"gw{a}{f}") for f in range(2)] for a in range(KA)]
+        gs = [sb([P, 512], U8, f"gs{f}") for f in range(2)]
         banks = [psum.tile([P, 512], F32, name=f"bank{i}") for i in range(8)]
-        yscales = keep.tile([P, NG * PAIRS], U8, name="yscales", align_bytes=64)
+        yscales = sb([P, NG * PAIRS], U8, "yscales")
         warm = keep.tile([P, 2], F32, name="warm")
 
         nc.vector.memset(tabs[:].bitcast(I32), 0)
+        nc.vector.memset(warm[:, 0:1], 1.0)
+        nc.scalar.activation(out=warm[:, 1:2], in_=warm[:, 0:1], func=ACT.Abs_reciprocal_sqrt)
         nc.vector.memset(w2sraw[:].bitcast(I32), 0)
         for b in range(1, HB):
             nc.vector.memset(w2s[b][:].bitcast(I32), 0)
-        nc.vector.memset(warm[:, 0:1], 1.0)
-        nc.scalar.activation(out=warm[:, 1:2], in_=warm[:, 0:1], func=ACT.Abs_reciprocal_sqrt)
 
         w1raw = {}
 
         def load_w1(b, a):
-            if a == 1:
-                w1raw[b, a] = keep.tile([P, 4, 512], F32, name=f"w1raw{b}", tag=f"raw{b}", align_bytes=64)
-            else:
-                w1raw[b, a] = ring.tile([P, 4, 512], F32, name="w1raw", bufs=NRAW, align_bytes=64)
+            w1raw[b, a] = sb([P, 4, 512], F32, f"raw{b}{a}")
             rows = w1[512 * a : 512 * (a + 1), 512 * b : 512 * (b + 1)]
             nc.sync.dma_start(out=w1raw[b, a][:], in_=rows.rearrange("(p j) c -> p j c", j=4))
 
         def load_w1_half(b, a, x):
-            w1raw[b, a, x] = keep.tile([P, 4, 256], F32, name=f"w1half{x}", align_bytes=64)
+            w1raw[b, a, x] = sb([P, 4, 256], F32, f"w1half{x}")
             rows = w1[512 * a : 512 * (a + 1), 512 * b + 256 * x : 512 * b + 256 * (x + 1)]
             nc.sync.dma_start(out=w1raw[b, a, x][:], in_=rows.rearrange("(p j) c -> p j c", j=4))
 
         def load_tab(a):
             nc.sync.dma_start(out=tabw[a][:].bitcast(I32), in_=tab_words[a].rearrange("p t i -> p (t i)").bitcast(I32))
 
+        scale_queue = nc.gpsimd if SCALEQ == "gpsimd" else nc.sync
         for q in range(4):
-            nc.gpsimd.dma_start(out=tabs[32 * q : 32 * q + 4 * KA, :].bitcast(I32), in_=tab_scales[:, 4 * q : 4 * q + 4, :].bitcast(I32))
+            scale_queue.dma_start(out=tabs[32 * q : 32 * q + 4 * KA, :].bitcast(I32), in_=tab_scales[:, 4 * q : 4 * q + 4, :].bitcast(I32))
         load_tab(0)
         nc.sync.dma_start(offs_t[:], offs)
         load_w1(0, 0)
         load_tab(1)
         load_w1_half(0, 1, 0)
         load_w1_half(0, 1, 1)
-        nc.sync.dma_start(pos1_t[:], pos1)
-        nc.sync.dma_start(pos2_t[:], pos2)
-        def load_w2(b):
-            nc.sync.dma_start(out=w2raw[:, 2 * N * b : 2 * N * (b + 1)].bitcast(I32), in_=w2_words[b].bitcast(I32))
-
-        for b in range(W2AT):
-            load_w2(b)
+        for b in range(HB):
+            nc.sync.dma_start(out=w2raw[b][:].bitcast(I32), in_=w2_words[b].bitcast(I32))
+            if b == 0:
+                nc.sync.dma_start(pos1_t[:], pos1)
+                nc.sync.dma_start(pos2_t[:], pos2)
         load_w1(1, 0)
         nc.sync.dma_start(out=vm[:], in_=vmax.rearrange("(b p t) -> p b t", p=P, t=4))
         load_w1(1, 1)
-        for b in range(W2AT, HB):
-            load_w2(b)
+        load_w1(2, 0)
+        load_w1(2, 1)
         for q in range(4):
             nc.sync.dma_start(out=w2sraw[32 * q : 32 * q + 4 * HB, :].bitcast(I32), in_=w2_scales[:, 4 * q : 4 * q + 4, :].bitcast(I32))
 
@@ -119,24 +123,26 @@ def tile_list_inhibited_enzyme_flux_kernel(
 
         grouped = {}
 
-        def round_piece(copy, g, raw, u, m0, m1, src_m0):
+        def round_pair(copy, g, raw, u, m0, m1, src_m0):
             dst = g.rearrange("p (t m j) -> p m j t", t=2, j=4)
             src = raw[:].rearrange("p j (m u t) -> p u m j t", u=2, t=2)
             copy(out=dst[:, m0:m1], in_=src[:, u, m0 - src_m0 : m1 - src_m0])
 
-        def round_w1(b, a):
-            if b == 2 and (GA, GB)[a] >= 0:
-                grouped[b, a] = keep.tile([P, 2048], BF16, name=f"w1late{a}", tag=f"gate{a}", align_bytes=64)
-            else:
-                grouped[b, a] = ring.tile([P, 2048], BF16, name="w1g", bufs=NG1, align_bytes=64)
+        def round_w1(b, a, mv, tag):
+            grouped[b, a] = sb([P, 2048], BF16, f"w1g{b}{a}", tag)
             dst = grouped[b, a][:].rearrange("p (t m j) -> p m j t", t=4, j=4)
             src = w1raw[b, a][:].rearrange("p j (m t) -> p m j t", t=4)
-            for m in range(0, P, P // 4):
-                nc.scalar.copy(out=dst[:, m : m + P // 4], in_=src[:, m : m + P // 4])
+            if mv:
+                nc.vector.tensor_copy(out=dst[:, :mv], in_=src[:, :mv])
+            nc.scalar.copy(out=dst[:, mv:], in_=src[:, mv:])
 
-        def quant_half(b, a, u):
-            cols = slice(256 * u, 256 * (u + 1))
-            nc.vector.quantize_mx(out=w1c[b, a][:, cols].bitcast(FP8X4), scales=w1s[b][a][:, cols], in_=grouped[b, a, u][:])
+        def last_w1():
+            both = sb([P, 4096], BF16, "w1g2", "h3")
+            for a, copy, ms in ((0, nc.vector.tensor_copy, slice(0, MV)), (0, nc.scalar.copy, slice(MV, P)), (1, nc.scalar.copy, slice(0, P))):
+                dst = both[:, 2048 * a : 2048 * (a + 1)].rearrange("p (t m j) -> p m j t", t=4, j=4)
+                if ms.start < ms.stop:
+                    copy(out=dst[:, ms], in_=w1raw[2, a][:].rearrange("p j (m t) -> p m j t", t=4)[:, ms])
+            nc.vector.quantize_mx(out=last_c[:].bitcast(FP8X4), scales=last_s[:], in_=both[:])
 
         def quant_w1(b, a):
             nc.vector.quantize_mx(out=w1c[b, a][:].bitcast(FP8X4), scales=w1s[b][a][:], in_=grouped[b, a][:])
@@ -145,46 +151,43 @@ def tile_list_inhibited_enzyme_flux_kernel(
         gather_words(0, 1)
         gather_scales(0)
         gather_scales(1)
-        w1c[0, 0] = keep.tile([P, 512], U32, name="w1c00", tag="tabs", align_bytes=64)
-        round_w1(0, 0)
+        w1c[0, 0] = sb([P, 512], U32, "w1c00", "tabs")
+        round_w1(0, 0, 0, "g0")
         quant_w1(0, 0)
         gather_words(1, 0)
         gather_words(1, 1)
         for u in range(2):
-            grouped[0, 1, u] = keep.tile([P, 1024], BF16, name=f"w1pair{u}", tag=f"w1pair{u}", align_bytes=64)
-            round_piece(nc.scalar.copy, grouped[0, 1, u][:], w1raw[0, 1, 0], u, 0, P // 2, 0)
-        round_piece(nc.vector.tensor_copy, grouped[0, 1, 0][:], w1raw[0, 1, 1], 0, P // 2, P, P // 2)
-        round_piece(nc.scalar.copy, grouped[0, 1, 1][:], w1raw[0, 1, 1], 1, P // 2, P, P // 2)
-        quant_half(0, 1, 0)
-        quant_half(0, 1, 1)
-        load_w1(2, 0)
-        load_w1(2, 1)
+            grouped[0, 1, u] = sb([P, 1024], BF16, f"w1pair{u}")
+            round_pair(nc.scalar.copy, grouped[0, 1, u][:], w1raw[0, 1, 0], u, 0, P // 2, 0)
+        round_pair(nc.vector.tensor_copy, grouped[0, 1, 0][:], w1raw[0, 1, 1], 0, P // 2, P, P // 2)
+        round_pair(nc.scalar.copy, grouped[0, 1, 1][:], w1raw[0, 1, 1], 1, P // 2, P, P // 2)
+        for u in range(2):
+            cols = slice(256 * u, 256 * (u + 1))
+            nc.vector.quantize_mx(out=w1c[0, 1][:, cols].bitcast(FP8X4), scales=w1s[0][1][:, cols], in_=grouped[0, 1, u][:])
 
         w2w = {}
-        for b in range(HB):
-            cols = slice(2 * N * b, 2 * N * (b + 1))
-            w2w[b] = keep.tile([P, 2 * N], U8, name=f"w2w{b}", tag=f"w1pair{b}", align_bytes=64)
+
+        def deal_words(b, tag):
+            w2w[b] = sb([P, 2 * N], U8, f"w2w{b}", tag)
             nc.vector.tensor_copy(
                 out=w2w[b][:].bitcast(U16).rearrange("p (x t m) -> p x t m", t=4, m=P),
-                in_=w2raw[:, cols].bitcast(U16).rearrange("p (x m t) -> p x t m", t=4, m=P),
+                in_=w2raw[b][:].bitcast(U16).rearrange("p (x m t) -> p x t m", t=4, m=P),
             )
-        nc.vector.tensor_copy(
-            out=w2s[0][:].rearrange("p (g t m) -> p g t m", t=4, m=P),
-            in_=w2sraw[:].rearrange("p (g m t) -> p g t m", t=4, m=P),
-        )
-        for b in range(1, HB):
-            nc.sync.dma_start(out=w2s[b][0 : P - 4 * b, :].bitcast(I32), in_=w2s[0][4 * b : P, :].bitcast(I32))
 
-        h, root, half, zc, zs = {}, {}, {}, {}, {}
+        def deal_scales():
+            w2s[0] = sb([P, N], U8, "w2s0", "h5")
+            nc.vector.tensor_copy(
+                out=w2s[0][:].rearrange("p (g t m) -> p g t m", t=4, m=P),
+                in_=w2sraw[:].rearrange("p (g m t) -> p g t m", t=4, m=P),
+            )
+            for b in range(1, HB):
+                nc.sync.dma_start(out=w2s[b][0 : P - 4 * b, :].bitcast(I32), in_=w2s[0][4 * b : P, :].bitcast(I32))
+
+        h = {}
 
         def make_h(r):
             b, t = divmod(r, 4)
-            if r in (GA, GB):
-                h[r] = keep.tile([P, S], F32, name=f"hgate{r}", tag=f"gate{(GA, GB).index(r)}", align_bytes=64)
-            elif r in (H1, H2):
-                h[r] = keep.tile([P, S], F32, name=f"hgate{r}", tag=f"raw{1 + r // 4}", align_bytes=64)
-            else:
-                h[r] = ring.tile([P, S], F32, name="h", bufs=NH)
+            h[r] = sb([P, S], F32, f"h{r}", H_TAG.get(r, f"h{r % NH}"))
             cols = slice(P * t, P * (t + 1))
             for f in range(2):
                 acc = banks[(2 * r + f) % 8]
@@ -200,118 +203,104 @@ def tile_list_inhibited_enzyme_flux_kernel(
                     )
                 nc.scalar.activation(out=h[r][:, 512 * f : 512 * (f + 1)], in_=acc[:], func=ACT.Relu)
 
-        units = [(b, 0, PAIRS, [t]) for b in range(HB - 1) for t in range(4)]
-        if WIDE:
-            units += [(HB - 1, 0, 2 * CHUNK, [0, 1]), (HB - 1, 0, 2 * CHUNK, [2, 3]), (HB - 1, 2 * CHUNK, CHUNK, [0, 1, 2, 3])]
-        else:
-            units += [(HB - 1, CHUNK * c, CHUNK, [0, 1, 2, 3]) for c in range(NC - 1)]
-        units += [(HB - 1, CHUNK * (NC - 1), CHUNK, ts) for ts in ([0, 1], [2, 3])]
+        work = [sb([P, T], F32, f"work{b}", f"tabw{b}") for b in range(HB - 1)]
+        sub = {b: work[b][:, :2048] for b in range(HB - 1)}
+        root = {1: work[1][:, 2048:]}
+        zc, zs, late, den = {}, {}, {}, {}
 
-        lag = [LAG_A if u < 8 else LAG_B for u in range(len(units))]
-        sub_t, den_t = {}, {}
-        work = [keep.tile([P, T], F32, name=f"work{a}", tag=f"tabw{a}", align_bytes=64) for a in range(KA)]
-        for u in range(len(units)):
-            sub_t[u] = picks[u % NSUB] if u < 8 else picks[(8 + OS + (u - 8) % NSUB2) % NSUB]
-            den_t[u] = picks[NSUB + u % NDEN] if u < 8 else picks[NSUB + (8 + OD + (u - 8) % NDEN2) % NDEN]
+        def pick(dst, den, todo):
+            for r, o, i0, w in todo:
+                nc.vector.tensor_copy(dst[:, o : o + w], h[r][:].indirect(pos1_t[:, i0 // 16 : (i0 + w) // 16]))
+            for r, o, i0, w in todo:
+                nc.vector.tensor_tensor(den[:, o : o + w], h[r][:].indirect(pos2_t[:, i0 // 16 : (i0 + w) // 16]), dst[:, o : o + w], ALU.add)
 
-        late = keep.tile([P, NG * 512], F32, name="late", align_bytes=64)
-        last_unit = len(units) - 1
-
-        def den_piece(u, x):
-            w = units[u][2]
-            return late[:, 512 * x : 512 * x + w] if u == last_unit else den_t[u][:, w * x : w * (x + 1)]
-
-        def den_all(u):
-            w, n = units[u][2], len(units[u][3])
-            if u == last_unit:
-                return late[:].rearrange("p (x c) -> p x c", x=n)[:, :, :w]
-            return den_t[u][:, : w * n].rearrange("p (x c) -> p x c", x=n)
-
-        def squared_on_scalar(u):
-            return SQ0 <= u < SQ1 and u not in (SKIPA, SKIPB)
-
-        def pieces(u):
-            b, i0, w, ts = units[u]
-            step = min(w, STEP if u < STEP_TO else 256)
-            return [(4 * b + t, x, i0, o, step) for x, t in enumerate(ts) for o in range(0, w, step)]
-
-        def pick_substrate(u):
-            w = units[u][2]
-            for r, x, i0, o, n in pieces(u):
-                nc.vector.tensor_copy(sub_t[u][:, w * x + o : w * x + o + n], h[r][:].indirect(pos1_t[:, (i0 + o) // 16 : (i0 + o + n) // 16]))
-
-        def pick_inhibitor(u):
-            w = units[u][2]
-            for r, x, i0, o, n in pieces(u):
-                nc.vector.tensor_tensor(
-                    den_piece(u, x)[:, o : o + n],
-                    h[r][:].indirect(pos2_t[:, (i0 + o) // 16 : (i0 + o + n) // 16]),
-                    sub_t[u][:, w * x + o : w * x + o + n],
-                    ALU.add,
-                )
-
-        def invert(u):
-            b, i0, w, ts = units[u]
-            if ts[0] == 0:
-                root[b, i0] = work[b][:, 2048:] if b < 2 else ring.tile([P, 4 * w], F32, name="rootc", bufs=NRC)
-            cols = slice(w * ts[0], w * (ts[-1] + 1))
-            den = den_all(u)
-            if squared_on_scalar(u):
-                first = ring.tile([P, 512], F32, name="first", bufs=NFIRST)
-                nc.scalar.activation(out=first[:, : w * len(ts)].rearrange("p (x c) -> p x c", c=w), in_=den, func=ACT.Abs_reciprocal_sqrt, bias=1.0)
-                nc.scalar.activation(out=root[b, i0][:, cols], in_=first[:, : w * len(ts)], func=ACT.Square)
+        def pick_slice(r):
+            b, t = divmod(r, 4)
+            if r == 3:
+                root[0] = sb([P, 4 * PAIRS], F32, "root0")[:]
+            if r >= 6 or r < 3:
+                late[r] = sb([P, PAIRS], F32, f"den{r}", f"x{r % 2}" if r > 2 else None)
+                pick(sub[b][:, PAIRS * t :], late[r][:], [(r, i0, i0, HALF) for i0 in (0, HALF)])
             else:
-                nc.scalar.activation(out=root[b, i0][:, cols].rearrange("p (x c) -> p x c", c=w), in_=den, func=ACT.Abs_reciprocal_sqrt, bias=1.0)
+                pick(sub[b], root[b], [(r, PAIRS * t + i0, i0, HALF) for i0 in (0, HALF)])
+            x = sub[b][:, PAIRS * t : PAIRS * (t + 1)]
+            if r != 2:
+                nc.gpsimd.tensor_scalar(out=x, in0=x, scalar1=vm[:, b, t : t + 1], scalar2=0.0, op0=ALU.mult, op1=ALU.add)
 
-        def scale(u):
-            b, i0, w, ts = units[u]
-            if ts[0] == 0:
-                half[b, i0] = work[b][:, :2048] if b < 2 else ring.tile([P, 4 * w], F32, name="halfc", bufs=NRC, align_bytes=64)
-            if squared_on_scalar(u):
-                for x, t in enumerate(ts):
-                    nc.scalar.activation(
-                        out=half[b, i0][:, w * t : w * (t + 1)],
-                        in_=sub_t[u][:, w * x : w * (x + 1)],
-                        func=ACT.Copy,
-                        scale=vm[:, b, t : t + 1],
-                    )
+        def pick_chunk(c):
+            sub[2, c] = sb([P, 4 * CHUNK], F32, f"subc{c}", f"x{c % 2}")[:]
+            den[c] = sb([P, 4 * CHUNK], F32, f"denc{c}")[:]
+            pick(sub[2, c], den[c], [(8 + t, CHUNK * t, CHUNK * c, CHUNK) for t in range(4)])
 
-        def rate(u):
-            b, i0, w, ts = units[u]
-            if not squared_on_scalar(u):
-                for x, t in enumerate(ts):
-                    nc.vector.scalar_tensor_tensor(
-                        out=half[b, i0][:, w * t : w * (t + 1)],
-                        in0=sub_t[u][:, w * x : w * (x + 1)],
-                        scalar=vm[:, b, t : t + 1],
-                        in1=root[b, i0][:, w * t : w * (t + 1)],
-                        op0=ALU.mult,
-                        op1=ALU.mult,
-                    )
+        def invert(x, y):
+            nc.scalar.activation(out=x, in_=y, func=ACT.Abs_reciprocal_sqrt, bias=1.0)
 
-        def weave(out, b, src0, i0, w):
-            hv, rv = [
-                x[b, src0][:].rearrange("p (t c i) -> p c t i", i=2, t=4)[:, (i0 - src0) // 2 : (i0 - src0 + w) // 2] for x in (half, root)
-            ]
+        def square(x, y):
+            nc.scalar.activation(out=x, in_=y, func=ACT.Square)
+
+        def scale(x, b, t):
+            nc.scalar.activation(out=x, in_=x, func=ACT.Copy, scale=vm[:, b, t : t + 1])
+
+        def rate(x, y, b, t):
+            nc.vector.scalar_tensor_tensor(out=x, in0=x, scalar=vm[:, b, t : t + 1], in1=y, op0=ALU.mult, op1=ALU.mult)
+
+        def invert_slice(r, i0=0, i1=PAIRS):
+            b, t = divmod(r, 4)
+            x = root[b][:, PAIRS * t + i0 : PAIRS * t + i1]
+            invert(x, late[r][:, i0:i1] if r in late else x)
+
+        def finish_slice(r):
+            b, t = divmod(r, 4)
+            cols = slice(PAIRS * t, PAIRS * (t + 1))
+            if r in ON_VECTOR:
+                rate(sub[b][:, cols], root[b][:, cols], b, t)
+            else:
+                scale(sub[b][:, cols], b, t)
+                square(root[b][:, cols], root[b][:, cols])
+
+        def finish_half(b, ts, i0):
+            x = root[b].rearrange("p (t i) -> p t i", t=4)[:, ts[0] : ts[-1] + 1, i0 : i0 + HALF]
+            square(x, x)
+            if b == 0:
+                scale(root[0][:, PAIRS * 2 + i0 : PAIRS * 2 + i0 + HALF], 0, 2)
+
+        def finish_chunk(c):
+            invert(den[c], den[c])
+            root[2, c] = den[c] if c in CHUNKS_ON_VECTOR else sb([P, 4 * CHUNK], F32, f"rootc{c}")[:]
+            for t in range(4):
+                cols = slice(CHUNK * t, CHUNK * (t + 1))
+                if c in CHUNKS_ON_VECTOR:
+                    rate(sub[2, c][:, cols], root[2, c][:, cols], 2, t)
+                else:
+                    scale(sub[2, c][:, cols], 2, t)
+            if c not in CHUNKS_ON_VECTOR:
+                square(root[2, c], den[c])
+
+        def weave(out, key, i0, w):
+            hv, rv = [v[key].rearrange("p (t c i) -> p c t i", i=2, t=4)[:, i0 // 2 : (i0 + w) // 2] for v in (sub, root)]
             nc.vector.tensor_tensor(out=out.rearrange("p (c i t) -> p c t i", i=2, t=4), in0=hv, in1=rv, op=ALU.mult)
 
-        def quant_z(parts):
-            width = sum(w for b, src0, i0, w in parts)
-            z4 = ring.tile([P, 4 * width], BF16, name="z4", bufs=NZ, align_bytes=64)
-            name = f"{parts[0][0]}_{parts[0][2]}"
-            codes = keep.tile([P, width], U32, name=f"zc{name}", align_bytes=64)
-            scales = keep.tile([P, width], U8, name=f"zs{name}", align_bytes=64)
-            o = 0
-            for b, src0, i0, w in parts:
-                weave(z4[:, 4 * o : 4 * (o + w)], b, src0, i0, w)
-                for j in range(0, w, CHUNK):
-                    zc[b, (i0 + j) // CHUNK] = codes[:, o + j : o + j + CHUNK]
-                    zs[b, (i0 + j) // CHUNK] = scales[:, o + j : o + j + CHUNK]
-                o += w
-            nc.vector.quantize_mx(out=codes[:].bitcast(FP8X4), scales=scales[:], in_=z4[:])
+        def quant_z(z4, name, parts):
+            width = CHUNK * len(parts)
+            codes = sb([P, width], U32, f"zc{name}")
+            scales = sb([P, width], U8, f"zs{name}")
+            for k, key in enumerate(parts):
+                zc[key] = codes[:, CHUNK * k : CHUNK * (k + 1)]
+                zs[key] = scales[:, CHUNK * k : CHUNK * (k + 1)]
+            nc.vector.quantize_mx(out=codes[:].bitcast(FP8X4), scales=scales[:], in_=z4)
 
-        def flux_pass(b, c):
-            codes, scales = zc[b, c], zs[b, c]
+        def rates_early(c):
+            z4 = sb([P, 8 * CHUNK], BF16, f"z4e{c}", f"denc{c - 1}" if c else None)
+            for b in range(HB - 1):
+                weave(z4[:, 4 * CHUNK * b : 4 * CHUNK * (b + 1)], b, CHUNK * c, CHUNK)
+            quant_z(z4[:], f"e{c}", [(0, c), (1, c)])
+
+        def rates_last(c):
+            z4 = sb([P, 4 * CHUNK], BF16, f"z4l{c}", f"z4l{c % 2}")
+            weave(z4[:], (2, c), 0, CHUNK)
+            quant_z(z4[:], f"l{c}", [(2, c)])
+
+        def flux_pass(b, c, first=0):
             for g in range(NG):
                 for t in range(4):
                     c0 = 512 * g + P * t
@@ -319,25 +308,23 @@ def tile_list_inhibited_enzyme_flux_kernel(
                         out=banks[NG * c + g][:, CHUNK * t : CHUNK * (t + 1)],
                         lhsT=w2w[b][:, 2 * c0 : 2 * (c0 + P)].bitcast(FP4X4),
                         lhsT_scale=w2s[b][:, c0 : c0 + P],
-                        rhs=codes.bitcast(FP8X4),
-                        rhs_scale=scales,
-                        start=(b == 0 and t == 0),
+                        rhs=zc[b, c].bitcast(FP8X4),
+                        rhs_scale=zs[b, c],
+                        start=(b == first and t == 0),
                         stop=(b == HB - 1 and t == 3),
                     )
 
         out_rows = out_0.rearrange("(g p t) i -> g p t i", p=P, t=4)
         out_words = out_1.rearrange("g p m t -> p g (m t)").bitcast(I32)
+        y4 = [sb([P, 4 * PAIRS], BF16, f"y4{g}") for g in range(NG)]
 
-        y4 = [keep.tile([P, 4 * PAIRS], BF16, name=f"y4{g}", align_bytes=64) for g in range(NG)]
-        ycodes = keep.tile([P, NG * PAIRS], U32, name="ycodes", align_bytes=64)
-
-        def store_rows(c, g):
-            if c == NC - 2:
-                y = late[:, 512 * g : 512 * (g + 1)]
-            else:
-                y = ring.tile([P, 4 * CHUNK], F32, name="y", bufs=NY, align_bytes=64)[:]
-            nc.scalar.copy(out=y, in_=banks[NG * c + g][:])
-            nc.sync.dma_start(out=out_rows[g, :, :, CHUNK * c : CHUNK * (c + 1)], in_=y.rearrange("p (t i) -> p t i", t=4))
+        def store_rows(c0, c1, g, tag):
+            w = CHUNK * (c1 - c0)
+            y = sb([P, 4, w], F32, f"y{c0}{g}", tag)
+            for c in range(c0, c1):
+                o = CHUNK * (c - c0)
+                nc.scalar.copy(out=y[:, :, o : o + CHUNK], in_=banks[NG * c + g][:].rearrange("p (t i) -> p t i", t=4))
+            nc.sync.dma_start(out=out_rows[g, :, :, CHUNK * c0 : CHUNK * c1], in_=y[:])
             return y
 
         def round_bank(c, g):
@@ -349,96 +336,113 @@ def tile_list_inhibited_enzyme_flux_kernel(
         def round_rows(c, g, y):
             nc.vector.tensor_copy(
                 out=y4[g][:, 4 * CHUNK * c : 4 * CHUNK * (c + 1)].rearrange("p (c i t) -> p c t i", i=4, t=4),
-                in_=y.rearrange("p (t c i) -> p c t i", i=4, t=4),
+                in_=y[:].rearrange("p t (c i) -> p c t i", i=4),
             )
 
+        planes = []
+
         def quant_rows(c0, c1, g):
+            if not planes:
+                planes.append(sb([P, NG * PAIRS], U32, "ycodes", YTAG))
+            ycodes = planes[0]
             lo, hi = CHUNK * c0, CHUNK * c1
             nc.vector.quantize_mx(
                 out=ycodes[:, PAIRS * g + lo : PAIRS * g + hi].bitcast(FP8X4),
                 scales=yscales[:, PAIRS * g + lo : PAIRS * g + hi],
                 in_=y4[g][:, 4 * lo : 4 * hi],
             )
-            if g == NG - 1:
-                nc.sync.dma_start(out=out_words[:, :, lo:hi], in_=ycodes[:].bitcast(I32).rearrange("p (g m) -> p g m", g=NG)[:, :, lo:hi])
 
-        def hand_out(c):
-            if c < NC - 2:
-                for g in range(NG):
-                    store_rows(c, g)
-                    round_bank(c, g)
-                if c == 0:
-                    for g in range(NG):
-                        quant_rows(0, 1, g)
-            elif c == NC - 1:
-                for g in range(NG):
-                    if g < YS:
-                        round_bank(c - 1, g)
-                    else:
-                        round_rows(c - 1, g, held[g])
-                for g in range(NG):
-                    quant_rows(1, c, g)
-                y = store_rows(c, 0)
-                round_bank(c, 1)
-                round_rows(c, 0, y)
-                quant_rows(c, NC, 0)
-                quant_rows(c, NC, 1)
-                store_rows(c, 1)
+        def store_codes(c0, c1):
+            lo, hi = CHUNK * c0, CHUNK * c1
+            nc.sync.dma_start(out=out_words[:, :, lo:hi], in_=planes[0][:].bitcast(I32).rearrange("p (g m) -> p g m", g=NG)[:, :, lo:hi])
 
-        held = []
-        made = MADE
-        for r in range(made):
+        for b in range(HB):
+            deal_words(b, f"w1pair{b}")
+
+        def step_w1(b, a, tag):
+            round_w1(b, a, M_VECTOR[b, a], tag)
+            quant_w1(b, a)
+
+        def step_h(r):
             make_h(r)
-        rated = 0
-        for u in range(len(units) + 1):
-            live = u < len(units)
-            if live:
-                pick_substrate(u)
-            else:
-                held.extend(store_rows(NC - 2, g) for g in range(NG))
-            finished = list(range(rated, u - lag[u] + 1 if live else u))
-            rated += len(finished)
-            for x in finished:
-                rate(x)
-            if live:
-                pick_inhibitor(u)
-                if not VM_LATE:
-                    scale(u)
-            if live and not ROUND_FIRST:
-                invert(u)
-            for k, at in enumerate((R0, R1, R2, R3)):
-                if u == at:
-                    round_w1(1 + k // 2, k % 2)
-                    quant_w1(1 + k // 2, k % 2)
-            if live and ROUND_FIRST:
-                invert(u)
-            if live and VM_LATE:
-                scale(u)
-            for x in finished:
-                b, i0, w, ts = units[x]
-                if ts[-1] == 3:
-                    if b == 0 or (b == 1 and SPLIT1 == 0):
-                        quant_z([(b, 0, 0, w)])
-                    if b == 1 and SPLIT1 == 2:
-                        quant_z([(b, 0, 0, w // 2)])
-                    if b == HB - 1:
-                        for j0 in range(i0, i0 + w, CHUNK):
-                            if SPLIT1 == 2 and j0 == CHUNK:
-                                quant_z([(1, 0, 2 * CHUNK, 2 * CHUNK)])
-                            if SPLIT1 == 1 and JOINT and j0 < 3 * CHUNK:
-                                quant_z([(1, 0, j0, CHUNK), (b, i0, j0, CHUNK)])
-                            else:
-                                if SPLIT1 == 1:
-                                    quant_z([(1, 0, j0, CHUNK)])
-                                quant_z([(b, i0, j0, CHUNK)])
-                            flux_pass(1, j0 // CHUNK)
-                            flux_pass(b, j0 // CHUNK)
-                            hand_out(j0 // CHUNK)
-            for r in range(made, min(4 * HB, made + (1 if u < TWO_FROM else 2))):
-                make_h(r)
-                made = r + 1
-                if r >= 8:
-                    flux_pass(0, r - 8)
+            if r < 8:
+                pick_slice(r)
+
+        def last_rates(c):
+            rates_last(c)
+            flux_pass(2, c)
+
+        def early_rates(c):
+            rates_early(c)
+            for b in range(HB - 1):
+                flux_pass(b, c)
+
+        step_h(0)
+        step_h(1)
+        step_w1(1, 0, "g1")
+        step_h(2)
+        step_w1(1, 1, "g0")
+        step_h(3)
+        invert_slice(0)
+        invert_slice(1)
+        step_h(4)
+        last_w1()
+        step_h(5)
+        invert_slice(2)
+        step_h(6)
+        deal_scales()
+        step_h(7)
+        invert_slice(3)
+        step_h(8)
+        step_h(9)
+        step_h(10)
+        step_h(11)
+        invert_slice(6)
+        pick_chunk(0)
+        finish_half(0, [0, 1, 2, 3], 0)
+        invert_slice(4)
+        invert_slice(5)
+        invert_slice(7)
+        pick_chunk(1)
+        finish_half(1, [0, 1, 2, 3], 0)
+        early_rates(0)
+        finish_chunk(0)
+        last_rates(0)
+        early_rates(1)
+        pick_chunk(2)
+        finish_half(0, [0, 1, 2, 3], HALF)
+        finish_half(1, [0, 1, 2, 3], HALF)
+        finish_chunk(1)
+        last_rates(1)
+        early_rates(2)
+        pick_chunk(3)
+        for g in range(NG):
+            store_rows(0, 1, g, ("raw00", "raw20")[g])
+        for g in range(NG):
+            round_bank(0, g)
+        finish_chunk(2)
+        last_rates(2)
+        early_rates(3)
+        for g in range(NG):
+            store_rows(1, 2, g, ("raw21", "w1half0")[g])
+        for g in range(NG):
+            round_bank(1, g)
+        finish_chunk(3)
+        last_rates(3)
+        for g in range(NG):
+            quant_rows(0, 2, g)
+        store_codes(0, 2)
+        held = [store_rows(2, 3, g, f"y2{g}") for g in range(NG)]
+        round_bank(2, 0)
+        round_rows(2, 1, held[1])
+        for g in range(NG):
+            quant_rows(2, 3, g)
+        store_codes(2, 3)
+        for g in range(NG):
+            round_rows(3, g, store_rows(3, 4, g, f"y3{g}"))
+        for g in range(NG):
+            quant_rows(3, 4, g)
+        store_codes(3, 4)
 
         queues = [nc.sync, nc.scalar, nc.sync, nc.scalar]
         for q in range(4):

@@ -20,19 +20,16 @@ P = 128
 KA = K // 512
 HB = H // 512
 NG = N // 512
+LAST = HB - 1
 CHUNK = 128
-HALF = PAIRS // 2
 NC = PAIRS // CHUNK
-ON_VECTOR = ()
-M_VECTOR = {(1, 0): 0, (1, 1): 0, (2, 0): 64, (2, 1): 64}
-CHUNKS_ON_VECTOR = ()
-W2_FIRST = 3
-MV = 128
-YTAG = None
-NH = 12
-H_TAG = {8: "h0", 9: "h1", 11: "h4"}
+HALF = PAIRS // 2
+M_VECTOR = 64
+
 PLACED = {"raw10": 12, "h2": 12, "w1g11": 16, "raw11": 0, "h3": 0, "root0": 4, "w1g2": 16}
-SCALEQ = "gpsimd"
+H_TAG = {8: "h0", 9: "h1", 11: "h4"}
+SUMS_APART = (0, 1, 2, 6, 7)
+VMAX_ON_ROOT = 2
 
 
 def tile_list_inhibited_enzyme_flux_kernel(
@@ -58,13 +55,13 @@ def tile_list_inhibited_enzyme_flux_kernel(
         w2sraw = sb([P, N], U8, "w2sraw")
         w2s = {b: sb([P, N], U8, f"w2s{b}") for b in range(1, HB)}
         vm = sb([P, HB, 4], F32, "vm")
-        w1c = {(b, a): sb([P, 512], U32, f"w1c{b}{a}") for a in range(KA) for b in range(HB - 1) if (b, a) != (0, 0)}
-        w1s = [[sb([P, 512], U8, f"w1s{b}{a}") for a in range(KA)] for b in range(HB - 1)]
-        last_c = sb([P, 1024], U32, "w1c2")
-        last_s = sb([P, 1024], U8, "w1s2")
-        w1s.append([last_s[:, 512 * a : 512 * (a + 1)] for a in range(KA)])
+        w1c = {(b, a): sb([P, 512], U32, f"w1c{b}{a}") for a in range(KA) for b in range(LAST) if (b, a) != (0, 0)}
+        w1s = {(b, a): sb([P, 512], U8, f"w1s{b}{a}") for b in range(LAST) for a in range(KA)}
+        last_codes = sb([P, KA * 512], U32, "last_codes")
+        last_scales = sb([P, KA * 512], U8, "last_scales")
         for a in range(KA):
-            w1c[2, a] = last_c[:, 512 * a : 512 * (a + 1)]
+            w1c[LAST, a] = last_codes[:, 512 * a : 512 * (a + 1)]
+            w1s[LAST, a] = last_scales[:, 512 * a : 512 * (a + 1)]
         gw = [[sb([P, 512], U32, f"gw{a}{f}") for f in range(2)] for a in range(KA)]
         gs = [sb([P, 512], U8, f"gs{f}") for f in range(2)]
         banks = [psum.tile([P, 512], F32, name=f"bank{i}") for i in range(8)]
@@ -85,23 +82,19 @@ def tile_list_inhibited_enzyme_flux_kernel(
             rows = w1[512 * a : 512 * (a + 1), 512 * b : 512 * (b + 1)]
             nc.sync.dma_start(out=w1raw[b, a][:], in_=rows.rearrange("(p j) c -> p j c", j=4))
 
-        def load_w1_half(b, a, x):
-            w1raw[b, a, x] = sb([P, 4, 256], F32, f"w1half{x}")
-            rows = w1[512 * a : 512 * (a + 1), 512 * b + 256 * x : 512 * b + 256 * (x + 1)]
-            nc.sync.dma_start(out=w1raw[b, a, x][:], in_=rows.rearrange("(p j) c -> p j c", j=4))
-
         def load_tab(a):
             nc.sync.dma_start(out=tabw[a][:].bitcast(I32), in_=tab_words[a].rearrange("p t i -> p (t i)").bitcast(I32))
 
-        scale_queue = nc.gpsimd if SCALEQ == "gpsimd" else nc.sync
         for q in range(4):
-            scale_queue.dma_start(out=tabs[32 * q : 32 * q + 4 * KA, :].bitcast(I32), in_=tab_scales[:, 4 * q : 4 * q + 4, :].bitcast(I32))
+            nc.gpsimd.dma_start(out=tabs[32 * q : 32 * q + 4 * KA, :].bitcast(I32), in_=tab_scales[:, 4 * q : 4 * q + 4, :].bitcast(I32))
         load_tab(0)
         nc.sync.dma_start(offs_t[:], offs)
         load_w1(0, 0)
         load_tab(1)
-        load_w1_half(0, 1, 0)
-        load_w1_half(0, 1, 1)
+        w1half = []
+        for x in range(2):
+            w1half.append(sb([P, 4, 256], F32, f"w1half{x}"))
+            nc.sync.dma_start(out=w1half[x][:], in_=w1[512:1024, 256 * x : 256 * (x + 1)].rearrange("(p j) c -> p j c", j=4))
         for b in range(HB):
             nc.sync.dma_start(out=w2raw[b][:].bitcast(I32), in_=w2_words[b].bitcast(I32))
             if b == 0:
@@ -110,68 +103,57 @@ def tile_list_inhibited_enzyme_flux_kernel(
         load_w1(1, 0)
         nc.sync.dma_start(out=vm[:], in_=vmax.rearrange("(b p t) -> p b t", p=P, t=4))
         load_w1(1, 1)
-        load_w1(2, 0)
-        load_w1(2, 1)
+        for a in range(KA):
+            load_w1(LAST, a)
         for q in range(4):
             nc.sync.dma_start(out=w2sraw[32 * q : 32 * q + 4 * HB, :].bitcast(I32), in_=w2_scales[:, 4 * q : 4 * q + 4, :].bitcast(I32))
 
-        def gather_words(a, f):
-            nc.vector.tensor_copy(gw[a][f][:], tabw[a][:].indirect(offs_t[:, 32 * f : 32 * (f + 1)]))
+        def gather_words(a):
+            for f in range(2):
+                nc.vector.tensor_copy(gw[a][f][:], tabw[a][:].indirect(offs_t[:, 32 * f : 32 * (f + 1)]))
 
-        def gather_scales(f):
+        def round_block(copy, out, raw, ms=slice(0, P)):
+            copy(out=out.rearrange("p (t m j) -> p m j t", t=4, j=4)[:, ms], in_=raw[:].rearrange("p j (m t) -> p m j t", t=4)[:, ms])
+
+        def quantise_block(b, a, tag):
+            rounded = sb([P, 2048], BF16, f"w1g{b}{a}", tag)
+            round_block(nc.scalar.copy, rounded[:], w1raw[b, a])
+            nc.vector.quantize_mx(out=w1c[b, a][:].bitcast(FP8X4), scales=w1s[b, a][:], in_=rounded[:])
+
+        def round_pair(copy, out, u, x):
+            dst = out[:].rearrange("p (t m j) -> p m j t", t=2, j=4)[:, 64 * x : 64 * (x + 1)]
+            copy(out=dst, in_=w1half[x][:].rearrange("p j (m u t) -> p u m j t", u=2, t=2)[:, u])
+
+        def quantise_last_pass():
+            rounded = sb([P, KA * 2048], BF16, "w1g2")
+            round_block(nc.vector.tensor_copy, rounded[:, :2048], w1raw[LAST, 0], slice(0, M_VECTOR))
+            round_block(nc.scalar.copy, rounded[:, 2048:], w1raw[LAST, 1])
+            round_block(nc.scalar.copy, rounded[:, :2048], w1raw[LAST, 0], slice(M_VECTOR, P))
+            nc.vector.quantize_mx(out=last_codes[:].bitcast(FP8X4), scales=last_scales[:], in_=rounded[:])
+
+        gather_words(0)
+        for f in range(2):
             nc.vector.tensor_copy(gs[f][:], tabs[:].indirect(offs_t[:, 32 * f : 32 * (f + 1)]))
-
-        grouped = {}
-
-        def round_pair(copy, g, raw, u, m0, m1, src_m0):
-            dst = g.rearrange("p (t m j) -> p m j t", t=2, j=4)
-            src = raw[:].rearrange("p j (m u t) -> p u m j t", u=2, t=2)
-            copy(out=dst[:, m0:m1], in_=src[:, u, m0 - src_m0 : m1 - src_m0])
-
-        def round_w1(b, a, mv, tag):
-            grouped[b, a] = sb([P, 2048], BF16, f"w1g{b}{a}", tag)
-            dst = grouped[b, a][:].rearrange("p (t m j) -> p m j t", t=4, j=4)
-            src = w1raw[b, a][:].rearrange("p j (m t) -> p m j t", t=4)
-            if mv:
-                nc.vector.tensor_copy(out=dst[:, :mv], in_=src[:, :mv])
-            nc.scalar.copy(out=dst[:, mv:], in_=src[:, mv:])
-
-        def last_w1():
-            both = sb([P, 4096], BF16, "w1g2", "h3")
-            for a, copy, ms in ((0, nc.vector.tensor_copy, slice(0, MV)), (0, nc.scalar.copy, slice(MV, P)), (1, nc.scalar.copy, slice(0, P))):
-                dst = both[:, 2048 * a : 2048 * (a + 1)].rearrange("p (t m j) -> p m j t", t=4, j=4)
-                if ms.start < ms.stop:
-                    copy(out=dst[:, ms], in_=w1raw[2, a][:].rearrange("p j (m t) -> p m j t", t=4)[:, ms])
-            nc.vector.quantize_mx(out=last_c[:].bitcast(FP8X4), scales=last_s[:], in_=both[:])
-
-        def quant_w1(b, a):
-            nc.vector.quantize_mx(out=w1c[b, a][:].bitcast(FP8X4), scales=w1s[b][a][:], in_=grouped[b, a][:])
-
-        gather_words(0, 0)
-        gather_words(0, 1)
-        gather_scales(0)
-        gather_scales(1)
         w1c[0, 0] = sb([P, 512], U32, "w1c00", "tabs")
-        round_w1(0, 0, 0, "g0")
-        quant_w1(0, 0)
-        gather_words(1, 0)
-        gather_words(1, 1)
+        quantise_block(0, 0, None)
+        gather_words(1)
+        pairs = []
         for u in range(2):
-            grouped[0, 1, u] = sb([P, 1024], BF16, f"w1pair{u}")
-            round_pair(nc.scalar.copy, grouped[0, 1, u][:], w1raw[0, 1, 0], u, 0, P // 2, 0)
-        round_pair(nc.vector.tensor_copy, grouped[0, 1, 0][:], w1raw[0, 1, 1], 0, P // 2, P, P // 2)
-        round_pair(nc.scalar.copy, grouped[0, 1, 1][:], w1raw[0, 1, 1], 1, P // 2, P, P // 2)
+            pairs.append(sb([P, 1024], BF16, f"w1pair{u}"))
+            round_pair(nc.scalar.copy, pairs[u], u, 0)
+        for u, copy in enumerate((nc.vector.tensor_copy, nc.scalar.copy)):
+            round_pair(copy, pairs[u], u, 1)
         for u in range(2):
             cols = slice(256 * u, 256 * (u + 1))
-            nc.vector.quantize_mx(out=w1c[0, 1][:, cols].bitcast(FP8X4), scales=w1s[0][1][:, cols], in_=grouped[0, 1, u][:])
+            nc.vector.quantize_mx(out=w1c[0, 1][:, cols].bitcast(FP8X4), scales=w1s[0, 1][:, cols], in_=pairs[u][:])
 
-        w2w = {}
+        w2w = []
 
-        def deal_words(b, tag):
-            w2w[b] = sb([P, 2 * N], U8, f"w2w{b}", tag)
+        def deal_words(b):
+            w2w.append(sb([P, 2 * N], U8, f"w2w{b}", f"w1pair{b}"))
             nc.vector.tensor_copy(
-                out=w2w[b][:].bitcast(U16).rearrange("p (x t m) -> p x t m", t=4, m=P),
-                in_=w2raw[b][:].bitcast(U16).rearrange("p (x m t) -> p x t m", t=4, m=P),
+                out=w2w[b][:].bitcast(U16).rearrange("p (g t m) -> p g t m", t=4, m=P),
+                in_=w2raw[b][:].bitcast(U16).rearrange("p (g m t) -> p g t m", t=4, m=P),
             )
 
         def deal_scales():
@@ -183,11 +165,14 @@ def tile_list_inhibited_enzyme_flux_kernel(
             for b in range(1, HB):
                 nc.sync.dma_start(out=w2s[b][0 : P - 4 * b, :].bitcast(I32), in_=w2s[0][4 * b : P, :].bitcast(I32))
 
-        h = {}
+        h, sums = {}, {}
+        work = [sb([P, T], F32, f"work{b}", f"tabw{b}") for b in range(LAST)]
+        sub = {b: work[b][:, : 4 * PAIRS] for b in range(LAST)}
+        root = {1: work[1][:, 4 * PAIRS :]}
 
         def make_h(r):
             b, t = divmod(r, 4)
-            h[r] = sb([P, S], F32, f"h{r}", H_TAG.get(r, f"h{r % NH}"))
+            h[r] = sb([P, S], F32, f"h{r}", H_TAG.get(r))
             cols = slice(P * t, P * (t + 1))
             for f in range(2):
                 acc = banks[(2 * r + f) % 8]
@@ -195,7 +180,7 @@ def tile_list_inhibited_enzyme_flux_kernel(
                     nc.tensor.matmul_mx(
                         out=acc[:],
                         lhsT=w1c[b, a][:, cols].bitcast(FP8X4),
-                        lhsT_scale=w1s[b][a][:, cols],
+                        lhsT_scale=w1s[b, a][:, cols],
                         rhs=gw[a][f][:].bitcast(FP8X4),
                         rhs_scale=gs[f][4 * a : P, :],
                         start=(a == 0),
@@ -203,128 +188,98 @@ def tile_list_inhibited_enzyme_flux_kernel(
                     )
                 nc.scalar.activation(out=h[r][:, 512 * f : 512 * (f + 1)], in_=acc[:], func=ACT.Relu)
 
-        work = [sb([P, T], F32, f"work{b}", f"tabw{b}") for b in range(HB - 1)]
-        sub = {b: work[b][:, :2048] for b in range(HB - 1)}
-        root = {1: work[1][:, 2048:]}
-        zc, zs, late, den = {}, {}, {}, {}
+        def pick(a_out, sum_out, pieces):
+            for k, (r, i0, w) in enumerate(pieces):
+                nc.vector.tensor_copy(a_out[:, w * k : w * (k + 1)], h[r][:].indirect(pos1_t[:, i0 // 16 : (i0 + w) // 16]))
+            for k, (r, i0, w) in enumerate(pieces):
+                cols = slice(w * k, w * (k + 1))
+                nc.vector.tensor_tensor(sum_out[:, cols], h[r][:].indirect(pos2_t[:, i0 // 16 : (i0 + w) // 16]), a_out[:, cols], ALU.add)
 
-        def pick(dst, den, todo):
-            for r, o, i0, w in todo:
-                nc.vector.tensor_copy(dst[:, o : o + w], h[r][:].indirect(pos1_t[:, i0 // 16 : (i0 + w) // 16]))
-            for r, o, i0, w in todo:
-                nc.vector.tensor_tensor(den[:, o : o + w], h[r][:].indirect(pos2_t[:, i0 // 16 : (i0 + w) // 16]), dst[:, o : o + w], ALU.add)
-
-        def pick_slice(r):
-            b, t = divmod(r, 4)
-            if r == 3:
-                root[0] = sb([P, 4 * PAIRS], F32, "root0")[:]
-            if r >= 6 or r < 3:
-                late[r] = sb([P, PAIRS], F32, f"den{r}", f"x{r % 2}" if r > 2 else None)
-                pick(sub[b][:, PAIRS * t :], late[r][:], [(r, i0, i0, HALF) for i0 in (0, HALF)])
-            else:
-                pick(sub[b], root[b], [(r, PAIRS * t + i0, i0, HALF) for i0 in (0, HALF)])
-            x = sub[b][:, PAIRS * t : PAIRS * (t + 1)]
-            if r != 2:
-                nc.gpsimd.tensor_scalar(out=x, in0=x, scalar1=vm[:, b, t : t + 1], scalar2=0.0, op0=ALU.mult, op1=ALU.add)
-
-        def pick_chunk(c):
-            sub[2, c] = sb([P, 4 * CHUNK], F32, f"subc{c}", f"x{c % 2}")[:]
-            den[c] = sb([P, 4 * CHUNK], F32, f"denc{c}")[:]
-            pick(sub[2, c], den[c], [(8 + t, CHUNK * t, CHUNK * c, CHUNK) for t in range(4)])
-
-        def invert(x, y):
-            nc.scalar.activation(out=x, in_=y, func=ACT.Abs_reciprocal_sqrt, bias=1.0)
-
-        def square(x, y):
-            nc.scalar.activation(out=x, in_=y, func=ACT.Square)
-
-        def scale(x, b, t):
-            nc.scalar.activation(out=x, in_=x, func=ACT.Copy, scale=vm[:, b, t : t + 1])
-
-        def rate(x, y, b, t):
-            nc.vector.scalar_tensor_tensor(out=x, in0=x, scalar=vm[:, b, t : t + 1], in1=y, op0=ALU.mult, op1=ALU.mult)
-
-        def invert_slice(r, i0=0, i1=PAIRS):
-            b, t = divmod(r, 4)
-            x = root[b][:, PAIRS * t + i0 : PAIRS * t + i1]
-            invert(x, late[r][:, i0:i1] if r in late else x)
-
-        def finish_slice(r):
+        def whole_slice(r):
+            make_h(r)
             b, t = divmod(r, 4)
             cols = slice(PAIRS * t, PAIRS * (t + 1))
-            if r in ON_VECTOR:
-                rate(sub[b][:, cols], root[b][:, cols], b, t)
+            if r == 3:
+                root[0] = sb([P, 4 * PAIRS], F32, "root0")[:]
+            if r in SUMS_APART:
+                sums[r] = sb([P, PAIRS], F32, f"sum{r}")[:]
             else:
-                scale(sub[b][:, cols], b, t)
-                square(root[b][:, cols], root[b][:, cols])
+                sums[r] = root[b][:, cols]
+            pick(sub[b][:, cols], sums[r], [(r, i0, HALF) for i0 in (0, HALF)])
+            if r != VMAX_ON_ROOT:
+                nc.gpsimd.tensor_scalar(out=sub[b][:, cols], in0=sub[b][:, cols], scalar1=vm[:, b, t : t + 1], scalar2=0.0, op0=ALU.mult, op1=ALU.add)
 
-        def finish_half(b, ts, i0):
-            x = root[b].rearrange("p (t i) -> p t i", t=4)[:, ts[0] : ts[-1] + 1, i0 : i0 + HALF]
-            square(x, x)
-            if b == 0:
-                scale(root[0][:, PAIRS * 2 + i0 : PAIRS * 2 + i0 + HALF], 0, 2)
+        def invert(out, x):
+            nc.scalar.activation(out=out, in_=x, func=ACT.Abs_reciprocal_sqrt, bias=1.0)
+
+        def invert_slice(r):
+            b, t = divmod(r, 4)
+            invert(root[b][:, PAIRS * t : PAIRS * (t + 1)], sums[r])
+
+        def times_vmax(x, r):
+            b, t = divmod(r, 4)
+            nc.scalar.activation(out=x, in_=x, func=ACT.Copy, scale=vm[:, b, t : t + 1])
+
+        def square_half(b, i0):
+            x = root[b].rearrange("p (t i) -> p t i", t=4)[:, :, i0 : i0 + HALF]
+            nc.scalar.activation(out=x, in_=x, func=ACT.Square)
+            if b == VMAX_ON_ROOT // 4:
+                times_vmax(x[:, VMAX_ON_ROOT % 4], VMAX_ON_ROOT)
+
+        def pick_chunk(c):
+            sub[LAST, c] = sb([P, 4 * CHUNK], F32, f"subc{c}", f"sum{6 + c % 2}")[:]
+            sums[LAST, c] = sb([P, 4 * CHUNK], F32, f"sumc{c}")[:]
+            pick(sub[LAST, c], sums[LAST, c], [(4 * LAST + t, CHUNK * c, CHUNK) for t in range(4)])
 
         def finish_chunk(c):
-            invert(den[c], den[c])
-            root[2, c] = den[c] if c in CHUNKS_ON_VECTOR else sb([P, 4 * CHUNK], F32, f"rootc{c}")[:]
+            invert(sums[LAST, c], sums[LAST, c])
+            root[LAST, c] = sb([P, 4 * CHUNK], F32, f"rootc{c}")[:]
             for t in range(4):
-                cols = slice(CHUNK * t, CHUNK * (t + 1))
-                if c in CHUNKS_ON_VECTOR:
-                    rate(sub[2, c][:, cols], root[2, c][:, cols], 2, t)
-                else:
-                    scale(sub[2, c][:, cols], 2, t)
-            if c not in CHUNKS_ON_VECTOR:
-                square(root[2, c], den[c])
+                times_vmax(sub[LAST, c][:, CHUNK * t : CHUNK * (t + 1)], 4 * LAST + t)
+            nc.scalar.activation(out=root[LAST, c], in_=sums[LAST, c], func=ACT.Square)
 
-        def weave(out, key, i0, w):
-            hv, rv = [v[key].rearrange("p (t c i) -> p c t i", i=2, t=4)[:, i0 // 2 : (i0 + w) // 2] for v in (sub, root)]
-            nc.vector.tensor_tensor(out=out.rearrange("p (c i t) -> p c t i", i=2, t=4), in0=hv, in1=rv, op=ALU.mult)
+        def weave(out, key, i0):
+            x, y = [v[key].rearrange("p (t c i) -> p c t i", i=2, t=4)[:, i0 // 2 : (i0 + CHUNK) // 2] for v in (sub, root)]
+            nc.vector.tensor_tensor(out=out.rearrange("p (c i t) -> p c t i", i=2, t=4), in0=x, in1=y, op=ALU.mult)
 
-        def quant_z(z4, name, parts):
-            width = CHUNK * len(parts)
-            codes = sb([P, width], U32, f"zc{name}")
-            scales = sb([P, width], U8, f"zs{name}")
-            for k, key in enumerate(parts):
-                zc[key] = codes[:, CHUNK * k : CHUNK * (k + 1)]
-                zs[key] = scales[:, CHUNK * k : CHUNK * (k + 1)]
-            nc.vector.quantize_mx(out=codes[:].bitcast(FP8X4), scales=scales[:], in_=z4)
+        def multiply(z4, passes, c):
+            codes = sb([P, CHUNK * len(passes)], U32, f"zc{passes[0]}{c}")
+            scales = sb([P, CHUNK * len(passes)], U8, f"zs{passes[0]}{c}")
+            nc.vector.quantize_mx(out=codes[:].bitcast(FP8X4), scales=scales[:], in_=z4[:])
+            for k, b in enumerate(passes):
+                cols = slice(CHUNK * k, CHUNK * (k + 1))
+                for g in range(NG):
+                    for t in range(4):
+                        c0 = 512 * g + P * t
+                        nc.tensor.matmul_mx(
+                            out=banks[NG * c + g][:, CHUNK * t : CHUNK * (t + 1)],
+                            lhsT=w2w[b][:, 2 * c0 : 2 * (c0 + P)].bitcast(FP4X4),
+                            lhsT_scale=w2s[b][:, c0 : c0 + P],
+                            rhs=codes[:, cols].bitcast(FP8X4),
+                            rhs_scale=scales[:, cols],
+                            start=(b == 0 and t == 0),
+                            stop=(b == LAST and t == 3),
+                        )
 
-        def rates_early(c):
-            z4 = sb([P, 8 * CHUNK], BF16, f"z4e{c}", f"denc{c - 1}" if c else None)
-            for b in range(HB - 1):
-                weave(z4[:, 4 * CHUNK * b : 4 * CHUNK * (b + 1)], b, CHUNK * c, CHUNK)
-            quant_z(z4[:], f"e{c}", [(0, c), (1, c)])
+        def first_passes(c):
+            z4 = sb([P, LAST * 4 * CHUNK], BF16, f"zfirst{c}", f"sumc{c - 1}" if c else None)
+            for b in range(LAST):
+                weave(z4[:, 4 * CHUNK * b : 4 * CHUNK * (b + 1)], b, CHUNK * c)
+            multiply(z4, range(LAST), c)
 
-        def rates_last(c):
-            z4 = sb([P, 4 * CHUNK], BF16, f"z4l{c}", f"z4l{c % 2}")
-            weave(z4[:], (2, c), 0, CHUNK)
-            quant_z(z4[:], f"l{c}", [(2, c)])
-
-        def flux_pass(b, c, first=0):
-            for g in range(NG):
-                for t in range(4):
-                    c0 = 512 * g + P * t
-                    nc.tensor.matmul_mx(
-                        out=banks[NG * c + g][:, CHUNK * t : CHUNK * (t + 1)],
-                        lhsT=w2w[b][:, 2 * c0 : 2 * (c0 + P)].bitcast(FP4X4),
-                        lhsT_scale=w2s[b][:, c0 : c0 + P],
-                        rhs=zc[b, c].bitcast(FP8X4),
-                        rhs_scale=zs[b, c],
-                        start=(b == first and t == 0),
-                        stop=(b == HB - 1 and t == 3),
-                    )
+        def last_pass(c):
+            z4 = sb([P, 4 * CHUNK], BF16, f"zlast{c}", f"zlast{c % 2}")
+            weave(z4[:], (LAST, c), 0)
+            multiply(z4, [LAST], c)
 
         out_rows = out_0.rearrange("(g p t) i -> g p t i", p=P, t=4)
         out_words = out_1.rearrange("g p m t -> p g (m t)").bitcast(I32)
         y4 = [sb([P, 4 * PAIRS], BF16, f"y4{g}") for g in range(NG)]
 
-        def store_rows(c0, c1, g, tag):
-            w = CHUNK * (c1 - c0)
-            y = sb([P, 4, w], F32, f"y{c0}{g}", tag)
-            for c in range(c0, c1):
-                o = CHUNK * (c - c0)
-                nc.scalar.copy(out=y[:, :, o : o + CHUNK], in_=banks[NG * c + g][:].rearrange("p (t i) -> p t i", t=4))
-            nc.sync.dma_start(out=out_rows[g, :, :, CHUNK * c0 : CHUNK * c1], in_=y[:])
+        def store_rows(c, g, tag=None):
+            y = sb([P, 4, CHUNK], F32, f"y{c}{g}", tag)
+            nc.scalar.copy(out=y[:], in_=banks[NG * c + g][:].rearrange("p (t i) -> p t i", t=4))
+            nc.sync.dma_start(out=out_rows[g, :, :, CHUNK * c : CHUNK * (c + 1)], in_=y[:])
             return y
 
         def round_bank(c, g):
@@ -335,118 +290,74 @@ def tile_list_inhibited_enzyme_flux_kernel(
 
         def round_rows(c, g, y):
             nc.vector.tensor_copy(
-                out=y4[g][:, 4 * CHUNK * c : 4 * CHUNK * (c + 1)].rearrange("p (c i t) -> p c t i", i=4, t=4),
-                in_=y[:].rearrange("p t (c i) -> p c t i", i=4),
-            )
-
-        planes = []
-
-        def quant_rows(c0, c1, g):
-            if not planes:
-                planes.append(sb([P, NG * PAIRS], U32, "ycodes", YTAG))
-            ycodes = planes[0]
-            lo, hi = CHUNK * c0, CHUNK * c1
-            nc.vector.quantize_mx(
-                out=ycodes[:, PAIRS * g + lo : PAIRS * g + hi].bitcast(FP8X4),
-                scales=yscales[:, PAIRS * g + lo : PAIRS * g + hi],
-                in_=y4[g][:, 4 * lo : 4 * hi],
+                out=y4[g][:, 4 * CHUNK * c : 4 * CHUNK * (c + 1)].rearrange("p (x i t) -> p x t i", i=4, t=4),
+                in_=y[:].rearrange("p t (x i) -> p x t i", i=4),
             )
 
         def store_codes(c0, c1):
             lo, hi = CHUNK * c0, CHUNK * c1
-            nc.sync.dma_start(out=out_words[:, :, lo:hi], in_=planes[0][:].bitcast(I32).rearrange("p (g m) -> p g m", g=NG)[:, :, lo:hi])
+            for g in range(NG):
+                cols = slice(PAIRS * g + lo, PAIRS * g + hi)
+                nc.vector.quantize_mx(out=ycodes[:, cols].bitcast(FP8X4), scales=yscales[:, cols], in_=y4[g][:, 4 * lo : 4 * hi])
+            nc.sync.dma_start(out=out_words[:, :, lo:hi], in_=ycodes[:].bitcast(I32).rearrange("p (g m) -> p g m", g=NG)[:, :, lo:hi])
 
         for b in range(HB):
-            deal_words(b, f"w1pair{b}")
-
-        def step_w1(b, a, tag):
-            round_w1(b, a, M_VECTOR[b, a], tag)
-            quant_w1(b, a)
-
-        def step_h(r):
-            make_h(r)
-            if r < 8:
-                pick_slice(r)
-
-        def last_rates(c):
-            rates_last(c)
-            flux_pass(2, c)
-
-        def early_rates(c):
-            rates_early(c)
-            for b in range(HB - 1):
-                flux_pass(b, c)
-
-        step_h(0)
-        step_h(1)
-        step_w1(1, 0, "g1")
-        step_h(2)
-        step_w1(1, 1, "g0")
-        step_h(3)
+            deal_words(b)
+        whole_slice(0)
+        whole_slice(1)
+        for a in range(KA):
+            quantise_block(1, a, None)
+            whole_slice(2 + a)
         invert_slice(0)
         invert_slice(1)
-        step_h(4)
-        last_w1()
-        step_h(5)
-        invert_slice(2)
-        step_h(6)
+        whole_slice(4)
+        quantise_last_pass()
+        whole_slice(5)
+        whole_slice(6)
         deal_scales()
-        step_h(7)
+        whole_slice(7)
+        invert_slice(2)
         invert_slice(3)
-        step_h(8)
-        step_h(9)
-        step_h(10)
-        step_h(11)
+        for t in range(4):
+            make_h(4 * LAST + t)
         invert_slice(6)
         pick_chunk(0)
-        finish_half(0, [0, 1, 2, 3], 0)
-        invert_slice(4)
-        invert_slice(5)
-        invert_slice(7)
+        square_half(0, 0)
+        for r in (4, 5, 7):
+            invert_slice(r)
         pick_chunk(1)
-        finish_half(1, [0, 1, 2, 3], 0)
-        early_rates(0)
-        finish_chunk(0)
-        last_rates(0)
-        early_rates(1)
-        pick_chunk(2)
-        finish_half(0, [0, 1, 2, 3], HALF)
-        finish_half(1, [0, 1, 2, 3], HALF)
-        finish_chunk(1)
-        last_rates(1)
-        early_rates(2)
-        pick_chunk(3)
-        for g in range(NG):
-            store_rows(0, 1, g, ("raw00", "raw20")[g])
-        for g in range(NG):
-            round_bank(0, g)
-        finish_chunk(2)
-        last_rates(2)
-        early_rates(3)
-        for g in range(NG):
-            store_rows(1, 2, g, ("raw21", "w1half0")[g])
-        for g in range(NG):
-            round_bank(1, g)
-        finish_chunk(3)
-        last_rates(3)
-        for g in range(NG):
-            quant_rows(0, 2, g)
-        store_codes(0, 2)
-        held = [store_rows(2, 3, g, f"y2{g}") for g in range(NG)]
-        round_bank(2, 0)
-        round_rows(2, 1, held[1])
-        for g in range(NG):
-            quant_rows(2, 3, g)
-        store_codes(2, 3)
-        for g in range(NG):
-            round_rows(3, g, store_rows(3, 4, g, f"y3{g}"))
-        for g in range(NG):
-            quant_rows(3, 4, g)
-        store_codes(3, 4)
+        square_half(1, 0)
 
-        queues = [nc.sync, nc.scalar, nc.sync, nc.scalar]
+        spent = (("raw00", "raw20"), ("raw21", "w1half0"))
+        first_passes(0)
+        for c in range(NC):
+            finish_chunk(c)
+            last_pass(c)
+            if c + 1 < NC:
+                first_passes(c + 1)
+            if c + 2 < NC:
+                pick_chunk(c + 2)
+            if c == 0:
+                for b in range(LAST):
+                    square_half(b, HALF)
+            elif c + 1 < NC:
+                for g in range(NG):
+                    store_rows(c - 1, g, spent[c - 1][g])
+                for g in range(NG):
+                    round_bank(c - 1, g)
+
+        ycodes = sb([P, NG * PAIRS], U32, "ycodes")
+        store_codes(0, NC - 2)
+        rows = [store_rows(NC - 2, g) for g in range(NG)]
+        round_bank(NC - 2, 0)
+        round_rows(NC - 2, 1, rows[1])
+        store_codes(NC - 2, NC - 1)
+        for g in range(NG):
+            round_rows(NC - 1, g, store_rows(NC - 1, g))
+        store_codes(NC - 1, NC)
+
         for q in range(4):
-            queues[q].dma_start(
+            (nc.sync, nc.scalar)[q % 2].dma_start(
                 out=out_2[:, 4 * q : 4 * q + 4, :].bitcast(I32).rearrange("g r m -> r g m"),
                 in_=yscales[32 * q : 32 * q + 4, :].bitcast(I32).rearrange("p (g m) -> p g m", g=NG),
             )

@@ -220,11 +220,15 @@ def tile_list_inhibited_enzyme_flux_kernel(
             b, t = divmod(r, 4)
             nc.scalar.activation(out=x, in_=x, func=ACT.Copy, scale=vm[:, b, t : t + 1])
 
-        def square_half(b, i0):
-            x = root[b].rearrange("p (t i) -> p t i", t=4)[:, :, i0 : i0 + HALF]
-            nc.scalar.activation(out=x, in_=x, func=ACT.Square)
+        def chunks(x, c0, c1):
+            return x.rearrange("p (t i) -> p t i", t=4)[:, :, CHUNK * c0 : CHUNK * c1]
+
+        def square(b, c0, c1, out=None):
+            x = chunks(root[b], c0, c1)
+            out = x if out is None else out
+            nc.scalar.activation(out=out, in_=x, func=ACT.Square)
             if b == VMAX_ON_ROOT // 4:
-                times_vmax(x[:, VMAX_ON_ROOT % 4], VMAX_ON_ROOT)
+                times_vmax(out[:, VMAX_ON_ROOT % 4], VMAX_ON_ROOT)
 
         def pick_chunk(c):
             sub[LAST, c] = sb([P, 4 * CHUNK], F32, f"subc{c}", f"sum{6 + c % 2}")[:]
@@ -238,14 +242,18 @@ def tile_list_inhibited_enzyme_flux_kernel(
                 times_vmax(sub[LAST, c][:, CHUNK * t : CHUNK * (t + 1)], 4 * LAST + t)
             nc.scalar.activation(out=root[LAST, c], in_=sums[LAST, c], func=ACT.Square)
 
-        def weave(out, key, i0):
-            x, y = [v[key].rearrange("p (t c i) -> p c t i", i=2, t=4)[:, i0 // 2 : (i0 + CHUNK) // 2] for v in (sub, root)]
+        def weave(out, x, y):
+            x, y = [v.rearrange("p t (c i) -> p c t i", i=2) for v in (x, y)]
             nc.vector.tensor_tensor(out=out.rearrange("p (c i t) -> p c t i", i=2, t=4), in0=x, in1=y, op=ALU.mult)
 
-        def multiply(z4, passes, c):
-            codes = sb([P, CHUNK * len(passes)], U32, f"zc{passes[0]}{c}")
+        def weave_gpsimd(out, x, y):
+            x, y = [v.rearrange("p t i -> p i t") for v in (x, y)]
+            nc.gpsimd.tensor_tensor(out=out.rearrange("p (i t) -> p i t", t=4), in0=x, in1=y, op=ALU.mult)
+
+        def multiply(z4, passes, c, tag=None):
+            codes = sb([P, CHUNK * len(passes)], U32, f"zc{passes[0]}{c}", tag)
             scales = sb([P, CHUNK * len(passes)], U8, f"zs{passes[0]}{c}")
-            nc.vector.quantize_mx(out=codes[:].bitcast(FP8X4), scales=scales[:], in_=z4[:])
+            nc.vector.quantize_mx(out=codes[:].bitcast(FP8X4), scales=scales[:], in_=z4)
             for k, b in enumerate(passes):
                 cols = slice(CHUNK * k, CHUNK * (k + 1))
                 for g in range(NG):
@@ -261,29 +269,39 @@ def tile_list_inhibited_enzyme_flux_kernel(
                             stop=(b == LAST and t == 3),
                         )
 
-        def first_passes(c):
-            z4 = sb([P, LAST * 4 * CHUNK], BF16, f"zfirst{c}", f"sumc{c - 1}" if c else None)
-            for b in range(LAST):
-                weave(z4[:, 4 * CHUNK * b : 4 * CHUNK * (b + 1)], b, CHUNK * c)
-            multiply(z4, range(LAST), c)
+        zfirst = {}
+        WIDE = 4 * CHUNK
 
-        def last_pass(c):
-            z4 = sb([P, 4 * CHUNK], BF16, f"zlast{c}", f"zlast{c % 2}")
-            weave(z4[:], (LAST, c), 0)
-            multiply(z4, [LAST], c)
+        def weave_first(c):
+            zfirst[c] = sb([P, WIDE], BF16, f"zfirst{c}", "sq00" if c % 2 else "zfirst0")
+            weave_gpsimd(zfirst[c][:], chunks(sub[0], c, c + 1), chunks(root[0], c, c + 1))
+
+        def products(c):
+            z4 = sb([P, LAST * WIDE], BF16, f"zlast{c}", f"zlast{c % 2}")
+            weave(z4[:, :WIDE], chunks(sub[1], c, c + 1), chunks(root[1], c, c + 1))
+            if c + 1 == NC:
+                multiply(zfirst[c][:], [0], c)
+                store_codes(0, NC - 2)
+                multiply(z4[:, :WIDE], [1], c)
+            weave(z4[:, WIDE:], chunks(sub[LAST, c], 0, 1), chunks(root[LAST, c], 0, 1))
+            if c + 1 == NC:
+                multiply(z4[:, WIDE:], [LAST], c)
+            else:
+                multiply(zfirst[c][:], [0], c, f"rootc{c}" if c + 2 < NC else None)
+                multiply(z4[:], [1, LAST], c)
 
         out_rows = out_0.rearrange("(g p t) i -> g p t i", p=P, t=4)
         out_words = out_1.rearrange("g p m t -> p g (m t)").bitcast(I32)
         y4 = [sb([P, 4 * PAIRS], BF16, f"y4{g}") for g in range(NG)]
 
-        def store_rows(c, g, tag=None):
+        def store_rows(c, g, tag=None, copy=nc.scalar.copy):
             y = sb([P, 4, CHUNK], F32, f"y{c}{g}", tag)
-            nc.scalar.copy(out=y[:], in_=banks[NG * c + g][:].rearrange("p (t i) -> p t i", t=4))
+            copy(out=y[:], in_=banks[NG * c + g][:].rearrange("p (t i) -> p t i", t=4))
             nc.sync.dma_start(out=out_rows[g, :, :, CHUNK * c : CHUNK * (c + 1)], in_=y[:])
             return y
 
-        def round_bank(c, g):
-            nc.scalar.copy(
+        def round_bank(c, g, copy=nc.scalar.copy):
+            copy(
                 out=y4[g][:, 4 * CHUNK * c : 4 * CHUNK * (c + 1)].rearrange("p (i t) -> p i t", t=4),
                 in_=banks[NG * c + g][:].rearrange("p (t i) -> p i t", t=4),
             )
@@ -322,38 +340,39 @@ def tile_list_inhibited_enzyme_flux_kernel(
             make_h(4 * LAST + t)
         invert_slice(6)
         pick_chunk(0)
-        square_half(0, 0)
+        sq00 = sb([P, WIDE], F32, "sq00")
+        square(0, 0, 1, chunks(sq00[:], 0, 1))
+        zfirst[0] = sb([P, WIDE], BF16, "zfirst0")
+        weave(zfirst[0][:], chunks(sub[0], 0, 1), chunks(sq00[:], 0, 1))
+        square(0, 1, 2)
         for r in (4, 5, 7):
             invert_slice(r)
         pick_chunk(1)
-        square_half(1, 0)
+        weave_first(1)
 
         spent = (("raw00", "raw20"), ("raw21", "w1half0"))
-        first_passes(0)
+        ycodes = sb([P, NG * PAIRS], U32, "ycodes")
         for c in range(NC):
+            square(1, c, c + 1)
             finish_chunk(c)
-            last_pass(c)
-            if c + 1 < NC:
-                first_passes(c + 1)
-            if c + 2 < NC:
-                pick_chunk(c + 2)
             if c == 0:
-                for b in range(LAST):
-                    square_half(b, HALF)
-            elif c + 1 < NC:
+                square(0, 2, NC)
+            products(c)
+            if c + 2 < NC:
+                weave_first(c + 2)
+                pick_chunk(c + 2)
+            if 0 < c < NC - 1:
                 for g in range(NG):
                     store_rows(c - 1, g, spent[c - 1][g])
                 for g in range(NG):
                     round_bank(c - 1, g)
 
-        ycodes = sb([P, NG * PAIRS], U32, "ycodes")
-        store_codes(0, NC - 2)
-        rows = [store_rows(NC - 2, g) for g in range(NG)]
-        round_bank(NC - 2, 0)
-        round_rows(NC - 2, 1, rows[1])
-        store_codes(NC - 2, NC - 1)
         for g in range(NG):
-            round_rows(NC - 1, g, store_rows(NC - 1, g))
+            round_rows(NC - 2, g, store_rows(NC - 2, g))
+        store_codes(NC - 2, NC - 1)
+        for g, copy in enumerate((nc.scalar.copy, nc.vector.tensor_copy)):
+            store_rows(NC - 1, g, None, copy)
+            round_bank(NC - 1, g, copy)
         store_codes(NC - 1, NC)
 
         for q in range(4):

@@ -247,8 +247,8 @@ def tile_list_inhibited_enzyme_flux_kernel(
             nc.vector.tensor_tensor(out=out.rearrange("p (c i t) -> p c t i", i=2, t=4), in0=x, in1=y, op=ALU.mult)
 
         def weave_gpsimd(out, x, y):
-            x, y = [v.rearrange("p t i -> p i t") for v in (x, y)]
-            nc.gpsimd.tensor_tensor(out=out.rearrange("p (i t) -> p i t", t=4), in0=x, in1=y, op=ALU.mult)
+            x, y = [v.rearrange("p t (c i) -> p c t i", i=4) for v in (x, y)]
+            nc.gpsimd.tensor_tensor(out=out.rearrange("p (c i t) -> p c t i", i=4, t=4), in0=x, in1=y, op=ALU.mult)
 
         def multiply(z4, passes, c, tag=None):
             codes = sb([P, CHUNK * len(passes)], U32, f"zc{passes[0]}{c}", tag)

@@ -26,10 +26,11 @@ NC = PAIRS // CHUNK
 HALF = PAIRS // 2
 M_VECTOR = 64
 
-PLACED = {"raw10": 12, "h2": 12, "w1g11": 16, "raw11": 0, "h3": 0, "root0": 4, "w1g2": 16}
+PLACED = {"raw10": 12, "h2": 12, "w1g11": 16, "raw11": 0, "h3": 0, "root0": 4}
 H_TAG = {8: "h0", 9: "h1", 11: "h4"}
 SUMS_APART = (0, 1, 2, 6, 7)
 VMAX_ON_ROOT = 2
+PLAIN = (1,)
 
 
 def tile_list_inhibited_enzyme_flux_kernel(
@@ -118,18 +119,17 @@ def tile_list_inhibited_enzyme_flux_kernel(
         def quantise_block(b, a, tag):
             rounded = sb([P, 2048], BF16, f"w1g{b}{a}", tag)
             round_block(nc.scalar.copy, rounded[:], w1raw[b, a])
-            nc.vector.quantize_mx(out=w1c[b, a][:].bitcast(FP8X4), scales=w1s[b, a][:], in_=rounded[:])
+            nc.vector.quantize_mx(out=w1c[b, a][:, :].bitcast(FP8X4), scales=w1s[b, a][:, :], in_=rounded[:])
 
         def round_pair(copy, out, u, x):
             dst = out[:].rearrange("p (t m j) -> p m j t", t=2, j=4)[:, 64 * x : 64 * (x + 1)]
             copy(out=dst, in_=w1half[x][:].rearrange("p j (m u t) -> p u m j t", u=2, t=2)[:, u])
 
-        def quantise_last_pass():
-            rounded = sb([P, KA * 2048], BF16, "w1g2")
-            round_block(nc.vector.tensor_copy, rounded[:, :2048], w1raw[LAST, 0], slice(0, M_VECTOR))
-            round_block(nc.scalar.copy, rounded[:, 2048:], w1raw[LAST, 1])
-            round_block(nc.scalar.copy, rounded[:, :2048], w1raw[LAST, 0], slice(M_VECTOR, P))
-            nc.vector.quantize_mx(out=last_codes[:].bitcast(FP8X4), scales=last_scales[:], in_=rounded[:])
+        def quantise_shared_block():
+            rounded = sb([P, 2048], BF16, "w1g2", "sum0")
+            round_block(nc.vector.tensor_copy, rounded[:], w1raw[LAST, 0], slice(0, M_VECTOR))
+            round_block(nc.scalar.copy, rounded[:], w1raw[LAST, 0], slice(M_VECTOR, P))
+            nc.vector.quantize_mx(out=w1c[LAST, 0].bitcast(FP8X4), scales=w1s[LAST, 0], in_=rounded[:])
 
         gather_words(0)
         for f in range(2):
@@ -157,7 +157,7 @@ def tile_list_inhibited_enzyme_flux_kernel(
             )
 
         def deal_scales():
-            w2s[0] = sb([P, N], U8, "w2s0", "h5")
+            w2s[0] = sb([P, N], U8, "w2s0", "sum2")
             nc.vector.tensor_copy(
                 out=w2s[0][:].rearrange("p (g t m) -> p g t m", t=4, m=P),
                 in_=w2sraw[:].rearrange("p (g m t) -> p g t m", t=4, m=P),
@@ -206,8 +206,7 @@ def tile_list_inhibited_enzyme_flux_kernel(
             else:
                 sums[r] = root[b][:, cols]
             pick(sub[b][:, cols], sums[r], [(r, i0, HALF) for i0 in (0, HALF)])
-            if r != VMAX_ON_ROOT:
-                nc.gpsimd.tensor_scalar(out=sub[b][:, cols], in0=sub[b][:, cols], scalar1=vm[:, b, t : t + 1], scalar2=0.0, op0=ALU.mult, op1=ALU.add)
+            nc.gpsimd.tensor_scalar(out=sub[b][:, cols], in0=sub[b][:, cols], scalar1=vm[:, b, t : t + 1], scalar2=0.0, op0=ALU.mult, op1=ALU.add)
 
         def invert(out, x):
             nc.scalar.activation(out=out, in_=x, func=ACT.Abs_reciprocal_sqrt, bias=1.0)
@@ -227,8 +226,6 @@ def tile_list_inhibited_enzyme_flux_kernel(
             x = chunks(root[b], c0, c1)
             out = x if out is None else out
             nc.scalar.activation(out=out, in_=x, func=ACT.Square)
-            if b == VMAX_ON_ROOT // 4:
-                times_vmax(out[:, VMAX_ON_ROOT % 4], VMAX_ON_ROOT)
 
         def pick_chunk(c):
             sub[LAST, c] = sb([P, 4 * CHUNK], F32, f"subc{c}", f"sum{6 + c % 2}")[:]
@@ -273,8 +270,15 @@ def tile_list_inhibited_enzyme_flux_kernel(
         WIDE = 4 * CHUNK
 
         def weave_first(c):
-            zfirst[c] = sb([P, WIDE], BF16, f"zfirst{c}", "sq00" if c % 2 else "zfirst0")
-            weave_gpsimd(zfirst[c][:], chunks(sub[0], c, c + 1), chunks(root[0], c, c + 1))
+            zfirst[c] = sb([P, WIDE], BF16, f"zfirst{c}", ("zfirst0", "sq00", "zfirst0", "zwoven1")[c])
+            if c in PLAIN:
+                nc.gpsimd.tensor_tensor(out=chunks(zfirst[c][:], 0, 1), in0=chunks(sub[0], c, c + 1), in1=chunks(root[0], c, c + 1), op=ALU.mult)
+            else:
+                weave_gpsimd(zfirst[c][:], chunks(sub[0], c, c + 1), chunks(root[0], c, c + 1))
+
+        def interleave(c):
+            plain, zfirst[c] = zfirst[c], sb([P, WIDE], BF16, f"zwoven{c}")
+            nc.scalar.copy(out=zfirst[c][:].rearrange("p (x i t) -> p x t i", i=4, t=4), in_=plain[:].rearrange("p (t x i) -> p x t i", i=4, t=4))
 
         def products(c):
             z4 = sb([P, LAST * WIDE], BF16, f"zlast{c}", f"zlast{c % 2}")
@@ -329,12 +333,13 @@ def tile_list_inhibited_enzyme_flux_kernel(
         invert_slice(0)
         invert_slice(1)
         whole_slice(4)
-        quantise_last_pass()
+        quantise_shared_block()
         whole_slice(5)
+        quantise_block(LAST, 1, None)
         whole_slice(6)
+        invert_slice(2)
         deal_scales()
         whole_slice(7)
-        invert_slice(2)
         invert_slice(3)
         for t in range(4):
             make_h(4 * LAST + t)
@@ -345,18 +350,24 @@ def tile_list_inhibited_enzyme_flux_kernel(
         zfirst[0] = sb([P, WIDE], BF16, "zfirst0")
         weave(zfirst[0][:], chunks(sub[0], 0, 1), chunks(sq00[:], 0, 1))
         square(0, 1, 2)
-        for r in (4, 5, 7):
-            invert_slice(r)
+        invert_slice(4)
+        invert_slice(7)
         pick_chunk(1)
+        invert_slice(5)
         weave_first(1)
 
         spent = (("raw00", "raw20"), ("raw21", "w1half0"))
         ycodes = sb([P, NG * PAIRS], U32, "ycodes")
         for c in range(NC):
-            square(1, c, c + 1)
+            if c != 2:
+                square(1, c, c + 1)
+            if c in PLAIN:
+                interleave(c)
             finish_chunk(c)
             if c == 0:
                 square(0, 2, NC)
+            if c == 1:
+                square(1, 2, 3)
             products(c)
             if c + 2 < NC:
                 weave_first(c + 2)

@@ -240,8 +240,8 @@ def tile_list_inhibited_enzyme_flux_kernel(
             nc.scalar.activation(out=root[LAST, c], in_=sums[LAST, c], func=ACT.Square)
 
         def weave(out, x, y):
-            x, y = [v.rearrange("p t (c i) -> p c t i", i=2) for v in (x, y)]
-            nc.vector.tensor_tensor(out=out.rearrange("p (c i t) -> p c t i", i=2, t=4), in0=x, in1=y, op=ALU.mult)
+            x, y = [v.rearrange("p t (c i) -> p c t i", i=4) for v in (x, y)]
+            nc.vector.tensor_tensor(out=out.rearrange("p (c i t) -> p c t i", i=4, t=4), in0=x, in1=y, op=ALU.mult)
 
         def weave_gpsimd(out, x, y):
             x, y = [v.rearrange("p t (c i) -> p c t i", i=4) for v in (x, y)]
@@ -359,15 +359,15 @@ def tile_list_inhibited_enzyme_flux_kernel(
         spent = (("raw00", "raw20"), ("raw21", "w1half0"))
         ycodes = sb([P, NG * PAIRS], U32, "ycodes")
         for c in range(NC):
-            if c != 2:
+            if c < 2:
                 square(1, c, c + 1)
             if c in PLAIN:
                 interleave(c)
             finish_chunk(c)
             if c == 0:
                 square(0, 2, NC)
-            if c == 1:
-                square(1, 2, 3)
+            if c in (1, 2):
+                square(1, c + 1, c + 2)
             products(c)
             if c + 2 < NC:
                 weave_first(c + 2)

@@ -21,16 +21,8 @@ KA = K // 512
 HB = H // 512
 NG = N // 512
 LAST = HB - 1
-CHUNK = 128
-NC = PAIRS // CHUNK
 HALF = PAIRS // 2
-M_VECTOR = 64
-
-PLACED = {"raw10": 12, "h2": 12, "w1g11": 16, "raw11": 0, "h3": 0, "root0": 4}
-H_TAG = {8: "h0", 9: "h1", 11: "h4"}
-SUMS_APART = (0, 1, 2, 6, 7)
-VMAX_ON_ROOT = 2
-PLAIN = (1,)
+CHUNKS = ((0, 128), (128, 256), (256, 384), (384, 512))
 
 
 def tile_list_inhibited_enzyme_flux_kernel(
@@ -39,30 +31,28 @@ def tile_list_inhibited_enzyme_flux_kernel(
     nc = tc.nc
     with ExitStack() as ctx:
         keep = ctx.enter_context(tc.tile_pool(name="keep", bufs=1))
-        lay = ctx.enter_context(tc.tile_pool(name="lay", bufs=1))
         psum = ctx.enter_context(tc.psum_pool(name="psum", bufs=1))
 
         def sb(shape, dtype, name, tag=None):
-            if name in PLACED:
-                return lay.tile(shape, dtype, name=name, offset=1024 * PLACED[name], align_bytes=64)
             return keep.tile(shape, dtype, name=name, tag=tag or name, align_bytes=64)
 
         offs_t = keep.tile([P, S // 16], U16, name="offs_t")
         pos1_t = keep.tile([P, PAIRS // 16], U16, name="pos1_t")
         pos2_t = keep.tile([P, PAIRS // 16], U16, name="pos2_t")
-        tabw = [sb([P, T], U32, f"tabw{a}") for a in range(KA)]
+        tab_all = sb([P, KA * T], U32, "tabw")
+        tabw = [tab_all[:, T * a : T * (a + 1)] for a in range(KA)]
         tabs = sb([P, T], U8, "tabs")
         w2raw = [sb([P, 2 * N], U8, f"w2raw{b}") for b in range(HB)]
         w2sraw = sb([P, N], U8, "w2sraw")
         w2s = {b: sb([P, N], U8, f"w2s{b}") for b in range(1, HB)}
         vm = sb([P, HB, 4], F32, "vm")
-        w1c = {(b, a): sb([P, 512], U32, f"w1c{b}{a}") for a in range(KA) for b in range(LAST) if (b, a) != (0, 0)}
-        w1s = {(b, a): sb([P, 512], U8, f"w1s{b}{a}") for b in range(LAST) for a in range(KA)}
-        last_codes = sb([P, KA * 512], U32, "last_codes")
-        last_scales = sb([P, KA * 512], U8, "last_scales")
+        w1c = {(b, a): sb([P, 512], U32, f"w1c{b}{a}")[:] for a in range(KA) for b in (0, LAST) if (b, a) != (0, 0)}
+        w1s = {(b, a): sb([P, 512], U8, f"w1s{b}{a}")[:] for b in (0, LAST) for a in range(KA)}
+        mid_codes = sb([P, KA * 512], U32, "mid_codes")
+        mid_scales = sb([P, KA * 512], U8, "mid_scales")
         for a in range(KA):
-            w1c[LAST, a] = last_codes[:, 512 * a : 512 * (a + 1)]
-            w1s[LAST, a] = last_scales[:, 512 * a : 512 * (a + 1)]
+            w1c[1, a] = mid_codes[:, 512 * a : 512 * (a + 1)]
+            w1s[1, a] = mid_scales[:, 512 * a : 512 * (a + 1)]
         gw = [[sb([P, 512], U32, f"gw{a}{f}") for f in range(2)] for a in range(KA)]
         gs = [sb([P, 512], U8, f"gs{f}") for f in range(2)]
         banks = [psum.tile([P, 512], F32, name=f"bank{i}") for i in range(8)]
@@ -84,7 +74,7 @@ def tile_list_inhibited_enzyme_flux_kernel(
             nc.sync.dma_start(out=w1raw[b, a][:], in_=rows.rearrange("(p j) c -> p j c", j=4))
 
         def load_tab(a):
-            nc.sync.dma_start(out=tabw[a][:].bitcast(I32), in_=tab_words[a].rearrange("p t i -> p (t i)").bitcast(I32))
+            nc.sync.dma_start(out=tabw[a].bitcast(I32), in_=tab_words[a].rearrange("p t i -> p (t i)").bitcast(I32))
 
         for q in range(4):
             nc.gpsimd.dma_start(out=tabs[32 * q : 32 * q + 4 * KA, :].bitcast(I32), in_=tab_scales[:, 4 * q : 4 * q + 4, :].bitcast(I32))
@@ -92,10 +82,15 @@ def tile_list_inhibited_enzyme_flux_kernel(
         nc.sync.dma_start(offs_t[:], offs)
         load_w1(0, 0)
         load_tab(1)
-        w1half = []
-        for x in range(2):
-            w1half.append(sb([P, 4, 256], F32, f"w1half{x}"))
-            nc.sync.dma_start(out=w1half[x][:], in_=w1[512:1024, 256 * x : 256 * (x + 1)].rearrange("(p j) c -> p j c", j=4))
+        def load_halves(b):
+            halves = []
+            for x in range(2):
+                halves.append(sb([P, 4, 256], F32, f"half{b}{x}"))
+                c0 = 512 * b + 256 * x
+                nc.sync.dma_start(out=halves[x][:], in_=w1[512:1024, c0 : c0 + 256].rearrange("(p j) c -> p j c", j=4))
+            return halves
+
+        w1half = load_halves(0)
         for b in range(HB):
             nc.sync.dma_start(out=w2raw[b][:].bitcast(I32), in_=w2_words[b].bitcast(I32))
             if b == 0:
@@ -103,7 +98,7 @@ def tile_list_inhibited_enzyme_flux_kernel(
                 nc.sync.dma_start(pos2_t[:], pos2)
         load_w1(1, 0)
         nc.sync.dma_start(out=vm[:], in_=vmax.rearrange("(b p t) -> p b t", p=P, t=4))
-        load_w1(1, 1)
+        mid_half = load_halves(1)
         for a in range(KA):
             load_w1(LAST, a)
         for q in range(4):
@@ -111,31 +106,29 @@ def tile_list_inhibited_enzyme_flux_kernel(
 
         def gather_words(a):
             for f in range(2):
-                nc.vector.tensor_copy(gw[a][f][:], tabw[a][:].indirect(offs_t[:, 32 * f : 32 * (f + 1)]))
+                nc.vector.tensor_copy(gw[a][f][:], tabw[a].indirect(offs_t[:, 32 * f : 32 * (f + 1)]))
 
-        def round_block(copy, out, raw, ms=slice(0, P)):
-            copy(out=out.rearrange("p (t m j) -> p m j t", t=4, j=4)[:, ms], in_=raw[:].rearrange("p j (m t) -> p m j t", t=4)[:, ms])
+        rounded = {}
 
-        def quantise_block(b, a, tag):
-            rounded = sb([P, 2048], BF16, f"w1g{b}{a}", tag)
-            round_block(nc.scalar.copy, rounded[:], w1raw[b, a])
-            nc.vector.quantize_mx(out=w1c[b, a][:, :].bitcast(FP8X4), scales=w1s[b, a][:, :], in_=rounded[:])
+        def round_block(b, a, tag=None, ms=slice(0, P), copy=nc.scalar.copy):
+            if (b, a) not in rounded:
+                rounded[b, a] = sb([P, 2048], BF16, f"w1g{b}{a}", tag)[:]
+            out = rounded[b, a].rearrange("p (t m j) -> p m j t", t=4, j=4)[:, ms]
+            copy(out=out, in_=w1raw[b, a][:].rearrange("p j (m t) -> p m j t", t=4)[:, ms])
+
+        def quantise_block(b, a):
+            nc.vector.quantize_mx(out=w1c[b, a].bitcast(FP8X4), scales=w1s[b, a], in_=rounded[b, a])
 
         def round_pair(copy, out, u, x):
             dst = out[:].rearrange("p (t m j) -> p m j t", t=2, j=4)[:, 64 * x : 64 * (x + 1)]
             copy(out=dst, in_=w1half[x][:].rearrange("p j (m u t) -> p u m j t", u=2, t=2)[:, u])
 
-        def quantise_shared_block():
-            rounded = sb([P, 2048], BF16, "w1g2", "sum0")
-            round_block(nc.vector.tensor_copy, rounded[:], w1raw[LAST, 0], slice(0, M_VECTOR))
-            round_block(nc.scalar.copy, rounded[:], w1raw[LAST, 0], slice(M_VECTOR, P))
-            nc.vector.quantize_mx(out=w1c[LAST, 0].bitcast(FP8X4), scales=w1s[LAST, 0], in_=rounded[:])
-
         gather_words(0)
         for f in range(2):
             nc.vector.tensor_copy(gs[f][:], tabs[:].indirect(offs_t[:, 32 * f : 32 * (f + 1)]))
-        w1c[0, 0] = sb([P, 512], U32, "w1c00", "tabs")
-        quantise_block(0, 0, None)
+        w1c[0, 0] = sb([P, 512], U32, "w1c00", "tabs")[:]
+        round_block(0, 0)
+        quantise_block(0, 0)
         gather_words(1)
         pairs = []
         for u in range(2):
@@ -156,8 +149,8 @@ def tile_list_inhibited_enzyme_flux_kernel(
                 in_=w2raw[b][:].bitcast(U16).rearrange("p (g m t) -> p g t m", t=4, m=P),
             )
 
-        def deal_scales():
-            w2s[0] = sb([P, N], U8, "w2s0", "sum2")
+        def deal_scales(tag):
+            w2s[0] = sb([P, N], U8, "w2s0", tag)
             nc.vector.tensor_copy(
                 out=w2s[0][:].rearrange("p (g t m) -> p g t m", t=4, m=P),
                 in_=w2sraw[:].rearrange("p (g m t) -> p g t m", t=4, m=P),
@@ -165,14 +158,32 @@ def tile_list_inhibited_enzyme_flux_kernel(
             for b in range(1, HB):
                 nc.sync.dma_start(out=w2s[b][0 : P - 4 * b, :].bitcast(I32), in_=w2s[0][4 * b : P, :].bitcast(I32))
 
-        h, sums = {}, {}
-        work = [sb([P, T], F32, f"work{b}", f"tabw{b}") for b in range(LAST)]
-        sub = {b: work[b][:, : 4 * PAIRS] for b in range(LAST)}
-        root = {1: work[1][:, 4 * PAIRS :]}
+        h = {}
+        work = sb([P, 8 * 1024], F32, "work", "tabw")
+        slots = work[:].rearrange("p (r x i) -> p r x i", x=2, i=PAIRS)
+        sub = {(b, 0): slots[:, 4 * b : 4 * b + 4, 0] for b in range(LAST)}
+        den = {(b, 0): slots[:, 4 * b : 4 * b + 4, 1] for b in range(LAST)}
+        rec = {}
 
-        def make_h(r):
+        def slot(r):
+            return work[:, 1024 * r : 1024 * (r + 1)].bitcast(BF16)
+
+        last = sb([P, 4 * 1024], F32, "last")
+        lslots = last[:].rearrange("p (t x i) -> p t x i", x=4, i=HALF)
+        sub[LAST, 0], sub[LAST, HALF], late = lslots[:, :, 0], lslots[:, :, 1], lslots[:, :, 2]
+
+        def part(d, r, lo, hi):
             b, t = divmod(r, 4)
-            h[r] = sb([P, S], F32, f"h{r}", H_TAG.get(r))
+            base = HALF if (b == LAST and lo >= HALF) else 0
+            return d[b, base][:, t, lo - base : hi - base]
+
+        def chunk(d, b, c):
+            base = HALF if (b == LAST and c >= 2) else 0
+            return d[b, base][:, :, 128 * c - base : 128 * (c + 1) - base]
+
+        def make_h(r, tag=None):
+            b, t = divmod(r, 4)
+            h[r] = sb([P, S], F32, f"h{r}", tag)
             cols = slice(P * t, P * (t + 1))
             for f in range(2):
                 acc = banks[(2 * r + f) % 8]
@@ -188,203 +199,247 @@ def tile_list_inhibited_enzyme_flux_kernel(
                     )
                 nc.scalar.activation(out=h[r][:, 512 * f : 512 * (f + 1)], in_=acc[:], func=ACT.Relu)
 
-        def pick(a_out, sum_out, pieces):
-            for k, (r, i0, w) in enumerate(pieces):
-                nc.vector.tensor_copy(a_out[:, w * k : w * (k + 1)], h[r][:].indirect(pos1_t[:, i0 // 16 : (i0 + w) // 16]))
-            for k, (r, i0, w) in enumerate(pieces):
-                cols = slice(w * k, w * (k + 1))
-                nc.vector.tensor_tensor(sum_out[:, cols], h[r][:].indirect(pos2_t[:, i0 // 16 : (i0 + w) // 16]), a_out[:, cols], ALU.add)
+        def pick_a(r, lo, hi):
+            nc.vector.tensor_copy(part(sub, r, lo, hi), h[r][:].indirect(pos1_t[:, lo // 16 : hi // 16]))
 
-        def whole_slice(r):
-            make_h(r)
-            b, t = divmod(r, 4)
-            cols = slice(PAIRS * t, PAIRS * (t + 1))
-            if r == 3:
-                root[0] = sb([P, 4 * PAIRS], F32, "root0")[:]
-            if r in SUMS_APART:
-                sums[r] = sb([P, PAIRS], F32, f"sum{r}")[:]
-            else:
-                sums[r] = root[b][:, cols]
-            pick(sub[b][:, cols], sums[r], [(r, i0, HALF) for i0 in (0, HALF)])
-            nc.gpsimd.tensor_scalar(out=sub[b][:, cols], in0=sub[b][:, cols], scalar1=vm[:, b, t : t + 1], scalar2=0.0, op0=ALU.mult, op1=ALU.add)
+        def pick_sum(r, lo, hi):
+            nc.vector.tensor_tensor(part(den, r, lo, hi), h[r][:].indirect(pos2_t[:, lo // 16 : hi // 16]), part(sub, r, lo, hi), ALU.add)
+
+        def times_vmax(r, lo, hi, out=None):
+            x = part(sub, r, lo, hi)
+            nc.gpsimd.tensor_scalar(out=x if out is None else out, in0=x, scalar1=vm[:, r // 4, r % 4 : r % 4 + 1], scalar2=0.0, op0=ALU.mult, op1=ALU.add)
+
+        def scalar_vmax(r, lo, hi, out=None):
+            x = part(sub, r, lo, hi)
+            nc.scalar.activation(out=x if out is None else out, in_=x, func=ACT.Copy, scale=vm[:, r // 4, r % 4 : r % 4 + 1])
+
+        def picks(r, lo, hi):
+            mid = (lo + hi) // 2
+            for pick in (pick_a, pick_sum):
+                pick(r, lo, mid)
+                pick(r, mid, hi)
+
+        def whole(r):
+            picks(r, 0, PAIRS)
+            times_vmax(r, 0, PAIRS)
 
         def invert(out, x):
             nc.scalar.activation(out=out, in_=x, func=ACT.Abs_reciprocal_sqrt, bias=1.0)
 
-        def invert_slice(r):
-            b, t = divmod(r, 4)
-            invert(root[b][:, PAIRS * t : PAIRS * (t + 1)], sums[r])
-
-        def times_vmax(x, r):
-            b, t = divmod(r, 4)
-            nc.scalar.activation(out=x, in_=x, func=ACT.Copy, scale=vm[:, b, t : t + 1])
-
-        def chunks(x, c0, c1):
-            return x.rearrange("p (t i) -> p t i", t=4)[:, :, CHUNK * c0 : CHUNK * c1]
-
-        def square(b, c0, c1, out=None):
-            x = chunks(root[b], c0, c1)
-            out = x if out is None else out
+        def square(out, x):
             nc.scalar.activation(out=out, in_=x, func=ACT.Square)
 
-        def pick_chunk(c):
-            sub[LAST, c] = sb([P, 4 * CHUNK], F32, f"subc{c}", f"sum{6 + c % 2}")[:]
-            sums[LAST, c] = sb([P, 4 * CHUNK], F32, f"sumc{c}")[:]
-            pick(sub[LAST, c], sums[LAST, c], [(4 * LAST + t, CHUNK * c, CHUNK) for t in range(4)])
+        z4, zc, zs = {}, {}, {}
 
-        def finish_chunk(c):
-            invert(sums[LAST, c], sums[LAST, c])
-            root[LAST, c] = sb([P, 4 * CHUNK], F32, f"rootc{c}")[:]
-            for t in range(4):
-                times_vmax(sub[LAST, c][:, CHUNK * t : CHUNK * (t + 1)], 4 * LAST + t)
-            nc.scalar.activation(out=root[LAST, c], in_=sums[LAST, c], func=ACT.Square)
+        def weave(b, c, tag=None, src=None):
+            if (b, c) not in z4:
+                z4[b, c] = sb([P, 512], BF16, f"z4{b}{c}", tag)[:]
+            x = chunk(sub, b, c) if src is None else src
+            x, y = [v.rearrange("p t (c i) -> p c t i", i=4) for v in (x, rec[b, c])]
+            nc.vector.tensor_tensor(out=z4[b, c].rearrange("p (c i t) -> p c t i", i=4, t=4), in0=x, in1=y, op=ALU.mult)
 
-        def weave(out, x, y):
-            x, y = [v.rearrange("p t (c i) -> p c t i", i=4) for v in (x, y)]
-            nc.vector.tensor_tensor(out=out.rearrange("p (c i t) -> p c t i", i=4, t=4), in0=x, in1=y, op=ALU.mult)
+        def out_bank(c, g, t):
+            w = CHUNKS[c][1] - CHUNKS[c][0]
+            first = CHUNKS[c][0] * 8 // PAIRS
+            at = (4 * g + t) * w
+            return banks[first + at // 512], at % 512, w
 
-        def weave_gpsimd(out, x, y):
-            x, y = [v.rearrange("p t (c i) -> p c t i", i=4) for v in (x, y)]
-            nc.gpsimd.tensor_tensor(out=out.rearrange("p (c i t) -> p c t i", i=4, t=4), in0=x, in1=y, op=ALU.mult)
-
-        def multiply(z4, passes, c, tag=None):
-            codes = sb([P, CHUNK * len(passes)], U32, f"zc{passes[0]}{c}", tag)
-            scales = sb([P, CHUNK * len(passes)], U8, f"zs{passes[0]}{c}")
-            nc.vector.quantize_mx(out=codes[:].bitcast(FP8X4), scales=scales[:], in_=z4)
-            for k, b in enumerate(passes):
-                cols = slice(CHUNK * k, CHUNK * (k + 1))
-                for g in range(NG):
-                    for t in range(4):
-                        c0 = 512 * g + P * t
-                        nc.tensor.matmul_mx(
-                            out=banks[NG * c + g][:, CHUNK * t : CHUNK * (t + 1)],
-                            lhsT=w2w[b][:, 2 * c0 : 2 * (c0 + P)].bitcast(FP4X4),
-                            lhsT_scale=w2s[b][:, c0 : c0 + P],
-                            rhs=codes[:, cols].bitcast(FP8X4),
-                            rhs_scale=scales[:, cols],
-                            start=(b == 0 and t == 0),
-                            stop=(b == LAST and t == 3),
-                        )
-
-        zfirst = {}
-        WIDE = 4 * CHUNK
-
-        def weave_first(c):
-            zfirst[c] = sb([P, WIDE], BF16, f"zfirst{c}", ("zfirst0", "sq00", "zfirst0", "zwoven1")[c])
-            if c in PLAIN:
-                nc.gpsimd.tensor_tensor(out=chunks(zfirst[c][:], 0, 1), in0=chunks(sub[0], c, c + 1), in1=chunks(root[0], c, c + 1), op=ALU.mult)
-            else:
-                weave_gpsimd(zfirst[c][:], chunks(sub[0], c, c + 1), chunks(root[0], c, c + 1))
-
-        def interleave(c):
-            plain, zfirst[c] = zfirst[c], sb([P, WIDE], BF16, f"zwoven{c}")
-            nc.scalar.copy(out=zfirst[c][:].rearrange("p (x i t) -> p x t i", i=4, t=4), in_=plain[:].rearrange("p (t x i) -> p x t i", i=4, t=4))
-
-        def products(c):
-            z4 = sb([P, LAST * WIDE], BF16, f"zlast{c}", f"zlast{c % 2}")
-            weave(z4[:, :WIDE], chunks(sub[1], c, c + 1), chunks(root[1], c, c + 1))
-            if c + 1 == NC:
-                multiply(zfirst[c][:], [0], c)
-                store_codes(0, NC - 2)
-                multiply(z4[:, :WIDE], [1], c)
-            weave(z4[:, WIDE:], chunks(sub[LAST, c], 0, 1), chunks(root[LAST, c], 0, 1))
-            if c + 1 == NC:
-                multiply(z4[:, WIDE:], [LAST], c)
-            else:
-                multiply(zfirst[c][:], [0], c, f"rootc{c}" if c + 2 < NC else None)
-                multiply(z4[:], [1, LAST], c)
+        def multiply(b, c, tag=None):
+            w = CHUNKS[c][1] - CHUNKS[c][0]
+            zc[b, c] = sb([P, w], U32, f"zc{b}{c}", tag)
+            zs[b, c] = sb([P, w], U8, f"zs{b}{c}")
+            nc.vector.quantize_mx(out=zc[b, c][:].bitcast(FP8X4), scales=zs[b, c][:], in_=z4[b, c])
+            for g in range(NG):
+                for t in range(4):
+                    bank, at, w = out_bank(c, g, t)
+                    c0 = 512 * g + P * t
+                    nc.tensor.matmul_mx(
+                        out=bank[:, at : at + w],
+                        lhsT=w2w[b][:, 2 * c0 : 2 * (c0 + P)].bitcast(FP4X4),
+                        lhsT_scale=w2s[b][:, c0 : c0 + P],
+                        rhs=zc[b, c][:].bitcast(FP8X4),
+                        rhs_scale=zs[b, c][:],
+                        start=(b == 0 and at == 0),
+                        stop=(b == LAST and at + w == 512),
+                    )
 
         out_rows = out_0.rearrange("(g p t) i -> g p t i", p=P, t=4)
         out_words = out_1.rearrange("g p m t -> p g (m t)").bitcast(I32)
-        y4 = [sb([P, 4 * PAIRS], BF16, f"y4{g}") for g in range(NG)]
+        y, y4 = {}, {}
 
-        def store_rows(c, g, tag=None, copy=nc.scalar.copy):
-            y = sb([P, 4, CHUNK], F32, f"y{c}{g}", tag)
-            copy(out=y[:], in_=banks[NG * c + g][:].rearrange("p (t i) -> p t i", t=4))
-            nc.sync.dma_start(out=out_rows[g, :, :, CHUNK * c : CHUNK * (c + 1)], in_=y[:])
-            return y
+        def empty(c, g, tag=None, copy=nc.scalar.copy):
+            lo, hi = CHUNKS[c]
+            y[c, g] = sb([P, 4, hi - lo], F32, f"y{c}{g}", tag)
+            step = 512 // (hi - lo)
+            for t in range(0, 4, step):
+                copy(out=y[c, g][:, t : t + step, :], in_=out_bank(c, g, t)[0][:].rearrange("p (t i) -> p t i", t=step))
+            nc.sync.dma_start(out=out_rows[g, :, :, lo:hi], in_=y[c, g][:])
 
-        def round_bank(c, g, copy=nc.scalar.copy):
-            copy(
-                out=y4[g][:, 4 * CHUNK * c : 4 * CHUNK * (c + 1)].rearrange("p (i t) -> p i t", t=4),
-                in_=banks[NG * c + g][:].rearrange("p (t i) -> p i t", t=4),
-            )
-
-        def round_rows(c, g, y):
+        def round_rows(c, g, tag=None):
+            lo, hi = CHUNKS[c]
+            y4[c, g] = sb([P, 4 * (hi - lo)], BF16, f"y4{c}{g}", tag)
             nc.vector.tensor_copy(
-                out=y4[g][:, 4 * CHUNK * c : 4 * CHUNK * (c + 1)].rearrange("p (x i t) -> p x t i", i=4, t=4),
-                in_=y[:].rearrange("p t (x i) -> p x t i", i=4),
+                out=y4[c, g][:].rearrange("p (x i t) -> p x t i", i=4, t=4),
+                in_=y[c, g][:].rearrange("p t (x i) -> p x t i", i=4),
             )
 
-        def store_codes(c0, c1):
-            lo, hi = CHUNK * c0, CHUNK * c1
+        def round_bank(c, g, copy, tag=None):
+            y4[c, g] = sb([P, 512], BF16, f"y4{c}{g}", tag)
+            copy(out=y4[c, g][:].rearrange("p (i t) -> p i t", t=4), in_=out_bank(c, g, 0)[0][:].rearrange("p (t i) -> p i t", t=4))
+
+        ycodes = sb([P, NG * PAIRS], U32, "ycodes")
+
+        def store_codes(c):
+            lo, hi = CHUNKS[c]
             for g in range(NG):
                 cols = slice(PAIRS * g + lo, PAIRS * g + hi)
-                nc.vector.quantize_mx(out=ycodes[:, cols].bitcast(FP8X4), scales=yscales[:, cols], in_=y4[g][:, 4 * lo : 4 * hi])
+                nc.vector.quantize_mx(out=ycodes[:, cols].bitcast(FP8X4), scales=yscales[:, cols], in_=y4[c, g][:])
             nc.sync.dma_start(out=out_words[:, :, lo:hi], in_=ycodes[:].bitcast(I32).rearrange("p (g m) -> p g m", g=NG)[:, :, lo:hi])
 
         for b in range(HB):
             deal_words(b)
-        whole_slice(0)
-        whole_slice(1)
-        for a in range(KA):
-            quantise_block(1, a, None)
-            whole_slice(2 + a)
-        invert_slice(0)
-        invert_slice(1)
-        whole_slice(4)
-        quantise_shared_block()
-        whole_slice(5)
-        quantise_block(LAST, 1, None)
-        whole_slice(6)
-        invert_slice(2)
-        deal_scales()
-        whole_slice(7)
-        invert_slice(3)
-        for t in range(4):
-            make_h(4 * LAST + t)
-        invert_slice(6)
-        pick_chunk(0)
-        sq00 = sb([P, WIDE], F32, "sq00")
-        square(0, 0, 1, chunks(sq00[:], 0, 1))
-        zfirst[0] = sb([P, WIDE], BF16, "zfirst0")
-        weave(zfirst[0][:], chunks(sub[0], 0, 1), chunks(sq00[:], 0, 1))
-        square(0, 1, 2)
-        invert_slice(4)
-        invert_slice(7)
-        pick_chunk(1)
-        invert_slice(5)
-        weave_first(1)
-
-        spent = (("raw00", "raw20"), ("raw21", "w1half0"))
-        ycodes = sb([P, NG * PAIRS], U32, "ycodes")
-        for c in range(NC):
-            if c < 2:
-                square(1, c, c + 1)
-            if c in PLAIN:
-                interleave(c)
-            finish_chunk(c)
-            if c == 0:
-                square(0, 2, NC)
-            if c in (1, 2):
-                square(1, c + 1, c + 2)
-            products(c)
-            if c + 2 < NC:
-                weave_first(c + 2)
-                pick_chunk(c + 2)
-            if 0 < c < NC - 1:
-                for g in range(NG):
-                    store_rows(c - 1, g, spent[c - 1][g])
-                for g in range(NG):
-                    round_bank(c - 1, g)
-
+        for r in range(3):
+            make_h(r)
+        whole(0)
+        mid = sb([P, KA * 2048], BF16, "mid")
+        rounded[1, 0] = mid[:, :2048]
+        round_block(1, 0)
+        whole(1)
+        for x in range(2):
+            nc.scalar.copy(out=mid[:, 2048:].rearrange("p (t m j) -> p m j t", t=4, j=4)[:, 64 * x : 64 * (x + 1)], in_=mid_half[x][:].rearrange("p j (m t) -> p m j t", t=4))
+        make_h(3, "half10")
+        whole(2)
+        nc.vector.quantize_mx(out=mid_codes[:].bitcast(FP8X4), scales=mid_scales[:], in_=mid[:])
+        round_block(2, 0, "w1g00", slice(0, 64))
+        make_h(4)
+        whole(3)
+        deal_scales("raw10")
+        make_h(5)
+        round_block(2, 0, None, slice(64, P))
+        whole(4)
+        make_h(6)
+        whole(5)
+        quantise_block(2, 0)
+        round_block(2, 1)
+        make_h(7)
+        whole(6)
+        quantise_block(2, 1)
+        whole(7)
+        arena = sb([P, 5120], F32, "arena", "raw21")
+        root_a = {c: arena[:, 1536 * c : 1536 * c + 1024].rearrange("p (r i) -> p r i", r=8) for c in range(2)}
+        root_b = arena[:, 3072:].rearrange("p (r i) -> p r i", r=8)
+        root_last = {0: arena[:, 1024:1536].rearrange("p (t i) -> p t i", t=4)}
+        for c in (1, 2):
+            root_last[c] = sb([P, 4, 128], F32, f"root_last{c}")[:]
+        den[LAST, 0] = lslots[:, :, 3]
+        den[LAST, HALF] = arena[:, 512:1536].rearrange("p (t i) -> p t i", t=4)
+        for c in (2, 3):
+            for b in range(LAST):
+                rec[b, c] = slots[:, 4 * b : 4 * b + 4, 1, 128 * c : 128 * (c + 1)]
+        root_last[3] = chunk(den, LAST, 3)
+        def pair_tile(c, tag):
+            both = sb([P, 1024], BF16, f"zpair{c}", tag)
+            for b in range(LAST):
+                z4[b, c] = both[:, 512 * b : 512 * (b + 1)]
+        def sums_early(c):
+            return slots[:, :, 1, 128 * c : 128 * (c + 1)]
+        def square_early(c):
+            square(sums_early(c), root_a[c])
+            for b in range(LAST):
+                rec[b, c] = sums_early(c)[:, 4 * b : 4 * b + 4]
+        def square_one(b, c):
+            rec[b, c] = sums_early(c)[:, 4 * b : 4 * b + 4]
+            square(rec[b, c], root_a[c][:, 4 * b : 4 * b + 4])
+        def invert_last(c):
+            invert(root_last[c], chunk(den, LAST, c))
+        def square_last(c):
+            square(chunk(den, LAST, c), root_last[c])
+            rec[LAST, c] = chunk(den, LAST, c)
+        def early_weaves(c):
+            for b in range(LAST):
+                weave(b, c)
+            for b in range(LAST):
+                multiply(b, c)
+        def both_vmax(r):
+            t = r - 8
+            x, out = lslots[:, t, 0:2], lslots[:, t, 0:3:2]
+            if r == 11:
+                nc.scalar.activation(out=out, in_=x, func=ACT.Copy, scale=vm[:, LAST, t : t + 1])
+            else:
+                nc.gpsimd.tensor_scalar(out=out, in0=x, scalar1=vm[:, LAST, t : t + 1], scalar2=0.0, op0=ALU.mult, op1=ALU.add)
+        invert(root_b[:, :4], slots[:, :4, 1, HALF:])
+        for c in range(2):
+            invert(root_a[c][:, :4], sums_early(c)[:, :4])
+        square(slots[:, :4, 1, HALF:], root_b[:, :4])
+        for r in range(8, 12):
+            make_h(r, f"h{r - 8}" if r < 11 else None)
+            for lo in (0, HALF):
+                pick_a(r, lo, lo + HALF)
+            pick_sum(r, 0, HALF)
+            if r < 11:
+                both_vmax(r)
+            if r in (9, 10):
+                invert(root_a[r - 9][:, 4:], sums_early(r - 9)[:, 4:])
+            if r == 10:
+                invert(root_b[:, 4:], slots[:, 4:, 1, HALF:])
+        square_early(0)
+        square(slots[:, 4:, 1, HALF:], root_b[:, 4:])
+        invert_last(0)
+        both_vmax(11)
+        square_last(0)
+        invert_last(1)
+        square_early(1)
+        square_last(1)
+        weave(0, 0)
+        weave(1, 0)
+        multiply(0, 0)
+        pick_sum(8, HALF, PAIRS)
+        multiply(1, 0)
+        pick_sum(9, HALF, PAIRS)
+        weave(LAST, 0)
+        pick_sum(10, HALF, PAIRS)
+        multiply(LAST, 0)
+        pick_sum(11, HALF, PAIRS)
+        early_weaves(1)
+        pair_tile(2, "root_last1")
+        weave(LAST, 1)
+        weave(0, 2)
+        multiply(LAST, 1)
+        weave(1, 2)
+        multiply(0, 2)
+        multiply(1, 2)
+        invert_last(2)
+        invert_last(3)
         for g in range(NG):
-            round_rows(NC - 2, g, store_rows(NC - 2, g))
-        store_codes(NC - 2, NC - 1)
+            empty(0, g, ("h4", "h5")[g])
+        round_bank(0, 0, nc.scalar.copy, "h6")
+        round_bank(0, 1, nc.scalar.copy, "h7")
+        store_codes(0)
+        square_last(2)
+        pair_tile(3, "root_last2")
+        weave(LAST, 2, None, late[:, :, :128])
+        weave(0, 3)
+        multiply(LAST, 2)
+        weave(1, 3)
+        multiply(0, 3)
+        multiply(1, 3)
+        empty(1, 0, "half00")
+        empty(1, 1, "half01")
+        square_last(3)
+        round_bank(1, 0, nc.scalar.copy, "w1g00")
+        weave(LAST, 3, None, late[:, :, 128:])
+        round_bank(1, 1, nc.scalar.copy, "w1g21")
+        multiply(LAST, 3)
+        store_codes(1)
+        for g in range(NG):
+            empty(2, g, ("h0", "h1")[g])
+        round_bank(2, 0, nc.scalar.copy, "mid")
+        round_bank(2, 1, nc.scalar.copy, "tabs")
+        store_codes(2)
         for g, copy in enumerate((nc.scalar.copy, nc.vector.tensor_copy)):
-            store_rows(NC - 1, g, None, copy)
-            round_bank(NC - 1, g, copy)
-        store_codes(NC - 1, NC)
+            empty(3, g, f"gw0{g}", copy)
+            round_bank(3, g, copy, f"gw1{g}")
+        store_codes(3)
 
         for q in range(4):
             (nc.sync, nc.scalar)[q % 2].dma_start(

@@ -22,6 +22,7 @@ HB = H // 512
 NG = N // 512
 LAST = HB - 1
 HALF = PAIRS // 2
+PLACED = {"raw21": 0, "root0": 0, "first": 0, "early_codes": 4}
 CHUNKS = ((0, 128), (128, 256), (256, 384), (384, 512))
 
 
@@ -31,9 +32,12 @@ def tile_list_inhibited_enzyme_flux_kernel(
     nc = tc.nc
     with ExitStack() as ctx:
         keep = ctx.enter_context(tc.tile_pool(name="keep", bufs=1))
+        lay = ctx.enter_context(tc.tile_pool(name="lay", bufs=1))
         psum = ctx.enter_context(tc.psum_pool(name="psum", bufs=1))
 
         def sb(shape, dtype, name, tag=None):
+            if name in PLACED:
+                return lay.tile(shape, dtype, name=name, offset=1024 * PLACED[name], align_bytes=64)
             return keep.tile(shape, dtype, name=name, tag=tag or name, align_bytes=64)
 
         offs_t = keep.tile([P, S // 16], U16, name="offs_t")
@@ -44,7 +48,9 @@ def tile_list_inhibited_enzyme_flux_kernel(
         tabs = sb([P, T], U8, "tabs")
         w2raw = [sb([P, 2 * N], U8, f"w2raw{b}") for b in range(HB)]
         w2sraw = sb([P, N], U8, "w2sraw")
-        w2s = {b: sb([P, N], U8, f"w2s{b}") for b in range(1, HB)}
+        w2s = {b: sb([P, N], U8, f"w2s{b}") for b in range(HB)}
+        w2sdealt = sb([P, N], U8, "w2sdealt")
+
         vm = sb([P, HB, 4], F32, "vm")
         w1c = {(b, a): sb([P, 512], U32, f"w1c{b}{a}")[:] for a in range(KA) for b in (0, LAST) if (b, a) != (0, 0)}
         w1s = {(b, a): sb([P, 512], U8, f"w1s{b}{a}")[:] for b in (0, LAST) for a in range(KA)}
@@ -54,7 +60,8 @@ def tile_list_inhibited_enzyme_flux_kernel(
             w1c[1, a] = mid_codes[:, 512 * a : 512 * (a + 1)]
             w1s[1, a] = mid_scales[:, 512 * a : 512 * (a + 1)]
         gw = [[sb([P, 512], U32, f"gw{a}{f}") for f in range(2)] for a in range(KA)]
-        gs = [sb([P, 512], U8, f"gs{f}") for f in range(2)]
+        gs_all = sb([P, S], U8, "gs")
+        gs = [gs_all[:, 512 * f : 512 * (f + 1)] for f in range(2)]
         banks = [psum.tile([P, 512], F32, name=f"bank{i}") for i in range(8)]
         yscales = sb([P, NG * PAIRS], U8, "yscales")
         warm = keep.tile([P, 2], F32, name="warm")
@@ -63,7 +70,7 @@ def tile_list_inhibited_enzyme_flux_kernel(
         nc.vector.memset(warm[:, 0:1], 1.0)
         nc.scalar.activation(out=warm[:, 1:2], in_=warm[:, 0:1], func=ACT.Abs_reciprocal_sqrt)
         nc.vector.memset(w2sraw[:].bitcast(I32), 0)
-        for b in range(1, HB):
+        for b in range(HB):
             nc.vector.memset(w2s[b][:].bitcast(I32), 0)
 
         w1raw = {}
@@ -78,6 +85,7 @@ def tile_list_inhibited_enzyme_flux_kernel(
 
         for q in range(4):
             nc.gpsimd.dma_start(out=tabs[32 * q : 32 * q + 4 * KA, :].bitcast(I32), in_=tab_scales[:, 4 * q : 4 * q + 4, :].bitcast(I32))
+        nc.gpsimd.dma_start(out=w2sraw[0:96:2, :].bitcast(I32), in_=w2_scales.rearrange("b q c -> (b q) c").bitcast(I32))
         load_tab(0)
         nc.sync.dma_start(offs_t[:], offs)
         load_w1(0, 0)
@@ -101,8 +109,6 @@ def tile_list_inhibited_enzyme_flux_kernel(
         mid_half = load_halves(1)
         for a in range(KA):
             load_w1(LAST, a)
-        for q in range(4):
-            nc.sync.dma_start(out=w2sraw[32 * q : 32 * q + 4 * HB, :].bitcast(I32), in_=w2_scales[:, 4 * q : 4 * q + 4, :].bitcast(I32))
 
         def gather_words(a):
             for f in range(2):
@@ -124,8 +130,11 @@ def tile_list_inhibited_enzyme_flux_kernel(
             copy(out=dst, in_=w1half[x][:].rearrange("p j (m u t) -> p u m j t", u=2, t=2)[:, u])
 
         gather_words(0)
-        for f in range(2):
-            nc.vector.tensor_copy(gs[f][:], tabs[:].indirect(offs_t[:, 32 * f : 32 * (f + 1)]))
+        nc.vector.tensor_copy(gs_all[:], tabs[:].indirect(offs_t[:]))
+        nc.vector.tensor_copy(
+            out=w2sdealt[:].rearrange("p (g t m) -> p g t m", t=4, m=P),
+            in_=w2sraw[:].rearrange("p (g m t) -> p g t m", t=4, m=P),
+        )
         w1c[0, 0] = sb([P, 512], U32, "w1c00", "tabs")[:]
         round_block(0, 0)
         quantise_block(0, 0)
@@ -149,14 +158,11 @@ def tile_list_inhibited_enzyme_flux_kernel(
                 in_=w2raw[b][:].bitcast(U16).rearrange("p (g m t) -> p g t m", t=4, m=P),
             )
 
-        def deal_scales(tag):
-            w2s[0] = sb([P, N], U8, "w2s0", tag)
-            nc.vector.tensor_copy(
-                out=w2s[0][:].rearrange("p (g t m) -> p g t m", t=4, m=P),
-                in_=w2sraw[:].rearrange("p (g m t) -> p g t m", t=4, m=P),
-            )
-            for b in range(1, HB):
-                nc.sync.dma_start(out=w2s[b][0 : P - 4 * b, :].bitcast(I32), in_=w2s[0][4 * b : P, :].bitcast(I32))
+        def move_scales():
+            for b in range(HB):
+                for q in range(4):
+                    row = 2 * (16 * b + 4 * q)
+                    nc.sync.dma_start(out=w2s[b][32 * q : 32 * q + 4, :].bitcast(I32), in_=w2sdealt[row : row + 8 : 2, :].bitcast(I32))
 
         h = {}
         work = sb([P, 8 * 1024], F32, "work", "tabw")
@@ -168,9 +174,9 @@ def tile_list_inhibited_enzyme_flux_kernel(
         def slot(r):
             return work[:, 1024 * r : 1024 * (r + 1)].bitcast(BF16)
 
-        last = sb([P, 4 * 1024], F32, "last")
-        lslots = last[:].rearrange("p (t x i) -> p t x i", x=4, i=HALF)
-        sub[LAST, 0], sub[LAST, HALF], late = lslots[:, :, 0], lslots[:, :, 1], lslots[:, :, 2]
+        last_a = sb([P, 4, PAIRS], F32, "last_a")
+        last_num = sb([P, 4, PAIRS], F32, "last_num")
+        sub[LAST, 0], sub[LAST, HALF] = last_a[:, :, :HALF], last_a[:, :, HALF:]
 
         def part(d, r, lo, hi):
             b, t = divmod(r, 4)
@@ -231,12 +237,12 @@ def tile_list_inhibited_enzyme_flux_kernel(
 
         z4, zc, zs = {}, {}, {}
 
-        def weave(b, c, tag=None, src=None):
+        def weave(b, c, tag=None, eng=nc.vector):
             if (b, c) not in z4:
                 z4[b, c] = sb([P, 512], BF16, f"z4{b}{c}", tag)[:]
-            x = chunk(sub, b, c) if src is None else src
+            x = chunk(sub, b, c) if b < LAST else last_num[:, :, 128 * c : 128 * (c + 1)]
             x, y = [v.rearrange("p t (c i) -> p c t i", i=4) for v in (x, rec[b, c])]
-            nc.vector.tensor_tensor(out=z4[b, c].rearrange("p (c i t) -> p c t i", i=4, t=4), in0=x, in1=y, op=ALU.mult)
+            eng.tensor_tensor(out=z4[b, c].rearrange("p (c i t) -> p c t i", i=4, t=4), in0=x, in1=y, op=ALU.mult)
 
         def out_bank(c, g, t):
             w = CHUNKS[c][1] - CHUNKS[c][0]
@@ -246,9 +252,10 @@ def tile_list_inhibited_enzyme_flux_kernel(
 
         def multiply(b, c, tag=None):
             w = CHUNKS[c][1] - CHUNKS[c][0]
-            zc[b, c] = sb([P, w], U32, f"zc{b}{c}", tag)
+            if (b, c) not in zc:
+                zc[b, c] = sb([P, w], U32, f"zc{b}{c}", tag)[:]
             zs[b, c] = sb([P, w], U8, f"zs{b}{c}")
-            nc.vector.quantize_mx(out=zc[b, c][:].bitcast(FP8X4), scales=zs[b, c][:], in_=z4[b, c])
+            nc.vector.quantize_mx(out=zc[b, c].bitcast(FP8X4), scales=zs[b, c][:], in_=z4[b, c])
             for g in range(NG):
                 for t in range(4):
                     bank, at, w = out_bank(c, g, t)
@@ -257,7 +264,7 @@ def tile_list_inhibited_enzyme_flux_kernel(
                         out=bank[:, at : at + w],
                         lhsT=w2w[b][:, 2 * c0 : 2 * (c0 + P)].bitcast(FP4X4),
                         lhsT_scale=w2s[b][:, c0 : c0 + P],
-                        rhs=zc[b, c][:].bitcast(FP8X4),
+                        rhs=zc[b, c].bitcast(FP8X4),
                         rhs_scale=zs[b, c][:],
                         start=(b == 0 and at == 0),
                         stop=(b == LAST and at + w == 512),
@@ -296,6 +303,7 @@ def tile_list_inhibited_enzyme_flux_kernel(
                 nc.vector.quantize_mx(out=ycodes[:, cols].bitcast(FP8X4), scales=yscales[:, cols], in_=y4[c, g][:])
             nc.sync.dma_start(out=out_words[:, :, lo:hi], in_=ycodes[:].bitcast(I32).rearrange("p (g m) -> p g m", g=NG)[:, :, lo:hi])
 
+        move_scales()
         for b in range(HB):
             deal_words(b)
         for r in range(3):
@@ -310,114 +318,103 @@ def tile_list_inhibited_enzyme_flux_kernel(
         make_h(3, "half10")
         whole(2)
         nc.vector.quantize_mx(out=mid_codes[:].bitcast(FP8X4), scales=mid_scales[:], in_=mid[:])
-        round_block(2, 0, "w1g00", slice(0, 64))
+        round_block(2, 0, "w1g00")
         make_h(4)
         whole(3)
-        deal_scales("raw10")
+        quantise_block(2, 0)
         make_h(5)
-        round_block(2, 0, None, slice(64, P))
         whole(4)
         make_h(6)
         whole(5)
-        quantise_block(2, 0)
         round_block(2, 1)
         make_h(7)
         whole(6)
         quantise_block(2, 1)
         whole(7)
-        arena = sb([P, 5120], F32, "arena", "raw21")
-        root_a = {c: arena[:, 1536 * c : 1536 * c + 1024].rearrange("p (r i) -> p r i", r=8) for c in range(2)}
-        root_b = arena[:, 3072:].rearrange("p (r i) -> p r i", r=8)
-        root_last = {0: arena[:, 1024:1536].rearrange("p (t i) -> p t i", t=4)}
-        for c in (1, 2):
-            root_last[c] = sb([P, 4, 128], F32, f"root_last{c}")[:]
-        den[LAST, 0] = lslots[:, :, 3]
-        den[LAST, HALF] = arena[:, 512:1536].rearrange("p (t i) -> p t i", t=4)
-        for c in (2, 3):
-            for b in range(LAST):
-                rec[b, c] = slots[:, 4 * b : 4 * b + 4, 1, 128 * c : 128 * (c + 1)]
-        root_last[3] = chunk(den, LAST, 3)
+        root0 = sb([P, 4, PAIRS], F32, "root0", "raw21")
+        arena = sb([P, 3072], F32, "arena", "raw20")
+        def view(lo, n):
+            return arena[:, lo : lo + 4 * n].rearrange("p (t i) -> p t i", t=4)
+        den[LAST, HALF] = view(1024, HALF)
+        for b in range(LAST):
+            for c in range(4):
+                rec[b, c] = chunk(den, b, c)
+        root10 = sb([P, 4, 128], F32, "root10")[:]
+        root11 = view(1024, 128)
+        root20 = view(1536, 128)
+        root1b = view(2048, HALF)
+        rootc = {c: sb([P, 4, 128], F32, f"rootc{c}")[:] for c in (1, 2)}
         def pair_tile(c, tag):
             both = sb([P, 1024], BF16, f"zpair{c}", tag)
             for b in range(LAST):
                 z4[b, c] = both[:, 512 * b : 512 * (b + 1)]
-        def sums_early(c):
-            return slots[:, :, 1, 128 * c : 128 * (c + 1)]
-        def square_early(c):
-            square(sums_early(c), root_a[c])
-            for b in range(LAST):
-                rec[b, c] = sums_early(c)[:, 4 * b : 4 * b + 4]
-        def square_one(b, c):
-            rec[b, c] = sums_early(c)[:, 4 * b : 4 * b + 4]
-            square(rec[b, c], root_a[c][:, 4 * b : 4 * b + 4])
-        def invert_last(c):
-            invert(root_last[c], chunk(den, LAST, c))
-        def square_last(c):
-            square(chunk(den, LAST, c), root_last[c])
-            rec[LAST, c] = chunk(den, LAST, c)
-        def early_weaves(c):
-            for b in range(LAST):
-                weave(b, c)
-            for b in range(LAST):
-                multiply(b, c)
-        def both_vmax(r):
-            t = r - 8
-            x, out = lslots[:, t, 0:2], lslots[:, t, 0:3:2]
-            if r == 11:
-                nc.scalar.activation(out=out, in_=x, func=ACT.Copy, scale=vm[:, LAST, t : t + 1])
-            else:
-                nc.gpsimd.tensor_scalar(out=out, in0=x, scalar1=vm[:, LAST, t : t + 1], scalar2=0.0, op0=ALU.mult, op1=ALU.add)
-        invert(root_b[:, :4], slots[:, :4, 1, HALF:])
+        def last_vmax(r):
+            nc.scalar.activation(out=last_num[:, r - 8], in_=last_a[:, r - 8], func=ACT.Copy, scale=vm[:, LAST, r - 8 : r - 7])
+        def pick_whole(r):
+            nc.vector.tensor_copy(last_a[:, r - 8], h[r][:].indirect(pos1_t[:]))
+        for u in range(2):
+            invert(root0[:, :, HALF * u : HALF * (u + 1)], den[0, 0][:, :, HALF * u : HALF * (u + 1)])
+        square(den[0, 0][:, :, :HALF], root0[:, :, :HALF])
+        square(rec[0, 2], root0[:, :, 256:384])
+        gz = sb([P, 1024], BF16, "gz", "h7")
         for c in range(2):
-            invert(root_a[c][:, :4], sums_early(c)[:, :4])
-        square(slots[:, :4, 1, HALF:], root_b[:, :4])
+            z4[0, c] = gz[:, 512 * c : 512 * (c + 1)]
+            weave(0, c, None, nc.gpsimd)
         for r in range(8, 12):
             make_h(r, f"h{r - 8}" if r < 11 else None)
-            for lo in (0, HALF):
-                pick_a(r, lo, lo + HALF)
+            pick_whole(r)
+        square(rec[0, 3], root0[:, :, 384:])
+        first = sb([P, 1024], F32, "first")
+        early_codes = sb([P, HALF], U32, "early_codes")
+        den[LAST, 0] = first[:].rearrange("p (t i) -> p t i", t=4)
+        for c in range(4):
+            rec[LAST, c] = chunk(den, LAST, c)
+        for c in range(2):
+            zc[0, c] = early_codes[:, 128 * c : 128 * (c + 1)]
+        for r in range(8, 12):
             pick_sum(r, 0, HALF)
-            if r < 11:
-                both_vmax(r)
-            if r in (9, 10):
-                invert(root_a[r - 9][:, 4:], sums_early(r - 9)[:, 4:])
-            if r == 10:
-                invert(root_b[:, 4:], slots[:, 4:, 1, HALF:])
-        square_early(0)
-        square(slots[:, 4:, 1, HALF:], root_b[:, 4:])
-        invert_last(0)
-        both_vmax(11)
-        square_last(0)
-        invert_last(1)
-        square_early(1)
-        square_last(1)
-        weave(0, 0)
-        weave(1, 0)
+        invert(root10, rec[1, 0])
+        invert(root11, rec[1, 1])
+        square(rec[1, 0], root10)
+        square(rec[1, 1], root11)
+        for r in range(8, 12):
+            last_vmax(r)
+        invert(root20, rec[LAST, 0])
+        invert(rootc[1], rec[LAST, 1])
+        square(rec[LAST, 0], root20)
+        invert(root1b, den[1, 0][:, :, HALF:])
+        square(rec[LAST, 1], rootc[1])
+        square(den[1, 0][:, :, HALF:], root1b)
         multiply(0, 0)
-        pick_sum(8, HALF, PAIRS)
+        multiply(0, 1)
+        z4[1, 0] = arena[:, :256].bitcast(BF16)
+        weave(1, 0)
+        weave(1, 1)
         multiply(1, 0)
+        pick_sum(8, HALF, PAIRS)
         pick_sum(9, HALF, PAIRS)
         weave(LAST, 0)
         pick_sum(10, HALF, PAIRS)
         multiply(LAST, 0)
         pick_sum(11, HALF, PAIRS)
-        early_weaves(1)
-        pair_tile(2, "root_last1")
+        multiply(1, 1)
+        pair_tile(2, "rootc1")
         weave(LAST, 1)
         weave(0, 2)
         multiply(LAST, 1)
         weave(1, 2)
         multiply(0, 2)
         multiply(1, 2)
-        invert_last(2)
-        invert_last(3)
+        invert(rootc[2], rec[LAST, 2])
+        invert(rec[LAST, 3], rec[LAST, 3])
         for g in range(NG):
             empty(0, g, ("h4", "h5")[g])
-        round_bank(0, 0, nc.scalar.copy, "h6")
-        round_bank(0, 1, nc.scalar.copy, "h7")
+        square(rec[LAST, 2], rootc[2])
+        for g in range(NG):
+            round_rows(0, g, ("h6", "half11")[g])
+        pair_tile(3, "rootc2")
+        weave(LAST, 2)
         store_codes(0)
-        square_last(2)
-        pair_tile(3, "root_last2")
-        weave(LAST, 2, None, late[:, :, :128])
         weave(0, 3)
         multiply(LAST, 2)
         weave(1, 3)
@@ -425,16 +422,16 @@ def tile_list_inhibited_enzyme_flux_kernel(
         multiply(1, 3)
         empty(1, 0, "half00")
         empty(1, 1, "half01")
-        square_last(3)
+        square(rec[LAST, 3], rec[LAST, 3])
         round_bank(1, 0, nc.scalar.copy, "w1g00")
-        weave(LAST, 3, None, late[:, :, 128:])
-        round_bank(1, 1, nc.scalar.copy, "w1g21")
+        weave(LAST, 3)
+        round_rows(1, 1, "raw10")
         multiply(LAST, 3)
         store_codes(1)
         for g in range(NG):
             empty(2, g, ("h0", "h1")[g])
         round_bank(2, 0, nc.scalar.copy, "mid")
-        round_bank(2, 1, nc.scalar.copy, "tabs")
+        round_rows(2, 1, "tabs")
         store_codes(2)
         for g, copy in enumerate((nc.scalar.copy, nc.vector.tensor_copy)):
             empty(3, g, f"gw0{g}", copy)

@@ -22,7 +22,7 @@ HB = H // 512
 NG = N // 512
 LAST = HB - 1
 HALF = PAIRS // 2
-PLACED = {"raw21": 0, "root0": 0, "first": 0, "early_codes": 4}
+PLACED = {"h4": 0, "root01": 0, "first": 1, "early_codes": 0, "h3": 12, "num0": 6, "w1g21": 14, "h7": 20, "num1": 15, "z400": 23}
 CHUNKS = ((0, 128), (128, 256), (256, 384), (384, 512))
 
 
@@ -104,11 +104,27 @@ def tile_list_inhibited_enzyme_flux_kernel(
             if b == 0:
                 nc.sync.dma_start(pos1_t[:], pos1)
                 nc.sync.dma_start(pos2_t[:], pos2)
-        load_w1(1, 0)
+        dens = sb([P, 8 * PAIRS], F32, "dens")
+        half = {}
+
+        def load_half(b, a, x, spot=None):
+            if spot is None:
+                half[b, a, x] = sb([P, 4, 256], F32, f"half{b}{a}{x}")[:]
+            elif b == LAST:
+                half[b, a, x] = dens[:, 4 * PAIRS :].rearrange("p (j x c) -> p x j c", j=4, x=2)[:, x]
+            else:
+                half[b, a, x] = dens[:, 1024 * spot : 1024 * (spot + 1)].rearrange("p (j c) -> p j c", j=4)
+            c0 = 512 * b + 256 * x
+            nc.sync.dma_start(out=half[b, a, x], in_=w1[512 * a : 512 * (a + 1), c0 : c0 + 256].rearrange("(p j) c -> p j c", j=4))
+
+        load_half(1, 0, 0)
+        load_half(1, 0, 1, 0)
         nc.sync.dma_start(out=vm[:], in_=vmax.rearrange("(b p t) -> p b t", p=P, t=4))
-        mid_half = load_halves(1)
-        for a in range(KA):
-            load_w1(LAST, a)
+        load_half(1, 1, 0)
+        load_half(1, 1, 1, 1)
+        load_w1(LAST, 0)
+        load_half(LAST, 1, 0, 2)
+        load_half(LAST, 1, 1, 3)
 
         def gather_words(a):
             for f in range(2):
@@ -121,6 +137,14 @@ def tile_list_inhibited_enzyme_flux_kernel(
                 rounded[b, a] = sb([P, 2048], BF16, f"w1g{b}{a}", tag)[:]
             out = rounded[b, a].rearrange("p (t m j) -> p m j t", t=4, j=4)[:, ms]
             copy(out=out, in_=w1raw[b, a][:].rearrange("p j (m t) -> p m j t", t=4)[:, ms])
+
+        def round_half(out, b, a, x, on_gpsimd=False):
+            dst = out.rearrange("p (t m j) -> p m t j", t=4, j=4)[:, 64 * x : 64 * (x + 1)]
+            src = half[b, a, x].rearrange("p j (m t) -> p m t j", t=4)
+            if on_gpsimd:
+                nc.gpsimd.tensor_scalar(out=dst, in0=src, scalar1=1.0, scalar2=0.0, op0=ALU.mult, op1=ALU.add)
+            else:
+                nc.scalar.copy(out=dst.rearrange("p m t j -> p m j t"), in_=src.rearrange("p m t j -> p m j t"))
 
         def quantise_block(b, a):
             nc.vector.quantize_mx(out=w1c[b, a].bitcast(FP8X4), scales=w1s[b, a], in_=rounded[b, a])
@@ -165,14 +189,11 @@ def tile_list_inhibited_enzyme_flux_kernel(
                     nc.sync.dma_start(out=w2s[b][32 * q : 32 * q + 4, :].bitcast(I32), in_=w2sdealt[row : row + 8 : 2, :].bitcast(I32))
 
         h = {}
-        work = sb([P, 8 * 1024], F32, "work", "tabw")
-        slots = work[:].rearrange("p (r x i) -> p r x i", x=2, i=PAIRS)
-        sub = {(b, 0): slots[:, 4 * b : 4 * b + 4, 0] for b in range(LAST)}
-        den = {(b, 0): slots[:, 4 * b : 4 * b + 4, 1] for b in range(LAST)}
+        subs = sb([P, 8, PAIRS], F32, "subs", "tabw")
+        sub = {(b, 0): subs[:, 4 * b : 4 * b + 4] for b in range(LAST)}
+        den = {(b, 0): dens[:].rearrange("p (r i) -> p r i", r=8)[:, 4 * b : 4 * b + 4] for b in range(LAST)}
+        num = {}
         rec = {}
-
-        def slot(r):
-            return work[:, 1024 * r : 1024 * (r + 1)].bitcast(BF16)
 
         last_a = sb([P, 4, PAIRS], F32, "last_a")
         last_num = sb([P, 4, PAIRS], F32, "last_num")
@@ -240,7 +261,7 @@ def tile_list_inhibited_enzyme_flux_kernel(
         def weave(b, c, tag=None, eng=nc.vector):
             if (b, c) not in z4:
                 z4[b, c] = sb([P, 512], BF16, f"z4{b}{c}", tag)[:]
-            x = chunk(sub, b, c) if b < LAST else last_num[:, :, 128 * c : 128 * (c + 1)]
+            x = (num[b] if b < LAST else last_num)[:, :, 128 * c : 128 * (c + 1)]
             x, y = [v.rearrange("p t (c i) -> p c t i", i=4) for v in (x, rec[b, c])]
             eng.tensor_tensor(out=z4[b, c].rearrange("p (c i t) -> p c t i", i=4, t=4), in0=x, in1=y, op=ALU.mult)
 
@@ -284,15 +305,16 @@ def tile_list_inhibited_enzyme_flux_kernel(
 
         def round_rows(c, g, tag=None):
             lo, hi = CHUNKS[c]
-            y4[c, g] = sb([P, 4 * (hi - lo)], BF16, f"y4{c}{g}", tag)
+            if (c, g) not in y4:
+                y4[c, g] = sb([P, 4 * (hi - lo)], BF16, f"y4{c}{g}", tag)[:]
             nc.vector.tensor_copy(
-                out=y4[c, g][:].rearrange("p (x i t) -> p x t i", i=4, t=4),
+                out=y4[c, g].rearrange("p (x i t) -> p x t i", i=4, t=4),
                 in_=y[c, g][:].rearrange("p t (x i) -> p x t i", i=4),
             )
 
         def round_bank(c, g, copy, tag=None):
-            y4[c, g] = sb([P, 512], BF16, f"y4{c}{g}", tag)
-            copy(out=y4[c, g][:].rearrange("p (i t) -> p i t", t=4), in_=out_bank(c, g, 0)[0][:].rearrange("p (t i) -> p i t", t=4))
+            y4[c, g] = sb([P, 512], BF16, f"y4{c}{g}", tag)[:]
+            copy(out=y4[c, g].rearrange("p (i t) -> p i t", t=4), in_=out_bank(c, g, 0)[0][:].rearrange("p (t i) -> p i t", t=4))
 
         ycodes = sb([P, NG * PAIRS], U32, "ycodes")
 
@@ -300,38 +322,45 @@ def tile_list_inhibited_enzyme_flux_kernel(
             lo, hi = CHUNKS[c]
             for g in range(NG):
                 cols = slice(PAIRS * g + lo, PAIRS * g + hi)
-                nc.vector.quantize_mx(out=ycodes[:, cols].bitcast(FP8X4), scales=yscales[:, cols], in_=y4[c, g][:])
+                nc.vector.quantize_mx(out=ycodes[:, cols].bitcast(FP8X4), scales=yscales[:, cols], in_=y4[c, g])
             nc.sync.dma_start(out=out_words[:, :, lo:hi], in_=ycodes[:].bitcast(I32).rearrange("p (g m) -> p g m", g=NG)[:, :, lo:hi])
 
         move_scales()
         for b in range(HB):
             deal_words(b)
-        for r in range(3):
-            make_h(r)
-        whole(0)
+        def run_a(b):
+            for r in range(4 * b, 4 * b + 4):
+                make_h(r)
+                pick_a(r, 0, PAIRS)
+        def run_vmax(b, tag):
+            num[b] = sb([P, 4, PAIRS], F32, f"num{b}", tag)
+            for r in range(4 * b, 4 * b + 4):
+                times_vmax(r, 0, PAIRS, num[b][:, r % 4])
+        run_a(0)
         mid = sb([P, KA * 2048], BF16, "mid")
-        rounded[1, 0] = mid[:, :2048]
-        round_block(1, 0)
-        whole(1)
+        round_half(mid[:, :2048], 1, 0, 0, True)
+        round_half(mid[:, :2048], 1, 0, 1)
+        pick_sum(0, 0, PAIRS)
+        pick_sum(1, 0, PAIRS)
         for x in range(2):
-            nc.scalar.copy(out=mid[:, 2048:].rearrange("p (t m j) -> p m j t", t=4, j=4)[:, 64 * x : 64 * (x + 1)], in_=mid_half[x][:].rearrange("p j (m t) -> p m j t", t=4))
-        make_h(3, "half10")
-        whole(2)
+            round_half(mid[:, 2048:], 1, 1, x)
         nc.vector.quantize_mx(out=mid_codes[:].bitcast(FP8X4), scales=mid_scales[:], in_=mid[:])
+        pick_sum(2, 0, PAIRS)
+        pick_sum(3, 0, PAIRS)
         round_block(2, 0, "w1g00")
-        make_h(4)
-        whole(3)
         quantise_block(2, 0)
-        make_h(5)
-        whole(4)
-        make_h(6)
-        whole(5)
-        round_block(2, 1)
-        make_h(7)
-        whole(6)
+        run_vmax(0, None)
+        run_a(1)
+        rounded[2, 1] = sb([P, 2048], BF16, "w1g21")[:]
+        round_half(rounded[2, 1], LAST, 1, 1)
+        round_half(rounded[2, 1], LAST, 1, 0, True)
         quantise_block(2, 1)
-        whole(7)
-        root0 = sb([P, 4, PAIRS], F32, "root0", "raw21")
+        for r in range(4, 8):
+            pick_sum(r, 0, PAIRS)
+        run_vmax(1, None)
+        root00 = subs[:, 3].rearrange("p (t i) -> p t i", t=4)
+        root0b = subs[:, 1:3].rearrange("p r (u i) -> p (r u) i", u=2)
+        root01 = sb([P, 4, 128], F32, "root01")
         arena = sb([P, 3072], F32, "arena", "raw20")
         def view(lo, n):
             return arena[:, lo : lo + 4 * n].rearrange("p (t i) -> p t i", t=4)
@@ -340,10 +369,10 @@ def tile_list_inhibited_enzyme_flux_kernel(
             for c in range(4):
                 rec[b, c] = chunk(den, b, c)
         root10 = sb([P, 4, 128], F32, "root10")[:]
-        root11 = view(1024, 128)
-        root20 = view(1536, 128)
+        root11 = view(256, 128)
+        root20 = den[LAST, HALF][:, :, :128]
         root1b = view(2048, HALF)
-        rootc = {c: sb([P, 4, 128], F32, f"rootc{c}")[:] for c in (1, 2)}
+        rootc = {c: sb([P, 4, 128], F32, f"rootc{c}")[:] for c in (1, 2, 3)}
         def pair_tile(c, tag):
             both = sb([P, 1024], BF16, f"zpair{c}", tag)
             for b in range(LAST):
@@ -352,25 +381,23 @@ def tile_list_inhibited_enzyme_flux_kernel(
             nc.scalar.activation(out=last_num[:, r - 8], in_=last_a[:, r - 8], func=ACT.Copy, scale=vm[:, LAST, r - 8 : r - 7])
         def pick_whole(r):
             nc.vector.tensor_copy(last_a[:, r - 8], h[r][:].indirect(pos1_t[:]))
-        for u in range(2):
-            invert(root0[:, :, HALF * u : HALF * (u + 1)], den[0, 0][:, :, HALF * u : HALF * (u + 1)])
-        square(den[0, 0][:, :, :HALF], root0[:, :, :HALF])
-        square(rec[0, 2], root0[:, :, 256:384])
-        gz = sb([P, 1024], BF16, "gz", "h7")
-        for c in range(2):
-            z4[0, c] = gz[:, 512 * c : 512 * (c + 1)]
-            weave(0, c, None, nc.gpsimd)
+        invert(root00, rec[0, 0])
+        invert(root0b, den[0, 0][:, :, HALF:])
+        square(rec[0, 0], root00)
+        invert(root01[:], rec[0, 1])
+        square(den[0, 0][:, :, HALF:], root0b)
+        z4[0, 0] = sb([P, 512], BF16, "z400")[:]
+        weave(0, 0, None, nc.gpsimd)
         for r in range(8, 12):
             make_h(r, f"h{r - 8}" if r < 11 else None)
             pick_whole(r)
-        square(rec[0, 3], root0[:, :, 384:])
+        square(rec[0, 1], root01[:])
         first = sb([P, 1024], F32, "first")
-        early_codes = sb([P, HALF], U32, "early_codes")
+        early_codes = sb([P, 128], U32, "early_codes")
         den[LAST, 0] = first[:].rearrange("p (t i) -> p t i", t=4)
         for c in range(4):
             rec[LAST, c] = chunk(den, LAST, c)
-        for c in range(2):
-            zc[0, c] = early_codes[:, 128 * c : 128 * (c + 1)]
+        zc[0, 0] = early_codes[:]
         for r in range(8, 12):
             pick_sum(r, 0, HALF)
         invert(root10, rec[1, 0])
@@ -386,18 +413,18 @@ def tile_list_inhibited_enzyme_flux_kernel(
         square(rec[LAST, 1], rootc[1])
         square(den[1, 0][:, :, HALF:], root1b)
         multiply(0, 0)
-        multiply(0, 1)
+        weave(0, 1)
         z4[1, 0] = arena[:, :256].bitcast(BF16)
         weave(1, 0)
+        multiply(0, 1)
         weave(1, 1)
         multiply(1, 0)
-        pick_sum(8, HALF, PAIRS)
-        pick_sum(9, HALF, PAIRS)
-        weave(LAST, 0)
-        pick_sum(10, HALF, PAIRS)
-        multiply(LAST, 0)
-        pick_sum(11, HALF, PAIRS)
         multiply(1, 1)
+        weave(LAST, 0)
+        pick_sum(8, HALF, PAIRS)
+        multiply(LAST, 0)
+        for r in range(9, 12):
+            pick_sum(r, HALF, PAIRS)
         pair_tile(2, "rootc1")
         weave(LAST, 1)
         weave(0, 2)
@@ -405,33 +432,36 @@ def tile_list_inhibited_enzyme_flux_kernel(
         weave(1, 2)
         multiply(0, 2)
         multiply(1, 2)
-        invert(rootc[2], rec[LAST, 2])
-        invert(rec[LAST, 3], rec[LAST, 3])
         for g in range(NG):
-            empty(0, g, ("h4", "h5")[g])
+            empty(0, g, ("h5", "half100")[g])
+        invert(rootc[2], rec[LAST, 2])
+        invert(rootc[3], rec[LAST, 3])
         square(rec[LAST, 2], rootc[2])
         for g in range(NG):
-            round_rows(0, g, ("h6", "half11")[g])
+            round_bank(0, g, nc.scalar.copy, ("h6", "half110")[g])
         pair_tile(3, "rootc2")
         weave(LAST, 2)
-        store_codes(0)
         weave(0, 3)
         multiply(LAST, 2)
         weave(1, 3)
         multiply(0, 3)
-        multiply(1, 3)
         empty(1, 0, "half00")
+        square(rec[LAST, 3], rootc[3])
         empty(1, 1, "half01")
-        square(rec[LAST, 3], rec[LAST, 3])
-        round_bank(1, 0, nc.scalar.copy, "w1g00")
+        multiply(1, 3)
+        store_codes(0)
         weave(LAST, 3)
-        round_rows(1, 1, "raw10")
+        held = sb([P, 2 * 512], BF16, "held", "rootc3")
+        for k in range(2):
+            y4[1, k] = held[:, 512 * k : 512 * (k + 1)]
+        round_rows(1, 0)
         multiply(LAST, 3)
-        store_codes(1)
+        round_rows(1, 1)
         for g in range(NG):
             empty(2, g, ("h0", "h1")[g])
         round_bank(2, 0, nc.scalar.copy, "mid")
-        round_rows(2, 1, "tabs")
+        round_bank(2, 1, nc.scalar.copy, "tabs")
+        store_codes(1)
         store_codes(2)
         for g, copy in enumerate((nc.scalar.copy, nc.vector.tensor_copy)):
             empty(3, g, f"gw0{g}", copy)

@@ -22,7 +22,7 @@ HB = H // 512
 NG = N // 512
 LAST = HB - 1
 HALF = PAIRS // 2
-PLACED = {"h4": 0, "root01": 0, "first": 1, "early_codes": 0, "h3": 12, "num0": 6, "w1g21": 14, "h7": 20, "num1": 15, "z400": 23}
+PLACED = {"h4": 0, "root03": 0, "first": 1, "early_codes": 0, "h3": 12, "num1": 6, "w1g21": 14}
 CHUNKS = ((0, 128), (128, 256), (256, 384), (384, 512))
 
 
@@ -110,6 +110,8 @@ def tile_list_inhibited_enzyme_flux_kernel(
         def load_half(b, a, x, spot=None):
             if spot is None:
                 half[b, a, x] = sb([P, 4, 256], F32, f"half{b}{a}{x}")[:]
+            elif not isinstance(spot, int):
+                half[b, a, x] = spot
             elif b == LAST:
                 half[b, a, x] = dens[:, 4 * PAIRS :].rearrange("p (j x c) -> p x j c", j=4, x=2)[:, x]
             else:
@@ -117,13 +119,14 @@ def tile_list_inhibited_enzyme_flux_kernel(
             c0 = 512 * b + 256 * x
             nc.sync.dma_start(out=half[b, a, x], in_=w1[512 * a : 512 * (a + 1), c0 : c0 + 256].rearrange("(p j) c -> p j c", j=4))
 
-        load_half(1, 0, 0)
+        num0 = sb([P, 4 * PAIRS + 768], F32, "num0")
+        load_half(1, 0, 0, num0[:, : 4 * PAIRS].rearrange("p (j x c) -> p x j c", j=4, x=2)[:, 0])
         load_half(1, 0, 1, 0)
         nc.sync.dma_start(out=vm[:], in_=vmax.rearrange("(b p t) -> p b t", p=P, t=4))
-        load_half(1, 1, 0)
+        load_half(1, 1, 0, num0[:, 7 * HALF :].rearrange("p (j c) -> p j c", j=4))
         load_half(1, 1, 1, 1)
         load_w1(LAST, 0)
-        load_half(LAST, 1, 0, 2)
+        load_half(LAST, 1, 0)
         load_half(LAST, 1, 1, 3)
 
         def gather_words(a):
@@ -328,17 +331,16 @@ def tile_list_inhibited_enzyme_flux_kernel(
         move_scales()
         for b in range(HB):
             deal_words(b)
-        def run_a(b):
+        def run_a(b, tag):
+            num[b] = sb([P, 4, PAIRS], F32, "num1")[:] if b else num0[:, : 4 * PAIRS].rearrange("p (t i) -> p t i", t=4)
             for r in range(4 * b, 4 * b + 4):
                 make_h(r)
                 pick_a(r, 0, PAIRS)
-        def run_vmax(b, tag):
-            num[b] = sb([P, 4, PAIRS], F32, f"num{b}", tag)
-            for r in range(4 * b, 4 * b + 4):
-                times_vmax(r, 0, PAIRS, num[b][:, r % 4])
-        run_a(0)
+                if r % 4 < 3:
+                    times_vmax(r, 0, PAIRS, num[b][:, r % 4])
         mid = sb([P, KA * 2048], BF16, "mid")
         round_half(mid[:, :2048], 1, 0, 0, True)
+        run_a(0, "half100")
         round_half(mid[:, :2048], 1, 0, 1)
         pick_sum(0, 0, PAIRS)
         pick_sum(1, 0, PAIRS)
@@ -347,20 +349,18 @@ def tile_list_inhibited_enzyme_flux_kernel(
         nc.vector.quantize_mx(out=mid_codes[:].bitcast(FP8X4), scales=mid_scales[:], in_=mid[:])
         pick_sum(2, 0, PAIRS)
         pick_sum(3, 0, PAIRS)
+        scalar_vmax(3, 0, PAIRS, num[0][:, 3])
         round_block(2, 0, "w1g00")
         quantise_block(2, 0)
-        run_vmax(0, None)
-        run_a(1)
         rounded[2, 1] = sb([P, 2048], BF16, "w1g21")[:]
-        round_half(rounded[2, 1], LAST, 1, 1)
         round_half(rounded[2, 1], LAST, 1, 0, True)
+        run_a(1, None)
+        round_half(rounded[2, 1], LAST, 1, 1)
         quantise_block(2, 1)
         for r in range(4, 8):
             pick_sum(r, 0, PAIRS)
-        run_vmax(1, None)
-        root00 = subs[:, 3].rearrange("p (t i) -> p t i", t=4)
-        root0b = subs[:, 1:3].rearrange("p r (u i) -> p (r u) i", u=2)
-        root01 = sb([P, 4, 128], F32, "root01")
+        root0a = sb([P, 4, 384], F32, "root0a", "half210")
+        root03 = sb([P, 4, 128], F32, "root03")
         arena = sb([P, 3072], F32, "arena", "raw20")
         def view(lo, n):
             return arena[:, lo : lo + 4 * n].rearrange("p (t i) -> p t i", t=4)
@@ -368,44 +368,46 @@ def tile_list_inhibited_enzyme_flux_kernel(
         for b in range(LAST):
             for c in range(4):
                 rec[b, c] = chunk(den, b, c)
-        root10 = sb([P, 4, 128], F32, "root10")[:]
-        root11 = view(256, 128)
-        root20 = den[LAST, HALF][:, :, :128]
+        root10 = view(256, HALF)
+        root20 = view(1280, 192)[:, :, :128]
         root1b = view(2048, HALF)
         rootc = {c: sb([P, 4, 128], F32, f"rootc{c}")[:] for c in (1, 2, 3)}
-        def pair_tile(c, tag):
-            both = sb([P, 1024], BF16, f"zpair{c}", tag)
-            for b in range(LAST):
-                z4[b, c] = both[:, 512 * b : 512 * (b + 1)]
+        def held_tile(units, tag):
+            both = sb([P, 512 * len(units)], BF16, f"zheld{tag}", tag)
+            for k, unit in enumerate(units):
+                z4[unit] = both[:, 512 * k : 512 * (k + 1)]
         def last_vmax(r):
             nc.scalar.activation(out=last_num[:, r - 8], in_=last_a[:, r - 8], func=ACT.Copy, scale=vm[:, LAST, r - 8 : r - 7])
         def pick_whole(r):
             nc.vector.tensor_copy(last_a[:, r - 8], h[r][:].indirect(pos1_t[:]))
-        invert(root00, rec[0, 0])
-        invert(root0b, den[0, 0][:, :, HALF:])
-        square(rec[0, 0], root00)
-        invert(root01[:], rec[0, 1])
-        square(den[0, 0][:, :, HALF:], root0b)
-        z4[0, 0] = sb([P, 512], BF16, "z400")[:]
-        weave(0, 0, None, nc.gpsimd)
+        invert(root0a[:], den[0, 0][:, :, :384])
+        scalar_vmax(7, 0, PAIRS, num[1][:, 3])
+        square(den[0, 0][:, :, :384], root0a[:])
+        invert(root03[:], rec[0, 3])
+        gz = sb([P, 1024], BF16, "gz", "h7")
+        for c in range(2):
+            z4[0, c] = gz[:, 512 * c : 512 * (c + 1)]
+            weave(0, c, None, nc.gpsimd)
         for r in range(8, 12):
             make_h(r, f"h{r - 8}" if r < 11 else None)
             pick_whole(r)
-        square(rec[0, 1], root01[:])
+            if r == 8:
+                nc.gpsimd.tensor_scalar(out=last_num[:, 0], in0=last_a[:, 0], scalar1=vm[:, LAST, 0:1], scalar2=0.0, op0=ALU.mult, op1=ALU.add)
+        square(rec[0, 3], root03[:])
         first = sb([P, 1024], F32, "first")
-        early_codes = sb([P, 128], U32, "early_codes")
+        early_codes = sb([P, HALF], U32, "early_codes")
         den[LAST, 0] = first[:].rearrange("p (t i) -> p t i", t=4)
         for c in range(4):
             rec[LAST, c] = chunk(den, LAST, c)
-        zc[0, 0] = early_codes[:]
+        for c in range(2):
+            zc[0, c] = early_codes[:, 128 * c : 128 * (c + 1)]
         for r in range(8, 12):
             pick_sum(r, 0, HALF)
-        invert(root10, rec[1, 0])
-        invert(root11, rec[1, 1])
-        square(rec[1, 0], root10)
-        square(rec[1, 1], root11)
-        for r in range(8, 12):
-            last_vmax(r)
+        invert(root10, den[1, 0][:, :, :HALF])
+        last_vmax(9)
+        square(den[1, 0][:, :, :HALF], root10)
+        last_vmax(10)
+        last_vmax(11)
         invert(root20, rec[LAST, 0])
         invert(rootc[1], rec[LAST, 1])
         square(rec[LAST, 0], root20)
@@ -413,55 +415,58 @@ def tile_list_inhibited_enzyme_flux_kernel(
         square(rec[LAST, 1], rootc[1])
         square(den[1, 0][:, :, HALF:], root1b)
         multiply(0, 0)
-        weave(0, 1)
-        z4[1, 0] = arena[:, :256].bitcast(BF16)
-        weave(1, 0)
         multiply(0, 1)
+        weave(1, 0)
         weave(1, 1)
         multiply(1, 0)
+        pick_sum(8, HALF, PAIRS)
         multiply(1, 1)
         weave(LAST, 0)
-        pick_sum(8, HALF, PAIRS)
+        pick_sum(9, HALF, PAIRS)
         multiply(LAST, 0)
-        for r in range(9, 12):
+        for r in range(10, 12):
             pick_sum(r, HALF, PAIRS)
-        pair_tile(2, "rootc1")
+        held_tile([(0, 2), (1, 2), (0, 3)], "rootc1")
         weave(LAST, 1)
         weave(0, 2)
         multiply(LAST, 1)
         weave(1, 2)
         multiply(0, 2)
+        weave(0, 3)
         multiply(1, 2)
         for g in range(NG):
-            empty(0, g, ("h5", "half100")[g])
+            empty(0, g, ("h5", "raw00")[g])
         invert(rootc[2], rec[LAST, 2])
         invert(rootc[3], rec[LAST, 3])
         square(rec[LAST, 2], rootc[2])
-        for g in range(NG):
-            round_bank(0, g, nc.scalar.copy, ("h6", "half110")[g])
-        pair_tile(3, "rootc2")
-        weave(LAST, 2)
-        weave(0, 3)
-        multiply(LAST, 2)
-        weave(1, 3)
+        held0 = sb([P, 1024], BF16, "held0", "h6")
+        for c in range(2):
+            y4[c, 0] = held0[:, 512 * c : 512 * (c + 1)]
+        nc.scalar.copy(out=y4[0, 0].rearrange("p (i t) -> p i t", t=4), in_=banks[0][:].rearrange("p (t i) -> p i t", t=4))
+        held_tile([(1, 3)], "rootc2")
         multiply(0, 3)
+        weave(LAST, 2)
+        weave(1, 3)
+        multiply(LAST, 2)
         empty(1, 0, "half00")
         square(rec[LAST, 3], rootc[3])
         empty(1, 1, "half01")
-        multiply(1, 3)
-        store_codes(0)
         weave(LAST, 3)
-        held = sb([P, 2 * 512], BF16, "held", "rootc3")
-        for k in range(2):
-            y4[1, k] = held[:, 512 * k : 512 * (k + 1)]
-        round_rows(1, 0)
+        multiply(1, 3)
+        held = sb([P, 1024], BF16, "held", "rootc3")
+        for c in range(2):
+            y4[c, 1] = held[:, 512 * c : 512 * (c + 1)]
+        round_rows(0, 1)
         multiply(LAST, 3)
         round_rows(1, 1)
+        round_rows(1, 0)
+        nc.vector.quantize_mx(out=ycodes[:, PAIRS : PAIRS + HALF].bitcast(FP8X4), scales=yscales[:, PAIRS : PAIRS + HALF], in_=held[:])
+        nc.vector.quantize_mx(out=ycodes[:, :HALF].bitcast(FP8X4), scales=yscales[:, :HALF], in_=held0[:])
+        nc.sync.dma_start(out=out_words[:, :, :HALF], in_=ycodes[:].bitcast(I32).rearrange("p (g m) -> p g m", g=NG)[:, :, :HALF])
         for g in range(NG):
             empty(2, g, ("h0", "h1")[g])
         round_bank(2, 0, nc.scalar.copy, "mid")
         round_bank(2, 1, nc.scalar.copy, "tabs")
-        store_codes(1)
         store_codes(2)
         for g, copy in enumerate((nc.scalar.copy, nc.vector.tensor_copy)):
             empty(3, g, f"gw0{g}", copy)

@@ -361,16 +361,16 @@ def tile_list_inhibited_enzyme_flux_kernel(
             pick_sum(r, 0, PAIRS)
         root0a = sb([P, 4, 384], F32, "root0a", "half210")
         root03 = sb([P, 4, 128], F32, "root03")
-        arena = sb([P, 3072], F32, "arena", "raw20")
+        arena = sb([P, 3328], F32, "arena", "raw20")
         def view(lo, n):
             return arena[:, lo : lo + 4 * n].rearrange("p (t i) -> p t i", t=4)
         den[LAST, HALF] = view(1024, HALF)
         for b in range(LAST):
             for c in range(4):
                 rec[b, c] = chunk(den, b, c)
-        root10 = view(256, HALF)
-        root20 = view(1280, 192)[:, :, :128]
-        root1b = view(2048, HALF)
+        root10 = view(768, HALF)
+        root20 = view(1792, 128)
+        root1b = arena[:, 2304:].rearrange("p (t i) -> p t i", t=4)
         rootc = {c: sb([P, 4, 128], F32, f"rootc{c}")[:] for c in (1, 2, 3)}
         def held_tile(units, tag):
             both = sb([P, 512 * len(units)], BF16, f"zheld{tag}", tag)
@@ -416,16 +416,16 @@ def tile_list_inhibited_enzyme_flux_kernel(
         square(den[1, 0][:, :, HALF:], root1b)
         multiply(0, 0)
         multiply(0, 1)
-        weave(1, 0)
-        weave(1, 1)
+        weave(1, 0, "half00")
+        weave(1, 1, "half01")
         multiply(1, 0)
         pick_sum(8, HALF, PAIRS)
         multiply(1, 1)
-        weave(LAST, 0)
         pick_sum(9, HALF, PAIRS)
+        pick_sum(10, HALF, PAIRS)
+        weave(LAST, 0)
+        pick_sum(11, HALF, PAIRS)
         multiply(LAST, 0)
-        for r in range(10, 12):
-            pick_sum(r, HALF, PAIRS)
         held_tile([(0, 2), (1, 2), (0, 3)], "rootc1")
         weave(LAST, 1)
         weave(0, 2)
@@ -434,34 +434,33 @@ def tile_list_inhibited_enzyme_flux_kernel(
         multiply(0, 2)
         weave(0, 3)
         multiply(1, 2)
-        for g in range(NG):
-            empty(0, g, ("h5", "raw00")[g])
         invert(rootc[2], rec[LAST, 2])
         invert(rootc[3], rec[LAST, 3])
+        empty(0, 0, "h5")
         square(rec[LAST, 2], rootc[2])
-        held0 = sb([P, 1024], BF16, "held0", "h6")
-        for c in range(2):
-            y4[c, 0] = held0[:, 512 * c : 512 * (c + 1)]
-        nc.scalar.copy(out=y4[0, 0].rearrange("p (i t) -> p i t", t=4), in_=banks[0][:].rearrange("p (t i) -> p i t", t=4))
+        empty(0, 1, "raw00")
         held_tile([(1, 3)], "rootc2")
         multiply(0, 3)
         weave(LAST, 2)
         weave(1, 3)
         multiply(LAST, 2)
-        empty(1, 0, "half00")
         square(rec[LAST, 3], rootc[3])
+        empty(1, 0, "half00")
         empty(1, 1, "half01")
         weave(LAST, 3)
         multiply(1, 3)
-        held = sb([P, 1024], BF16, "held", "rootc3")
+        both = sb([P, 2048], BF16, "held", "rootc3")
+        held0, held = both[:, :1024], both[:, 1024:]
         for c in range(2):
+            y4[c, 0] = held0[:, 512 * c : 512 * (c + 1)]
             y4[c, 1] = held[:, 512 * c : 512 * (c + 1)]
-        round_rows(0, 1)
+        round_rows(0, 0)
         multiply(LAST, 3)
-        round_rows(1, 1)
+        round_rows(0, 1)
         round_rows(1, 0)
-        nc.vector.quantize_mx(out=ycodes[:, PAIRS : PAIRS + HALF].bitcast(FP8X4), scales=yscales[:, PAIRS : PAIRS + HALF], in_=held[:])
-        nc.vector.quantize_mx(out=ycodes[:, :HALF].bitcast(FP8X4), scales=yscales[:, :HALF], in_=held0[:])
+        round_rows(1, 1)
+        nc.vector.quantize_mx(out=ycodes[:, PAIRS : PAIRS + HALF].bitcast(FP8X4), scales=yscales[:, PAIRS : PAIRS + HALF], in_=held)
+        nc.vector.quantize_mx(out=ycodes[:, :HALF].bitcast(FP8X4), scales=yscales[:, :HALF], in_=held0)
         nc.sync.dma_start(out=out_words[:, :, :HALF], in_=ycodes[:].bitcast(I32).rearrange("p (g m) -> p g m", g=NG)[:, :, :HALF])
         for g in range(NG):
             empty(2, g, ("h0", "h1")[g])

@@ -274,12 +274,20 @@ def tile_list_inhibited_enzyme_flux_kernel(
             at = (4 * g + t) * w
             return banks[first + at // 512], at % 512, w
 
-        def multiply(b, c, tag=None):
-            w = CHUNKS[c][1] - CHUNKS[c][0]
-            if (b, c) not in zc:
-                zc[b, c] = sb([P, w], U32, f"zc{b}{c}", tag)[:]
-            zs[b, c] = sb([P, w], U8, f"zs{b}{c}")
-            nc.vector.quantize_mx(out=zc[b, c].bitcast(FP8X4), scales=zs[b, c][:], in_=z4[b, c])
+        def multiply_two(b, woven, codes):
+            scales = sb([P, HALF], U8, f"zs{b}")
+            nc.vector.quantize_mx(out=codes[:].bitcast(FP8X4), scales=scales[:], in_=woven[:])
+            for c in range(2):
+                zc[b, c], zs[b, c] = codes[:, 128 * c : 128 * (c + 1)], scales[:, 128 * c : 128 * (c + 1)]
+                products(b, c)
+
+        def multiply(b, c):
+            zc[b, c] = sb([P, 128], U32, f"zc{b}{c}")[:]
+            zs[b, c] = sb([P, 128], U8, f"zs{b}{c}")[:]
+            nc.vector.quantize_mx(out=zc[b, c].bitcast(FP8X4), scales=zs[b, c], in_=z4[b, c])
+            products(b, c)
+
+        def products(b, c):
             for g in range(NG):
                 for t in range(4):
                     bank, at, w = out_bank(c, g, t)
@@ -289,7 +297,7 @@ def tile_list_inhibited_enzyme_flux_kernel(
                         lhsT=w2w[b][:, 2 * c0 : 2 * (c0 + P)].bitcast(FP4X4),
                         lhsT_scale=w2s[b][:, c0 : c0 + P],
                         rhs=zc[b, c].bitcast(FP8X4),
-                        rhs_scale=zs[b, c][:],
+                        rhs_scale=zs[b, c],
                         start=(b == 0 and at == 0),
                         stop=(b == LAST and at + w == 512),
                     )
@@ -385,9 +393,8 @@ def tile_list_inhibited_enzyme_flux_kernel(
         square(den[0, 0][:, :, :384], root0a[:])
         invert(root03[:], rec[0, 3])
         gz = sb([P, 1024], BF16, "gz", "h7")
-        for c in range(2):
-            z4[0, c] = gz[:, 512 * c : 512 * (c + 1)]
-            weave(0, c, None, nc.gpsimd)
+        x, r = [v[:, :, : 256].rearrange("p t (c i) -> p c t i", i=4) for v in (num[0], den[0, 0])]
+        nc.gpsimd.tensor_tensor(out=gz[:].rearrange("p (c i t) -> p c t i", i=4, t=4), in0=x, in1=r, op=ALU.mult)
         for r in range(8, 12):
             make_h(r, f"h{r - 8}" if r < 11 else None)
             pick_whole(r)
@@ -399,8 +406,6 @@ def tile_list_inhibited_enzyme_flux_kernel(
         den[LAST, 0] = first[:].rearrange("p (t i) -> p t i", t=4)
         for c in range(4):
             rec[LAST, c] = chunk(den, LAST, c)
-        for c in range(2):
-            zc[0, c] = early_codes[:, 128 * c : 128 * (c + 1)]
         for r in range(8, 12):
             pick_sum(r, 0, HALF)
         invert(root10, den[1, 0][:, :, :HALF])
@@ -414,13 +419,12 @@ def tile_list_inhibited_enzyme_flux_kernel(
         invert(root1b, den[1, 0][:, :, HALF:])
         square(rec[LAST, 1], rootc[1])
         square(den[1, 0][:, :, HALF:], root1b)
-        multiply(0, 0)
-        multiply(0, 1)
-        weave(1, 0, "half00")
-        weave(1, 1, "half01")
-        multiply(1, 0)
+        multiply_two(0, gz, early_codes)
+        vz = sb([P, 1024], BF16, "vz", "half00")
+        x, r = [v[:, :, :HALF].rearrange("p t (c i) -> p c t i", i=4) for v in (num[1], den[1, 0])]
+        nc.vector.tensor_tensor(out=vz[:].rearrange("p (c i t) -> p c t i", i=4, t=4), in0=x, in1=r, op=ALU.mult)
         pick_sum(8, HALF, PAIRS)
-        multiply(1, 1)
+        multiply_two(1, vz, sb([P, HALF], U32, "zc1"))
         pick_sum(9, HALF, PAIRS)
         pick_sum(10, HALF, PAIRS)
         weave(LAST, 0)

from contextlib import ExitStack

import concourse.mybir as mybir

K, T, S, PAIRS, H, N = 1024, 4096, 1024, 512, 1536, 1024
FLOPS = 2 * K * H * S + 2 * H * N * PAIRS

F32 = mybir.dt.float32
BF16 = mybir.dt.bfloat16
I32 = mybir.dt.int32
U32 = mybir.dt.uint32
U16 = mybir.dt.uint16
U8 = mybir.dt.uint8
FP8X4 = mybir.dt.float8_e4m3fn_x4
FP4X4 = mybir.dt.float4_e2m1fn_x4
ACT = mybir.ActivationFunctionType
ALU = mybir.AluOpType

P = 128
KA = K // 512
HB = H // 512
NG = N // 512
LAST = HB - 1
HALF = PAIRS // 2
PLACED = {"h4": 0, "root03": 0, "first": 1, "early_codes": 0, "h3": 12, "num1": 6, "w1g21": 14}
CHUNKS = ((0, 128), (128, 256), (256, 384), (384, 512))


def tile_list_inhibited_enzyme_flux_kernel(
    tc, tab_words, tab_scales, offs, pos1, pos2, w1, vmax, w2_words, w2_scales, out_0, out_1, out_2
):
    nc = tc.nc
    with ExitStack() as ctx:
        keep = ctx.enter_context(tc.tile_pool(name="keep", bufs=1))
        lay = ctx.enter_context(tc.tile_pool(name="lay", bufs=1))
        psum = ctx.enter_context(tc.psum_pool(name="psum", bufs=1))

        def sb(shape, dtype, name, tag=None):
            if name in PLACED:
                return lay.tile(shape, dtype, name=name, offset=1024 * PLACED[name], align_bytes=64)
            return keep.tile(shape, dtype, name=name, tag=tag or name, align_bytes=64)

        offs_t = keep.tile([P, S // 16], U16, name="offs_t")
        pos1_t = keep.tile([P, PAIRS // 16], U16, name="pos1_t")
        pos2_t = keep.tile([P, PAIRS // 16], U16, name="pos2_t")
        tab_all = sb([P, KA * T], U32, "tabw")
        tabw = [tab_all[:, T * a : T * (a + 1)] for a in range(KA)]
        tabs = sb([P, T], U8, "tabs")
        w2raw = [sb([P, 2 * N], U8, f"w2raw{b}") for b in range(HB)]
        w2sraw = sb([P, N], U8, "w2sraw")
        w2s = {b: sb([P, N], U8, f"w2s{b}") for b in range(HB)}
        w2sdealt = sb([P, N], U8, "w2sdealt")

        vm = sb([P, HB, 4], F32, "vm")
        w1c = {(b, a): sb([P, 512], U32, f"w1c{b}{a}")[:] for a in range(KA) for b in (0, LAST) if (b, a) != (0, 0)}
        w1s = {(b, a): sb([P, 512], U8, f"w1s{b}{a}")[:] for b in (0, LAST) for a in range(KA)}
        mid_codes = sb([P, KA * 512], U32, "mid_codes")
        mid_scales = sb([P, KA * 512], U8, "mid_scales")
        for a in range(KA):
            w1c[1, a] = mid_codes[:, 512 * a : 512 * (a + 1)]
            w1s[1, a] = mid_scales[:, 512 * a : 512 * (a + 1)]
        gw = [[sb([P, 512], U32, f"gw{a}{f}") for f in range(2)] for a in range(KA)]
        gs_all = sb([P, S], U8, "gs")
        gs = [gs_all[:, 512 * f : 512 * (f + 1)] for f in range(2)]
        banks = [psum.tile([P, 512], F32, name=f"bank{i}") for i in range(8)]
        yscales = sb([P, NG * PAIRS], U8, "yscales")
        warm = keep.tile([P, 2], F32, name="warm")

        nc.vector.memset(tabs[:].bitcast(I32), 0)
        nc.vector.memset(warm[:, 0:1], 1.0)
        nc.scalar.activation(out=warm[:, 1:2], in_=warm[:, 0:1], func=ACT.Abs_reciprocal_sqrt)
        nc.vector.memset(w2sraw[:].bitcast(I32), 0)
        for b in range(HB):
            nc.vector.memset(w2s[b][:].bitcast(I32), 0)

        w1raw = {}

        def load_w1(b, a):
            w1raw[b, a] = sb([P, 4, 512], F32, f"raw{b}{a}")
            rows = w1[512 * a : 512 * (a + 1), 512 * b : 512 * (b + 1)]
            nc.sync.dma_start(out=w1raw[b, a][:], in_=rows.rearrange("(p j) c -> p j c", j=4))

        def load_tab(a):
            nc.sync.dma_start(out=tabw[a].bitcast(I32), in_=tab_words[a].rearrange("p t i -> p (t i)").bitcast(I32))

        for q in range(4):
            nc.gpsimd.dma_start(out=tabs[32 * q : 32 * q + 4 * KA, :].bitcast(I32), in_=tab_scales[:, 4 * q : 4 * q + 4, :].bitcast(I32))
        nc.gpsimd.dma_start(out=w2sraw[0:96:2, :].bitcast(I32), in_=w2_scales.rearrange("b q c -> (b q) c").bitcast(I32))
        load_tab(0)
        nc.sync.dma_start(offs_t[:], offs)
        load_w1(0, 0)
        load_tab(1)
        def load_halves(b):
            halves = []
            for x in range(2):
                halves.append(sb([P, 4, 256], F32, f"half{b}{x}"))
                c0 = 512 * b + 256 * x
                nc.sync.dma_start(out=halves[x][:], in_=w1[512:1024, c0 : c0 + 256].rearrange("(p j) c -> p j c", j=4))
            return halves

        w1half = load_halves(0)
        for b in range(HB):
            nc.sync.dma_start(out=w2raw[b][:].bitcast(I32), in_=w2_words[b].bitcast(I32))
            if b == 0:
                nc.sync.dma_start(pos1_t[:], pos1)
                nc.sync.dma_start(pos2_t[:], pos2)
        dens = sb([P, 8 * PAIRS], F32, "dens")
        half = {}

        def load_half(b, a, x, spot=None):
            if spot is None:
                half[b, a, x] = sb([P, 4, 256], F32, f"half{b}{a}{x}")[:]
            elif not isinstance(spot, int):
                half[b, a, x] = spot
            elif b == LAST:
                half[b, a, x] = dens[:, 4 * PAIRS :].rearrange("p (j x c) -> p x j c", j=4, x=2)[:, x]
            else:
                half[b, a, x] = dens[:, 1024 * spot : 1024 * (spot + 1)].rearrange("p (j c) -> p j c", j=4)
            c0 = 512 * b + 256 * x
            nc.sync.dma_start(out=half[b, a, x], in_=w1[512 * a : 512 * (a + 1), c0 : c0 + 256].rearrange("(p j) c -> p j c", j=4))

        num0 = sb([P, 4 * PAIRS + 768], F32, "num0")
        load_half(1, 0, 0, num0[:, : 4 * PAIRS].rearrange("p (j x c) -> p x j c", j=4, x=2)[:, 0])
        load_half(1, 0, 1, 0)
        nc.sync.dma_start(out=vm[:], in_=vmax.rearrange("(b p t) -> p b t", p=P, t=4))
        load_half(1, 1, 0, num0[:, 7 * HALF :].rearrange("p (j c) -> p j c", j=4))
        load_half(1, 1, 1, 1)
        load_w1(LAST, 0)
        load_half(LAST, 1, 0)
        load_half(LAST, 1, 1, 3)

        def gather_words(a):
            for f in range(2):
                nc.vector.tensor_copy(gw[a][f][:], tabw[a].indirect(offs_t[:, 32 * f : 32 * (f + 1)]))

        rounded = {}

        def round_block(b, a, tag=None, ms=slice(0, P), copy=nc.scalar.copy):
            if (b, a) not in rounded:
                rounded[b, a] = sb([P, 2048], BF16, f"w1g{b}{a}", tag)[:]
            out = rounded[b, a].rearrange("p (t m j) -> p m j t", t=4, j=4)[:, ms]
            copy(out=out, in_=w1raw[b, a][:].rearrange("p j (m t) -> p m j t", t=4)[:, ms])

        def round_half(out, b, a, x, on_gpsimd=False):
            dst = out.rearrange("p (t m j) -> p m t j", t=4, j=4)[:, 64 * x : 64 * (x + 1)]
            src = half[b, a, x].rearrange("p j (m t) -> p m t j", t=4)
            if on_gpsimd:
                nc.gpsimd.tensor_scalar(out=dst, in0=src, scalar1=1.0, scalar2=0.0, op0=ALU.mult, op1=ALU.add)
            else:
                nc.scalar.copy(out=dst.rearrange("p m t j -> p m j t"), in_=src.rearrange("p m t j -> p m j t"))

        def quantise_block(b, a):
            nc.vector.quantize_mx(out=w1c[b, a].bitcast(FP8X4), scales=w1s[b, a], in_=rounded[b, a])

        def round_pair(copy, out, u, x):
            dst = out[:].rearrange("p (t m j) -> p m j t", t=2, j=4)[:, 64 * x : 64 * (x + 1)]
            copy(out=dst, in_=w1half[x][:].rearrange("p j (m u t) -> p u m j t", u=2, t=2)[:, u])

        gather_words(0)
        nc.vector.tensor_copy(gs_all[:], tabs[:].indirect(offs_t[:]))
        nc.vector.tensor_copy(
            out=w2sdealt[:].rearrange("p (g t m) -> p g t m", t=4, m=P),
            in_=w2sraw[:].rearrange("p (g m t) -> p g t m", t=4, m=P),
        )
        w1c[0, 0] = sb([P, 512], U32, "w1c00", "tabs")[:]
        round_block(0, 0)
        quantise_block(0, 0)
        gather_words(1)
        pairs = []
        for u in range(2):
            pairs.append(sb([P, 1024], BF16, f"w1pair{u}"))
            round_pair(nc.scalar.copy, pairs[u], u, 0)
        for u, copy in enumerate((nc.vector.tensor_copy, nc.scalar.copy)):
            round_pair(copy, pairs[u], u, 1)
        for u in range(2):
            cols = slice(256 * u, 256 * (u + 1))
            nc.vector.quantize_mx(out=w1c[0, 1][:, cols].bitcast(FP8X4), scales=w1s[0, 1][:, cols], in_=pairs[u][:])

        w2w = []

        def deal_words(b):
            w2w.append(sb([P, 2 * N], U8, f"w2w{b}", f"w1pair{b}"))
            nc.vector.tensor_copy(
                out=w2w[b][:].bitcast(U16).rearrange("p (g t m) -> p g t m", t=4, m=P),
                in_=w2raw[b][:].bitcast(U16).rearrange("p (g m t) -> p g t m", t=4, m=P),
            )

        def move_scales():
            for b in range(HB):
                for q in range(4):
                    row = 2 * (16 * b + 4 * q)
                    nc.sync.dma_start(out=w2s[b][32 * q : 32 * q + 4, :].bitcast(I32), in_=w2sdealt[row : row + 8 : 2, :].bitcast(I32))

        h = {}
        subs = sb([P, 8, PAIRS], F32, "subs", "tabw")
        sub = {(b, 0): subs[:, 4 * b : 4 * b + 4] for b in range(LAST)}
        den = {(b, 0): dens[:].rearrange("p (r i) -> p r i", r=8)[:, 4 * b : 4 * b + 4] for b in range(LAST)}
        num = {}
        rec = {}

        last_a = sb([P, 4, PAIRS], F32, "last_a")
        last_num = sb([P, 4, PAIRS], F32, "last_num")
        sub[LAST, 0], sub[LAST, HALF] = last_a[:, :, :HALF], last_a[:, :, HALF:]

        def part(d, r, lo, hi):
            b, t = divmod(r, 4)
            base = HALF if (b == LAST and lo >= HALF) else 0
            return d[b, base][:, t, lo - base : hi - base]

        def chunk(d, b, c):
            base = HALF if (b == LAST and c >= 2) else 0
            return d[b, base][:, :, 128 * c - base : 128 * (c + 1) - base]

        def make_h(r, tag=None):
            b, t = divmod(r, 4)
            h[r] = sb([P, S], F32, f"h{r}", tag)
            cols = slice(P * t, P * (t + 1))
            for f in range(2):
                acc = banks[(2 * r + f) % 8]
                for a in range(KA):
                    nc.tensor.matmul_mx(
                        out=acc[:],
                        lhsT=w1c[b, a][:, cols].bitcast(FP8X4),
                        lhsT_scale=w1s[b, a][:, cols],
                        rhs=gw[a][f][:].bitcast(FP8X4),
                        rhs_scale=gs[f][4 * a : P, :],
                        start=(a == 0),
                        stop=(a == KA - 1),
                    )
                nc.scalar.activation(out=h[r][:, 512 * f : 512 * (f + 1)], in_=acc[:], func=ACT.Relu)

        def pick_a(r, lo, hi):
            nc.vector.tensor_copy(part(sub, r, lo, hi), h[r][:].indirect(pos1_t[:, lo // 16 : hi // 16]))

        def pick_sum(r, lo, hi):
            nc.vector.tensor_tensor(part(den, r, lo, hi), h[r][:].indirect(pos2_t[:, lo // 16 : hi // 16]), part(sub, r, lo, hi), ALU.add)

        def times_vmax(r, lo, hi, out=None):
            x = part(sub, r, lo, hi)
            nc.gpsimd.tensor_scalar(out=x if out is None else out, in0=x, scalar1=vm[:, r // 4, r % 4 : r % 4 + 1], scalar2=0.0, op0=ALU.mult, op1=ALU.add)

        def scalar_vmax(r, lo, hi, out=None):
            x = part(sub, r, lo, hi)
            nc.scalar.activation(out=x if out is None else out, in_=x, func=ACT.Copy, scale=vm[:, r // 4, r % 4 : r % 4 + 1])

        def picks(r, lo, hi):
            mid = (lo + hi) // 2
            for pick in (pick_a, pick_sum):
                pick(r, lo, mid)
                pick(r, mid, hi)

        def whole(r):
            picks(r, 0, PAIRS)
            times_vmax(r, 0, PAIRS)

        def invert(out, x):
            nc.scalar.activation(out=out, in_=x, func=ACT.Abs_reciprocal_sqrt, bias=1.0)

        def square(out, x):
            nc.scalar.activation(out=out, in_=x, func=ACT.Square)

        z4, zc, zs = {}, {}, {}

        def weave(b, c, tag=None, eng=nc.vector):
            if (b, c) not in z4:
                z4[b, c] = sb([P, 512], BF16, f"z4{b}{c}", tag)[:]
            x = (num[b] if b < LAST else last_num)[:, :, 128 * c : 128 * (c + 1)]
            x, y = [v.rearrange("p t (c i) -> p c t i", i=4) for v in (x, rec[b, c])]
            eng.tensor_tensor(out=z4[b, c].rearrange("p (c i t) -> p c t i", i=4, t=4), in0=x, in1=y, op=ALU.mult)

        def out_bank(c, g, t):
            w = CHUNKS[c][1] - CHUNKS[c][0]
            first = CHUNKS[c][0] * 8 // PAIRS
            at = (4 * g + t) * w
            return banks[first + at // 512], at % 512, w

        def multiply_two(b, woven, codes):
            scales = sb([P, HALF], U8, f"zs{b}")
            nc.vector.quantize_mx(out=codes[:].bitcast(FP8X4), scales=scales[:], in_=woven[:])
            for c in range(2):
                zc[b, c], zs[b, c] = codes[:, 128 * c : 128 * (c + 1)], scales[:, 128 * c : 128 * (c + 1)]
                products(b, c)

        def multiply(b, c):
            zc[b, c] = sb([P, 128], U32, f"zc{b}{c}")[:]
            zs[b, c] = sb([P, 128], U8, f"zs{b}{c}")[:]
            nc.vector.quantize_mx(out=zc[b, c].bitcast(FP8X4), scales=zs[b, c], in_=z4[b, c])
            products(b, c)

        def products(b, c):
            for g in range(NG):
                for t in range(4):
                    bank, at, w = out_bank(c, g, t)
                    c0 = 512 * g + P * t
                    nc.tensor.matmul_mx(
                        out=bank[:, at : at + w],
                        lhsT=w2w[b][:, 2 * c0 : 2 * (c0 + P)].bitcast(FP4X4),
                        lhsT_scale=w2s[b][:, c0 : c0 + P],
                        rhs=zc[b, c].bitcast(FP8X4),
                        rhs_scale=zs[b, c],
                        start=(b == 0 and at == 0),
                        stop=(b == LAST and at + w == 512),
                    )

        out_rows = out_0.rearrange("(g p t) i -> g p t i", p=P, t=4)
        out_words = out_1.rearrange("g p m t -> p g (m t)").bitcast(I32)
        y, y4 = {}, {}

        def empty(c, g, tag=None, copy=nc.scalar.copy):
            lo, hi = CHUNKS[c]
            y[c, g] = sb([P, 4, hi - lo], F32, f"y{c}{g}", tag)
            step = 512 // (hi - lo)
            for t in range(0, 4, step):
                copy(out=y[c, g][:, t : t + step, :], in_=out_bank(c, g, t)[0][:].rearrange("p (t i) -> p t i", t=step))
            nc.sync.dma_start(out=out_rows[g, :, :, lo:hi], in_=y[c, g][:])

        def round_rows(c, g, tag=None):
            lo, hi = CHUNKS[c]
            if (c, g) not in y4:
                y4[c, g] = sb([P, 4 * (hi - lo)], BF16, f"y4{c}{g}", tag)[:]
            nc.vector.tensor_copy(
                out=y4[c, g].rearrange("p (x i t) -> p x t i", i=4, t=4),
                in_=y[c, g][:].rearrange("p t (x i) -> p x t i", i=4),
            )

        def round_bank(c, g, copy, tag=None):
            y4[c, g] = sb([P, 512], BF16, f"y4{c}{g}", tag)[:]
            copy(out=y4[c, g].rearrange("p (i t) -> p i t", t=4), in_=out_bank(c, g, 0)[0][:].rearrange("p (t i) -> p i t", t=4))

        ycodes = sb([P, NG * PAIRS], U32, "ycodes")

        def store_codes(c):
            lo, hi = CHUNKS[c]
            for g in range(NG):
                cols = slice(PAIRS * g + lo, PAIRS * g + hi)
                nc.vector.quantize_mx(out=ycodes[:, cols].bitcast(FP8X4), scales=yscales[:, cols], in_=y4[c, g])
            nc.sync.dma_start(out=out_words[:, :, lo:hi], in_=ycodes[:].bitcast(I32).rearrange("p (g m) -> p g m", g=NG)[:, :, lo:hi])

        move_scales()
        for b in range(HB):
            deal_words(b)
        def run_a(b, tag):
            num[b] = sb([P, 4, PAIRS], F32, "num1")[:] if b else num0[:, : 4 * PAIRS].rearrange("p (t i) -> p t i", t=4)
            for r in range(4 * b, 4 * b + 4):
                make_h(r)
                pick_a(r, 0, PAIRS)
                if r % 4 < 3:
                    times_vmax(r, 0, PAIRS, num[b][:, r % 4])
        mid = sb([P, KA * 2048], BF16, "mid")
        round_half(mid[:, :2048], 1, 0, 0, True)
        run_a(0, "half100")
        round_half(mid[:, :2048], 1, 0, 1)
        pick_sum(0, 0, PAIRS)
        pick_sum(1, 0, PAIRS)
        for x in range(2):
            round_half(mid[:, 2048:], 1, 1, x)
        nc.vector.quantize_mx(out=mid_codes[:].bitcast(FP8X4), scales=mid_scales[:], in_=mid[:])
        pick_sum(2, 0, PAIRS)
        pick_sum(3, 0, PAIRS)
        scalar_vmax(3, 0, PAIRS, num[0][:, 3])
        round_block(2, 0, "w1g00")
        quantise_block(2, 0)
        rounded[2, 1] = sb([P, 2048], BF16, "w1g21")[:]
        round_half(rounded[2, 1], LAST, 1, 0, True)
        run_a(1, None)
        round_half(rounded[2, 1], LAST, 1, 1)
        quantise_block(2, 1)
        for r in range(4, 8):
            pick_sum(r, 0, PAIRS)
        root0a = sb([P, 4, 384], F32, "root0a", "half210")
        root03 = sb([P, 4, 128], F32, "root03")
        arena = sb([P, 3328], F32, "arena", "raw20")
        def view(lo, n):
            return arena[:, lo : lo + 4 * n].rearrange("p (t i) -> p t i", t=4)
        den[LAST, HALF] = view(1024, HALF)
        for b in range(LAST):
            for c in range(4):
                rec[b, c] = chunk(den, b, c)
        root10 = view(768, HALF)
        root20 = view(1792, 128)
        root1b = arena[:, 2304:].rearrange("p (t i) -> p t i", t=4)
        rootc = {c: sb([P, 4, 128], F32, f"rootc{c}")[:] for c in (1, 2, 3)}
        def held_tile(units, tag):
            both = sb([P, 512 * len(units)], BF16, f"zheld{tag}", tag)
            for k, unit in enumerate(units):
                z4[unit] = both[:, 512 * k : 512 * (k + 1)]
        def last_vmax(r):
            nc.scalar.activation(out=last_num[:, r - 8], in_=last_a[:, r - 8], func=ACT.Copy, scale=vm[:, LAST, r - 8 : r - 7])
        def pick_whole(r):
            nc.vector.tensor_copy(last_a[:, r - 8], h[r][:].indirect(pos1_t[:]))
        invert(root0a[:], den[0, 0][:, :, :384])
        scalar_vmax(7, 0, PAIRS, num[1][:, 3])
        square(den[0, 0][:, :, :384], root0a[:])
        invert(root03[:], rec[0, 3])
        gz = sb([P, 1024], BF16, "gz", "h7")
        x, r = [v[:, :, : 256].rearrange("p t (c i) -> p c t i", i=4) for v in (num[0], den[0, 0])]
        nc.gpsimd.tensor_tensor(out=gz[:].rearrange("p (c i t) -> p c t i", i=4, t=4), in0=x, in1=r, op=ALU.mult)
        for r in range(8, 12):
            make_h(r, f"h{r - 8}" if r < 11 else None)
            pick_whole(r)
            if r == 8:
                nc.gpsimd.tensor_scalar(out=last_num[:, 0], in0=last_a[:, 0], scalar1=vm[:, LAST, 0:1], scalar2=0.0, op0=ALU.mult, op1=ALU.add)
        square(rec[0, 3], root03[:])
        first = sb([P, 1024], F32, "first")
        early_codes = sb([P, HALF], U32, "early_codes")
        den[LAST, 0] = first[:].rearrange("p (t i) -> p t i", t=4)
        for c in range(4):
            rec[LAST, c] = chunk(den, LAST, c)
        for r in range(8, 12):
            pick_sum(r, 0, HALF)
        invert(root10, den[1, 0][:, :, :HALF])
        last_vmax(9)
        square(den[1, 0][:, :, :HALF], root10)
        last_vmax(10)
        last_vmax(11)
        invert(root20, rec[LAST, 0])
        invert(rootc[1], rec[LAST, 1])
        square(rec[LAST, 0], root20)
        invert(root1b, den[1, 0][:, :, HALF:])
        square(rec[LAST, 1], rootc[1])
        square(den[1, 0][:, :, HALF:], root1b)
        multiply_two(0, gz, early_codes)
        vz = sb([P, 1024], BF16, "vz", "half00")
        x, r = [v[:, :, :HALF].rearrange("p t (c i) -> p c t i", i=4) for v in (num[1], den[1, 0])]
        nc.vector.tensor_tensor(out=vz[:].rearrange("p (c i t) -> p c t i", i=4, t=4), in0=x, in1=r, op=ALU.mult)
        pick_sum(8, HALF, PAIRS)
        multiply_two(1, vz, sb([P, HALF], U32, "zc1"))
        pick_sum(9, HALF, PAIRS)
        pick_sum(10, HALF, PAIRS)
        weave(LAST, 0)
        pick_sum(11, HALF, PAIRS)
        multiply(LAST, 0)
        held_tile([(0, 2), (1, 2), (0, 3)], "rootc1")
        weave(LAST, 1)
        weave(0, 2)
        multiply(LAST, 1)
        weave(1, 2)
        multiply(0, 2)
        weave(0, 3)
        multiply(1, 2)
        invert(rootc[2], rec[LAST, 2])
        invert(rootc[3], rec[LAST, 3])
        empty(0, 0, "h5")
        square(rec[LAST, 2], rootc[2])
        empty(0, 1, "raw00")
        held_tile([(1, 3)], "rootc2")
        multiply(0, 3)
        weave(LAST, 2)
        weave(1, 3)
        multiply(LAST, 2)
        square(rec[LAST, 3], rootc[3])
        empty(1, 0, "half00")
        empty(1, 1, "half01")
        weave(LAST, 3)
        multiply(1, 3)
        both = sb([P, 2048], BF16, "held", "rootc3")
        held0, held = both[:, :1024], both[:, 1024:]
        for c in range(2):
            y4[c, 0] = held0[:, 512 * c : 512 * (c + 1)]
            y4[c, 1] = held[:, 512 * c : 512 * (c + 1)]
        round_rows(0, 0)
        multiply(LAST, 3)
        round_rows(0, 1)
        round_rows(1, 0)
        round_rows(1, 1)
        nc.vector.quantize_mx(out=ycodes[:, PAIRS : PAIRS + HALF].bitcast(FP8X4), scales=yscales[:, PAIRS : PAIRS + HALF], in_=held)
        nc.vector.quantize_mx(out=ycodes[:, :HALF].bitcast(FP8X4), scales=yscales[:, :HALF], in_=held0)
        nc.sync.dma_start(out=out_words[:, :, :HALF], in_=ycodes[:].bitcast(I32).rearrange("p (g m) -> p g m", g=NG)[:, :, :HALF])
        for g in range(NG):
            empty(2, g, ("h0", "h1")[g])
        round_bank(2, 0, nc.scalar.copy, "mid")
        round_bank(2, 1, nc.scalar.copy, "tabs")
        store_codes(2)
        for g, copy in enumerate((nc.scalar.copy, nc.vector.tensor_copy)):
            empty(3, g, f"gw0{g}", copy)
            round_bank(3, g, copy, f"gw1{g}")
        store_codes(3)

        for q in range(4):
            (nc.sync, nc.scalar)[q % 2].dma_start(
                out=out_2[:, 4 * q : 4 * q + 4, :].bitcast(I32).rearrange("g r m -> r g m"),
                in_=yscales[32 * q : 32 * q + 4, :].bitcast(I32).rearrange("p (g m) -> p g m", g=NG),
            )
